import numpy as np, ml_dtypes
CORES = [2,3,42,43,82,83,122,123]
N = 8
import mx_ref
BF = ml_dtypes.bfloat16
def gcols(t, e):
    v = np.concatenate([t.reshape(8, 16, -1, 4), np.zeros((8, 16, 1, 4), BF)], axis=2)
    return np.ascontiguousarray(np.stack([v[g][:, e[g]] for g in range(8)])).reshape(128, -1)
def gpick(z, e):
    return np.concatenate([z[16 * g:16 * g + 16][:, e[g]] for g in range(8)])
def tile(rs):
    return np.stack(rs, axis=2).reshape(128, -1).astype(BF)
def pick(q, e):
    c = np.concatenate([q[0].reshape(128, -1, 4), np.zeros((128, 1, 4), np.uint8)], axis=1); s = np.concatenate([q[1], np.ones((16, 1), np.uint8)], axis=1)
    return (np.ascontiguousarray(c[:, e].reshape(128, -1)), np.ascontiguousarray(s[:, e]))
def join(*qs):
    return (np.concatenate([q[0] for q in qs], axis=1), np.concatenate([q[1] for q in qs], axis=1))
def put(q, e, v):
    c, s = q[0].reshape(128, -1, 4).copy(), q[1].copy(); c[:, e] = v[0].reshape(128, -1, 4); s[:, e] = v[1]
    return (c.reshape(128, -1), s)
def pk(c, s):
    return (np.ascontiguousarray(c), mx_ref.live(s))
def emit(q):
    return q[0], q[1]
def packed(v, rng):
    q = [mx_ref.quantize(np.ascontiguousarray(v[r])) for r in range(N)]
    return np.stack([a for a, b in q]), np.stack([mx_ref.plane(b, rng) for a, b in q])
def values_of_codes():
    e, c = np.zeros((128, 128, 4), np.float32), np.zeros((128, 2, 4), np.uint8)
    e[np.arange(128), np.arange(128), 0] = 1
    c[:127, :, 0] = np.arange(256).reshape(2, 128).T[:127]
    return mx_ref.matmul(mx_ref.quantize(e.reshape(128, 512).astype(BF)), (c.reshape(128, 8), np.full((16, 2), 127, np.uint8))).T.reshape(-1).astype(np.float64)
CODE_VALUE, SCALE_VALUE = values_of_codes(), 2.0 ** (np.arange(256) - 127.0)
def decode(q):
    return (CODE_VALUE[q[0]].reshape(16, 8, -1, 4) * SCALE_VALUE[q[1]][:, None, :, None] + 0.0).reshape(128, -1).astype(np.float32)
def f(rng, *shape):
    return mx_ref.flush((rng.standard_normal(shape, dtype=np.float32) * np.exp2(rng.integers(-2, 3, shape[:-1] + (1,)))).astype(BF))
def wide(rng, *shape, cols=0):
    v = rng.standard_normal(shape, dtype=np.float32) * np.exp2(rng.integers(-12, 13, shape)).astype(np.float32)
    if cols: v *= np.repeat(np.exp2(rng.integers(-cols, cols + 1, shape[:-2] + (1, shape[-1] // 4))) * (rng.random(shape[:-2] + (1, shape[-1] // 4)) > 0.0625), 4, axis=-1).astype(np.float32)
    return mx_ref.flush(v.astype(BF))
C, K, R = 256, 64, 3
STEP = [1, 2, 4]
def partner(r, t):
    return r ^ STEP[t]
def basins(s):
    s = s + np.float32(0.0)
    j = np.arange(C)
    o = np.argsort(-s, axis=1, kind="stable")
    w = C - 1 - np.argsort(o, axis=1)
    up = w[:, None, :] > w[:, :, None]
    before, behind = j < j[:, None], j > j[:, None]
    l = np.max(np.where(up & before, j, -1), axis=2)
    r = np.min(np.where(up & behind, j, C), axis=2)
    a = np.where(l < 0, -1, np.min(np.where(before & (j > l[:, :, None]), w[:, None, :], C), axis=2))
    b = np.where(r == C, -1, np.min(np.where(behind & (j < r[:, :, None]), w[:, None, :], C), axis=2))
    other = (a < C) & (b < C) & (w < C - 1)
    q = np.where(other, np.take_along_axis(o, np.where(other, C - 1 - np.maximum(a, b), 0), axis=1), j)
    p = s - np.take_along_axis(s, q, axis=1)
    first = np.where(w == C - 1, 0, np.where(other, 1, 2))
    e = np.sort(np.lexsort((-p, first))[:, :K], axis=1)
    edge = np.full((8, 1), -1)
    beside = np.where(np.concatenate([edge, w[:, :-1]], axis=1) > np.concatenate([w[:, 1:], edge], axis=1), j - 1, j + 1)
    to = np.where(other, np.where(a > b, l, r), beside)
    np.put_along_axis(to, e, e, axis=1)
    for i in range(C.bit_length()): to = np.take_along_axis(to, to, axis=1)
    k = np.zeros((8, C), np.int64)
    np.put_along_axis(k, e, np.tile(np.arange(K), (8, 1)), axis=1)
    return e, np.take_along_axis(q, e, axis=1), to, np.take_along_axis(k, to, axis=1)
def big(v):
    v = v.astype(np.float32)
    v[np.abs(v) < np.float32(2.0 ** -16)] = 0
    return v.astype(BF)
def numbers_of(rng):
    return {"x": big(f(rng, N, 128, 4 * C)), "u": np.array(f(rng, N, 128, 512)), "v": np.array(f(rng, N, 128, 512))}
def weights(rng, w):
    c, p = packed(w, rng)
    return {"wc": c, "ws": p}
def some(rng, keep):
    w = np.array(f(rng, N, 128, 2048)).reshape(N, 128, 4, 8, 16, 4)
    w[:, :, :, :, [i for i in range(16) if i not in keep]] = 0
    return weights(rng, w.reshape(N, 128, 2048))
def unit(rng, keep, a):
    w = np.zeros((N, 128, 4, 128, 4), np.float32)
    i = np.array([i for i in range(128) if i % 16 in keep])
    for b in range(4): w[:, i, b, i, b] = a
    return weights(rng, w.reshape(N, 128, 2048).astype(BF))
def whole(rng, *shape):
    return rng.integers(4, 8, shape) * rng.choice([-1.0, 1.0], shape)
def plant(d, s, c, m, top, k):
    x = d["x"].astype(np.float32).reshape(N, 8, 16, C, 4)
    x[:, :, 0] = 0
    x[:, :, 0, :, 0] = c * m
    u = d["u"].reshape(N, 128, 128, 4)
    u[:, :, ::16] = 0
    for i in range(3): x[:, :, 8 + i] = ((s[..., None] >> np.arange(4 * i, 4 * i + 4)) & 1) * 2.0 ** np.arange(4) * m
    for h in range(0, 128, 16):
        u[:, h, h, 0] = (k * top).astype(np.float32).astype(BF)
        for i in range(3): u[:, h + 8 + i, h] = (k * 16.0 ** i).astype(np.float32).astype(BF)[:, None]
    return {"x": x.reshape(N, 128, 4 * C).astype(BF), "u": u.reshape(N, 128, 512), "v": d["v"]}
def setup_inputs(rng):
    return {**numbers_of(rng), **weights(rng, f(rng, N, 128, 2048))}
def setup_inputs_ties(rng):
    d = numbers_of(rng)
    e = rng.permutation(N)
    x = d["x"].reshape(N, 8, 16, C, 4)
    for r in range(N):
        k = np.zeros(C, int) if r == e[0] else rng.permutation(C) % 3
        a = x[r][:, :8, :3].copy()
        a[:, :, 2] = 0
        x[r][:, :8] = a[:, :, k]
    x[e[1]] = 0
    u = d["u"].reshape(N, 8, 16, 128, 4)
    u[:, :, 8:, ::16] = 0
    return {"x": x.reshape(N, 128, 4 * C), "u": u.reshape(N, 128, 512), "v": d["v"], **some(rng, range(8, 16))}
def setup_inputs_near(rng):
    d = numbers_of(rng)
    m = 2.0 ** -29
    x = np.zeros((N, 8, 16, C, 4), np.float32)
    x[:, :, 1:8] = whole(rng, N, 8, 7, C, 4) * 4 * m
    x[:, :, 11:] = whole(rng, N, 8, 5, C, 4) * m
    d["x"] = x
    j = np.arange(C)
    fall = C // 2 - 1 - j // 2
    fall = fall + 2 * (fall == C // 2 - K - 1) - 2 * (fall == C // 2 - K + 1)
    c, s = np.zeros((N, 8, C)), np.zeros((N, 8, C), np.int64)
    for r in range(N):
        g = rng.permutation(8)
        for i in range(8):
            c[r, i] = np.where(j % 2 == 1, 1.0, -1.0 * (g[i] % 2))
            s[r, i] = np.where(j % 2 == 1, fall if g[i] == 3 else j // 2, 0)
            if g[i] >= 4:
                s[r, i] = rng.integers(0, 256, C)
                c[r, i, 2 * rng.permutation(C // 2)[:2] + 1] = 2.0 ** 30
    k = np.where(rng.permutation(N) < N // 2, 2.0 ** -30, 1.0)
    return {**plant(d, s, c, m, 2.0 ** 23, k), **unit(rng, range(1, 8), 32)}
def setup_inputs_slopes(rng):
    d = numbers_of(rng)
    j = np.arange(C)
    e = np.stack([j, C - 1 - j, np.minimum(j, C - 1 - j), np.abs(j - C // 2), 0 * j, j // 2, j // 8, np.where(j < 2 * K, j % 2 * (C + j), C - 1 - j)])
    s = np.stack([e[rng.permutation(8)] for r in range(N)])
    c = np.where(rng.permutation(N) < N // 2, -1.0, 0.0)[:, None, None] * np.ones((N, 8, C))
    return {**plant(d, s, c, 1.0, 4096.0, np.ones(N)), **some(rng, range(1, 8))}
def setup_inputs_huge(rng):
    d = numbers_of(rng)
    x = 2.0 ** 30 * (0.5 + 0.3 * rng.random((N, 128, C, 4)))
    c = np.tile(np.arange(C) % 2 * 2.0 - 1.0, (N, 1))
    c[rng.permutation(N) < N // 2] = 1
    x *= c[:, None, :, None]
    g = np.stack([rng.permutation(8) % 2 * 2.0 - 1.0 for r in range(N)])
    u = d["u"].reshape(N, 128, 128, 4)
    u[:, :, ::16] = (2.0 ** 30 * (1 - 0.25 * rng.random((N, 128, 8, 4))) * g[:, None, :, None]).astype(np.float32).astype(BF)
    return {"x": x.astype(np.float32).reshape(N, 128, 4 * C).astype(BF), "u": u.reshape(N, 128, 512), "v": d["v"], **unit(rng, range(16), 1)}
def setup_inputs_spread(rng):
    d = setup_inputs(rng)
    d["x"] = big(wide(rng, N, 128, 4 * C, cols=6))
    return d
def check_inputs(d):
    b = []
    for k in ("x", "u", "v"):
        a = np.abs(d[k].astype(np.float32))
        if not (np.isfinite(a).all() and ((a == 0) | (a >= 2.0 ** -30) & (a <= 2.0 ** 30)).all()): b.append("a value of " + k)
    return b
def reference(x, u, v, wc, ws):
    qu = [mx_ref.quantize(u[r]) for r in range(N)]
    lay = [pk(wc[r], ws[r]) for r in range(N)]
    now = [x[r] for r in range(N)]
    ends = [None] * N
    for t in range(R):
        held, place, sent = [], [], []
        for r in range(N):
            q = mx_ref.quantize(now[r])
            held.append(decode(q))
            e, low, ends[r], h = basins(mx_ref.matmul(qu[r], q)[::16])
            place.append(h)
            own = held[r].astype(BF)
            blend = (gcols(own, e).astype(np.float32) + gcols(own, low).astype(np.float32)) * np.float32(0.5)
            sent.append(mx_ref.quantize(blend.astype(BF)))
        for r in range(N):
            came = sent[partner(r, t)]
            made = [np.maximum(mx_ref.matmul(pick(lay[r], np.arange(128 * b, 128 * b + 128)), came), np.float32(0.0)) * np.float32(0.03125) for b in range(4)]
            now[r] = tile([held[r][:, b::4] + gpick(made[b], place[r]) for b in range(4)])
    y, ol = np.zeros((N, 128, C), np.float32), np.zeros((N, 8, C), np.float32)
    oc, osc = np.zeros((N, 128, 4 * C), np.uint8), np.zeros((N, 16, C), np.uint8)
    for r in range(N):
        q = mx_ref.quantize(now[r])
        y[r] = mx_ref.matmul(mx_ref.quantize(v[r]), q)
        ol[r] = ends[r]
        oc[r], osc[r] = emit(q)
    return {"y": y, "ol": ol, "oc": oc, "osc": osc}

@@ -1,0 +1,412 @@
+import numpy as np
+import math
+from concourse.mybir import dt, AluOpType, AxisListType, ActivationFunctionType
+import comms_topo
+
+C, K, R = 256, 64, 3
+STEP = [1, 2, 4]
+F32, B16, I32, U16, U8, MX = "float32", "bfloat16", "int32", "uint16", "uint8", "float8_e4m3fn_x4"
+INIT = float(2 ** 20 + 256)
+
+_SB = {
+    F32: {"cf": 256, "jc": 128, "iw": 776, "col": 256, "sm": 64, "Sw": 1032, "M": 128, "VV": 128, "PK": 128, "tm": 128, "tsV": 128, "tsM": 128,
+          "tsN": 128, "tsK": 128, "JL": 128, "JR": 128, "nkL": 128, "nkR": 128, "RL": 128, "RR": 128, "sad": 128, "Gp": 128, "np": 128, "cm": 128,
+          "yk": 128, "CG": 256, "ct": 256, "g64": 64, "s64": 64, "H": 256, "G3": 256, "rmx": 136, "rm": 256, "lm": 256, "out": 256, "yb": 256},
+    B16: {"X0": 1024, "X1": 1024, "ut": 512, "vt": 512, "et": 2048, "rbt": 512, "idn": 128, "mk": 256, "sg": 256, "ng": 128, "A": 272, "pk": 256,
+          "npk": 256, "np2": 256, "ni": 256, "nf": 256, "th": 256, "hp": 128, "FV": 1024, "UL": 1024, "UR": 1024, "eqf": 128, "pe": 128, "kept": 128,
+          "K": 256, "pcw": 272, "ed": 256, "Tf": 768, "Th": 1024, "TE": 256, "F": 512, "NR": 128, "rec": 128, "rnk": 128, "nPL": 128, "tmb": 256,
+          "tsb": 256, "vLR": 128, "z": 128, "wl": 128, "uu": 256, "Bar": 256, "bv": 256, "BB1": 256, "BB2": 256, "D": 256, "nW": 256, "vl": 256,
+          "hv": 256},
+    I32: {"ci": 256, "cj": 256, "si": 32},
+    U16: {"su": 64},
+    MX: {"uq0": 128, "uq": 128, "vq": 128, "wq": 512, "eq": 512, "rbq": 128, "zq": 128, "FVq": 256, "XQ": 256},
+    U8: {"us0": 128, "us": 128, "vs": 128, "wp": 512, "es": 512, "rbs": 128, "zs": 128, "FVs": 256, "XS": 256},
+}
+SCRATCH = {n: ("sbuf", [128, w], d) for d, l in _SB.items() for n, w in l.items()}
+for _t in range(R):
+    for _n, _d in (("Fq", MX), ("Fs", U8), ("lc", MX), ("ls", U8)):
+        SCRATCH["%s%d" % (_n, _t)] = ("sbuf", [128, 128], _d)
+SCRATCH["pss"] = ("psum", [128, 512], F32)
+SCRATCH["psr"] = ("psum", [128, 512], F32)
+SCRATCH["pst"] = ("psum", [128, 2048], F32)
+_PS = ("pss", "psr", "pst")
+SEMAPHORES = ["qv", "qa", "qt", "qg"] + ["d%d" % i for i in range(24)] + ["arr%d" % t for t in range(R)] + ["snt"]
+
+
+def maker(g, T):
+    eng = {"v": g.vector, "a": g.scalar, "t": g.tensor, "g": g, "s": g.sync}
+    count, known, snap, log, nd = {}, {q: {} for q in eng}, {}, {}, [0]
+
+    def span(v):
+        n, a, b, s = v
+        if n in _PS:
+            return n, a // 512 * 512, (b + 511) // 512 * 512, 1
+        if s < 0:
+            k = (a - b + (-s) - 1) // (-s)
+            return n, a + s * (k - 1), a + 1, -s
+        return n, a, b, s
+
+    def meet(x, y):
+        (_, a, b, s), (_, c, d, r) = x, y
+        if a >= d or c >= b:
+            return False
+        return not (s == r and s > 1 and (a - c) % s)
+
+    def need(q, reads, writes):
+        want = {}
+        for kind, vs in (("r", reads), ("w", writes)):
+            for v in vs:
+                x = span(v)
+                for (y, k2, q2, n2) in log.get(x[0], []):
+                    if meet(x, y) and (kind == "w" or k2 == "w" or (x[0] in _PS and q2 != q)):
+                        want[q2] = max(want.get(q2, 0), n2)
+        return want
+
+    def wait(q, want):
+        for q2, n in sorted(want.items()):
+            if known[q].get(q2, 0) >= n:
+                continue
+            eng[q].wait_ge(T.sem[q2], n)
+            known[q][q2] = n
+            for k, m in snap.get((q2, n), {}).items():
+                known[q][k] = max(known[q].get(k, 0), m)
+
+    def note(q2, n, reads, writes):
+        for kind, vs in (("r", reads), ("w", writes)):
+            for v in vs:
+                x = span(v)
+                l = log.setdefault(x[0], [])
+                if kind == "w" and x[3] == 1:
+                    l[:] = [e for e in l if not (x[1] <= e[0][1] and e[0][2] <= x[2])]
+                l.append((x, kind, q2, n))
+
+    def do(q, call, reads, writes):
+        wait(q, need(q, reads, writes))
+        s = "q" + q
+        count[s] = count.get(s, 0) + 1
+        call(eng[q]).then_inc(T.sem[s], 1)
+        snap[(s, count[s])] = dict(known[q])
+        note(s, count[s], reads, writes)
+
+    def dma(q, out, in_, reads, writes):
+        wait(q, need(q, reads, writes))
+        s = "d%d" % nd[0]
+        nd[0] += 1
+        eng[q].dma_start(out, in_).then_inc(T.sem[s], 16)
+        count[s] = 16
+        snap[(s, 16)] = dict(known[q])
+        note(s, 16, reads, writes)
+
+    def finish():
+        for s in sorted(count):
+            if known["g"].get(s, 0) < count[s]:
+                g.wait_ge(T.sem[s], count[s])
+    return do, dma, need, wait, note, count, finish
+
+
+def rank_program(g, core, T, topo):
+    rank = T.rank_of(core)
+    if rank is None:
+        return
+    OP, AF, AX = AluOpType, ActivationFunctionType, AxisListType.X
+    do, dma, need, wait, note, count, finish = maker(g, T)
+
+    def V(n, a=None, b=None, s=1):
+        if a is None:
+            return (n, 0, SCRATCH[n][1][1], 1)
+        return (n, a, b, s)
+
+    def ap(v):
+        n, a, b, s = v
+        if s < 0:
+            return T[n][:, a:(b if b >= 0 else None):s]
+        return T[n][:, a:b:s] if s != 1 else T[n][:, a:b]
+
+    def ind(v, l):
+        return ap(v).indirect(ap(l))
+
+    def sc(x):
+        return ap(x) if isinstance(x, tuple) else x
+
+    def scr(*xs):
+        return [x for x in xs if isinstance(x, tuple)]
+
+    def tt(out, a, b, op, l=None):
+        do("v", lambda e: e.tensor_tensor(ap(out), ind(a, l) if l else ap(a), ap(b), op), [a, b] + scr(l), [out])
+
+    def ts(out, a, s1, s2, op0, op1=None):
+        if op1 is None:
+            do("v", lambda e: e.tensor_scalar(ap(out), ap(a), sc(s1), None, op0), [a] + scr(s1), [out])
+        else:
+            do("v", lambda e: e.tensor_scalar(ap(out), ap(a), sc(s1), sc(s2), op0, op1), [a] + scr(s1, s2), [out])
+
+    def scan(out, d0, d1, init, op0, op1):
+        do("v", lambda e: e.tensor_tensor_scan(ap(out), ap(d0), ap(d1), init, op0, op1), [d0, d1], [out])
+
+    def copy(out, a):
+        do("v", lambda e: e.tensor_copy(ap(out), ap(a)), [a], [out])
+
+    def fill(v, c):
+        do("v", lambda e: e.memset(ap(v), c), [], [v])
+
+    def act(out, a, f, bias=0.0, scale=1.0, l=None, acc=None):
+        def call(e):
+            kw = {}
+            if isinstance(bias, tuple) or bias != 0.0:
+                kw["bias"] = sc(bias)
+            if isinstance(scale, tuple) or scale != 1.0:
+                kw["scale"] = sc(scale)
+            if acc:
+                kw["accum_out"] = ap(acc)
+            return e.activation(ap(out), ind(a, l) if l else ap(a), f, **kw)
+        do("a", call, [a] + scr(bias, scale, l), [out] + scr(acc))
+
+    def quant(q, s, x):
+        do("v", lambda e: e.quantize_mx(ap(q), ap(s), ap(x)), [x], [q, s])
+
+    def mm(out, l, ls, r, rs, start=True, stop=True):
+        do("t", lambda e: e.matmul_mx(ap(out), ap(l), ap(ls), ap(r), ap(rs), start, stop), [l, ls, r, rs], [out])
+
+    def iota(v, pat, base, cm):
+        kw = {} if v[0] in ("ci", "cj") else {"allow_small_or_imprecise_dtypes": True}
+        do("g", lambda e: e.iota(ap(v), pat, base, cm, **kw), [], [v])
+
+    def select(v, pat, op, base, cm):
+        do("g", lambda e: e.affine_select(ap(v), ap(v), pat, op, 0.0, base, cm), [v], [v])
+
+    def bits(out, a, n):
+        do("v", lambda e: e.tensor_scalar(ap(out), ap(a), n, None, OP.bitwise_and), [a], [out])
+
+    def diag(out, src, tmp, n):
+        tt(tmp, src, V("mk", 0, n), OP.mult)
+        scan(out, V("sg", 0, n), tmp, 0.0, OP.mult, OP.add)
+
+    LI, EL, QL, PL, HL, UO = V("su", 0, 8), V("su", 8, 12), V("su", 12, 16), V("su", 16, 24), V("su", 24, 40), V("su", 40, 48)
+    CS, TH = V("sm", 8, 9), V("sm", 9, 10)
+
+    dma("s", ap(V("X0")), T.x[:, :], [], [V("X0")])
+    dma("a", ap(V("ut")), T.u[:, :], [], [V("ut")])
+    dma("s", ap(V("wq")).bitcast(dt.uint8), T.wc[:, :], [], [V("wq")])
+    dma("a", ap(V("wp")), T.ws[:, :], [], [V("wp")])
+    dma("s", ap(V("vt")), T.v[:, :], [], [V("vt")])
+
+    iota(V("ci", 0, 8), [[16, 8]], 0, 0)
+    copy(UO, V("ci", 0, 8))
+    iota(V("ci"), [[1, 256]], 256, -1)
+    bits(V("cj"), V("ci"), 15)
+    copy(V("cf"), V("cj"))
+    ts(V("mk"), V("cf"), 0.0, None, OP.is_equal)
+    iota(V("col"), [[0, 16], [1, 16]], 0, 0)
+    ts(V("sg"), V("col"), 1.0, None, OP.min)
+    fill(V("idn"), 1.0)
+    fill(V("rbt"), 1024.0)
+    select(V("idn"), [[-1, 128]], OP.is_equal, 0, 1)
+    select(V("rbt"), [[-16, 8], [0, 64]], OP.is_ge, 0, 1)
+    select(V("rbt"), [[16, 8], [0, 64]], OP.is_ge, 15, -1)
+    fill(V("Sw"), -1e25)
+    fill(V("et"), 0.0)
+    quant(V("uq0"), V("us0"), V("ut"))
+    do("v", lambda e: e.tensor_copy(T.uq[:, 0:128].bitcast(dt.uint32), T.uq0[:, 0:128].bitcast(dt.uint32).indirect(ap(UO))), [V("uq0"), UO], [V("uq")])
+    do("v", lambda e: e.tensor_copy(T.us[:, 0:128], T.us0[:, 0:128].indirect(ap(UO))), [V("us0"), UO], [V("us")])
+    iota(V("ci"), [[0, 256]], 0, 1)
+    iota(V("jc"), [[2, 128]], 131072, 0)
+    iota(V("ng"), [[-1, 128]], 128, 0)
+    iota(V("col"), [[1, 256]], 0, 0)
+    iota(V("iw"), [[1, 776]], 1024, 0)
+
+    def late():
+        for b in range(4):
+            copy(V("et", 512 * b + b, 512 * b + 512, 4), V("idn"))
+        quant(V("eq"), V("es"), V("et"))
+        quant(V("rbq"), V("rbs"), V("rbt"))
+        bits(V("cj"), V("ci"), 15)
+        copy(V("cf", 0, 8), V("cj", 0, 8))
+        for m in range(4):
+            ts(V("sm", m, m + 1), V("cf", 0, 1), 16.0 * m + 0.5, None, OP.add)
+        for n, c in (("A", 0.0), ("D", 1.0), ("nW", 1.0), ("RL", INIT), ("RR", INIT), ("nPL", 200.0), ("rmx", 1e25), ("F", 0.0), ("UL", 0.0), ("pcw", 0.0)):
+            fill(V(n), c)
+        fill(V("iw", 256, 257), 0.0)
+
+    def later():
+        fill(V("rbt"), 0.0)
+        quant(V("zq"), V("zs"), V("rbt"))
+        for t in range(R):
+            dma("s", T["lc%d" % t][:, 64:128].bitcast(dt.uint8), T.zq[:, 64:128].bitcast(dt.uint8), [V("zq")], [V("lc%d" % t, 64, 128)])
+            dma("s", T["ls%d" % t][:, 64:128], T.zs[:, 64:128], [V("zs")], [V("ls%d" % t, 64, 128)])
+        quant(V("vq"), V("vs"), V("vt"))
+
+    far = [T.cores[rank ^ s] for s in STEP]
+    engs = topo.engines(core, far[1])
+    mask = 0
+    for e in engs:
+        mask |= 1 << e
+
+    S, XQ, XS, P = V("pss", 0, 256), V("XQ"), V("XS"), V("psr", 0, 128)
+    pc = V("pcw", 16, 272)
+
+    def ranks():
+        quant(V("FVq"), V("FVs"), V("FV"))
+        for h in range(2):
+            mm(P, V("rbq"), V("rbs"), V("FVq", 128 * h, 128 * h + 128), V("FVs", 128 * h, 128 * h + 128), h == 0, h == 1)
+
+    def slot(m):
+        b = 512 * (m // 4) + m % 4
+        return V("FV", b, 512 * (m // 4) + 512, 4)
+
+    for t in range(R):
+        quant(XQ, XS, V("X%d" % (t % 2)))
+        mm(S, V("uq"), V("us"), XQ, XS)
+        copy(V("Sw", 8, 264), S)
+        tt(V("VV"), V("pss", 0, 256, 2), V("Sw", 7, 263, 2), OP.min)
+        diag(V("tsV"), V("VV"), V("tm"), 128)
+        for m in range(8):
+            act(slot(m), V("VV"), AF.Sign, bias=V("tsV", 16 * m + 15, 16 * m + 16), scale=-1.0)
+        tt(V("M"), V("pss", 0, 256, 2), V("Sw", 9, 264, 2), OP.max)
+        if t == 0:
+            late()
+        for b in range(4):
+            mm(V("pst", 512 * b, 512 * b + 256), V("eq", 128 * b, 128 * b + 128), V("es", 128 * b, 128 * b + 128), XQ, XS)
+        tt(V("A", 0, 256), S, V("Sw", 7, 263), OP.is_gt)
+        tt(V("nW", 1, 256), V("pss", 0, 255), V("Sw", 10, 265), OP.is_ge)
+        tt(V("pk"), V("A", 0, 256), V("A", 1, 257), OP.is_gt)
+        tt(V("hp"), V("pk", 0, 256, 2), V("pk", 1, 256, 2), OP.max)
+        ts(V("hp"), V("hp"), 1.0, 1e29, OP.subtract, OP.mult)
+        tt(V("PK"), V("M"), V("hp"), OP.add)
+        diag(V("tsM"), V("PK"), V("tm"), 128)
+        for m in range(7, -1, -1):
+            act(V("UL", 128 * m, 128 * m + 16 * m + 16), V("M", 0, 16 * m + 16), AF.Relu, bias=V("tsM", 16 * m + 15, 16 * m + 16), scale=-1.0)
+        act(V("UL"), V("UL"), AF.Sign)
+        ranks()
+        tt(V("JL"), V("jc"), V("A", 0, 256, 2), OP.subtract)
+        act(V("JR"), V("JL"), AF.Copy, bias=512.0)
+        for m in range(8):
+            ts(V("UR", 128 * m + 16 * m, 128 * m + 128), V("M", 16 * m, 128), V("tsM", 16 * m + 15, 16 * m + 16), None, OP.is_le)
+        act(V("Sw", 520, 776), V("Sw", 8, 264), AF.Copy)
+        act(V("npk"), V("pk"), AF.Copy, bias=1.0, scale=-1.0)
+        act(V("np2"), V("pk"), AF.Copy, bias=2.0, scale=-1.0)
+        for b in range(4):
+            act(V("Th", 256 * b, 256 * b + 256), V("pst", 512 * b, 512 * b + 256), AF.Copy, scale=0.5)
+        tt(V("nkR"), P, V("JR"), OP.add)
+        tt(V("nkL"), P, V("JL"), OP.add)
+        for m in range(8):
+            a = 16 * m
+            scan(V("RR", 126, a - 1, -1), V("UR", 128 * m + 127, 128 * m + a, -1), V("nkR", 127, a, -1), INIT, OP.mult, OP.max)
+        for m in range(7, -1, -1):
+            n = 16 * m + 15
+            scan(V("RL", 1, n + 1), V("UL", 128 * m, 128 * m + n), V("nkL", 1, n + 1), INIT, OP.mult, OP.max)
+        tt(V("sad"), V("RL"), V("RR"), OP.min)
+        diag(V("tsK"), V("sad"), V("tm"), 128)
+        copy(V("si", 0, 8), V("tsK", 15, 128, 16))
+        bits(V("si", 8, 16), V("si", 0, 8), 1023)
+        copy(LI, V("si", 8, 16))
+        tt(V("np"), V("Sw", 8, 784), V("PK"), OP.subtract, l=LI)
+        diag(V("tsN"), V("np"), V("tm"), 128)
+        for m in range(5, 8):
+            act(slot(m), V("np"), AF.Relu, bias=V("tsN", 16 * m + 15, 16 * m + 16), scale=-1.0)
+            act(slot(m), slot(m), AF.Sign)
+        for m in range(5):
+            ts(slot(m), V("np"), V("tsN", 16 * m + 15, 16 * m + 16), None, OP.is_lt)
+        ranks()
+        act(V("Gp"), V("iw"), AF.Copy, l=LI)
+        scan(V("ni"), V("npk"), V("npk"), 0.0, OP.add, OP.max)
+        ts(V("sm", 10, 11), V("ni", 255, 256), -1.0, 192.0, OP.mult, OP.add)
+        act(V("nf"), V("ni"), AF.Relu, bias=V("sm", 10, 11))
+        act(V("nf"), V("nf"), AF.Sign)
+        for m in range(7, -1, -1):
+            n = 16 * m + 15
+            scan(V("nPL", 1, n + 1), V("UL", 128 * m, 128 * m + n), V("ng", 0, n), 200.0, OP.mult, OP.max)
+        ts(V("eqf"), P, 65536.0, None, OP.is_lt)
+        tt(V("cm"), P, V("eqf"), OP.mult)
+        do("v", lambda e: e.tensor_reduce(ap(CS), T.cm[:, 0:128], AX, OP.max), [V("cm")], [CS])
+        ts(V("eqf"), P, CS, None, OP.is_equal)
+        ts(TH, CS, 1.0 - 1.0 / 1024, 65.0, OP.mult, OP.add)
+        scan(V("pe", 127, -1, -1), V("eqf", 127, -1, -1), V("eqf", 127, -1, -1), 0.0, OP.add, OP.max)
+        tt(V("yk"), P, V("pe"), OP.add)
+        ts(V("kept"), V("yk"), TH, None, OP.is_ge)
+        act(V("NR"), V("kept"), AF.Copy, scale=-1e29)
+        tt(V("th"), V("np2"), V("nf"), OP.mult)
+        for p in range(2):
+            tt(V("K", p, 256, 2), V("kept"), V("th", p, 256, 2), OP.is_ge)
+        scan(pc, V("K"), V("K"), 0.0, OP.add, OP.max)
+        for m in range(4):
+            act(V("ed"), pc, AF.Sign, bias=V("sm", m, m + 1), scale=-1.0, acc=V("sm", 16 + m, 17 + m))
+        if t < R - 1:
+            for b in range(3):
+                act(V("Tf", 256 * b, 256 * b + 256), V("pst", 512 * b, 512 * b + 256), AF.Copy)
+        for p in range(2):
+            tt(V("ct", p, 256, 2), V("Gp"), V("pk", p, 256, 2), OP.mult)
+        tt(V("CG"), V("ct"), V("col"), OP.max)
+        scan(V("rmx", 1, 129), V("NR"), V("M"), 1e25, OP.add, OP.max)
+        ts(EL, V("sm", 16, 20), 0.5, 128.0, OP.mult, OP.add)
+        for b in range(4):
+            act(V("TE", 64 * b, 64 * b + 64), V("Th", 256 * b, 256 * b + 256), AF.Copy, l=EL)
+        tt(V("g64"), V("CG"), V("mk", 0, 64), OP.mult, l=EL)
+        scan(V("s64"), V("sg", 0, 64), V("g64"), 0.0, OP.mult, OP.add)
+        copy(V("si", 16, 20), V("s64", 15, 64, 16))
+        bits(V("si", 20, 24), V("si", 16, 20), 255)
+        copy(QL, V("si", 20, 24))
+        for b in range(4):
+            tt(V("F", b, 256, 4), V("Th", 256 * b, 256 * b + 256), V("TE", 64 * b, 64 * b + 64), OP.add, l=QL)
+        FQ, FS = V("Fq%d" % t), V("Fs%d" % t)
+        quant(FQ, FS, V("F"))
+        rid, pid, _ = topo.addr(far[t])
+        wait("g", need("g", [FQ, FS], []))
+        arr = T.sem["arr%d" % t]
+        g.remote_dma(T["lc%d" % t][:, 0:64].bitcast(dt.uint8), T["Fq%d" % t][:, 0:64].bitcast(dt.uint8), arr, T.sem.snt, pid, rid, mask)
+        g.remote_dma(T["ls%d" % t][:, 0:64], T["Fs%d" % t][:, 0:64], arr, T.sem.snt, pid, rid, mask)
+        count["snt"] = count.get("snt", 0) + 2 * len(engs)
+        count["arr%d" % t] = 2 * len(engs)
+        note("arr%d" % t, 2 * len(engs), [], [V("lc%d" % t, 0, 64), V("ls%d" % t, 0, 64)])
+        if t == 0:
+            later()
+        diag(V("tsb", 0, 128), V("nPL"), V("tmb", 0, 128), 128)
+        ts(V("sm", 24, 32), V("tsb", 15, 128, 16), -2.0, 273.0, OP.mult, OP.add)
+        ts(V("sm", 32, 40), V("si", 8, 16), 512.0, None, OP.is_lt)
+        tt(V("sm", 24, 32), V("sm", 24, 32), V("sm", 32, 40), OP.mult)
+        copy(PL, V("sm", 24, 32))
+        act(V("vLR"), V("pcw"), AF.Copy, l=PL)
+        tt(V("rec"), V("PK"), V("rmx", 0, 128), OP.is_gt)
+        tt(V("z"), V("rec"), V("kept"), OP.max)
+        for p in range(2):
+            tt(V("Bar", p, 256, 2), V("z"), V("th", p, 256, 2), OP.is_ge)
+        act(V("BB1"), V("Bar"), AF.Copy, bias=-1e29, scale=1.1e29)
+        act(V("BB2"), V("Bar"), AF.Copy, bias=-1e29, scale=2e29)
+        tt(V("rnk"), V("rec"), V("kept"), OP.is_gt)
+        tt(V("wl"), V("pcw", 17, 272, 2), V("vLR"), OP.subtract)
+        tt(V("wl"), V("wl"), V("rnk"), OP.mult)
+        for p in range(2):
+            tt(V("uu", p, 256, 2), V("pcw", 16 + p, 272, 2), V("wl"), OP.subtract)
+        tt(V("bv"), V("Bar"), V("uu"), OP.mult)
+        scan(V("rm"), V("Sw", 8, 264), V("BB1"), -1e26, OP.min, OP.max)
+        scan(V("lm", 255, -1, -1), V("Sw", 263, 7, -1), V("BB2", 255, -1, -1), -1e25, OP.min, OP.max)
+        tt(V("D"), V("rm"), V("lm"), OP.is_ge)
+        scan(V("D", 255, -1, -1), V("nW", 255, -1, -1), V("D", 255, -1, -1), 1.0, OP.max, OP.min)
+        scan(V("vl"), V("D"), V("bv"), 0.0, OP.mult, OP.add)
+        ts(V("uu"), V("vl"), 0.0, None, OP.is_equal)
+        scan(V("hv", 255, -1, -1), V("uu", 255, -1, -1), V("vl", 255, -1, -1), 0.0, OP.mult, OP.add)
+        diag(V("tsb"), V("hv"), V("tmb"), 256)
+        ts(HL, V("tsb", 15, 256, 16), -1.0, None, OP.add)
+        if t == R - 1:
+            act(V("s64"), V("col"), AF.Copy, l=EL)
+            act(V("out"), V("s64"), AF.Copy, l=HL)
+            dma("s", T.ol[:, :], T.out[0:128:16, :], [V("out")], [])
+            for b in range(3):
+                act(V("Tf", 256 * b, 256 * b + 256), V("pst", 512 * b, 512 * b + 256), AF.Copy)
+        X = "X%d" % ((t + 1) % 2)
+        for b in (3, 0, 1, 2):
+            o = "psr" if b == 3 else "pst"
+            k = 0 if b == 3 else 512 * b
+            mm(V(o, k, k + 128), V("wq", 128 * b, 128 * b + 128), V("wp", 128 * b, 128 * b + 128), V("lc%d" % t), V("ls%d" % t))
+            act(V("H", 64 * b, 64 * b + 64), V(o, k, k + 64), AF.Relu, scale=0.03125)
+        act(V("G3"), V("H", 192, 256), AF.Copy, l=HL)
+        for b in range(3):
+            tt(V(X, b, 1024, 4), V("H", 64 * b, 64 * b + 64), V("Tf", 256 * b, 256 * b + 256), OP.add, l=HL)
+        tt(V(X, 3, 1024, 4), V("pst", 1536, 1792), V("G3"), OP.add)
+    quant(XQ, XS, V("X%d" % (R % 2)))
+    dma("s", T.oc[:, :], T.XQ[:, :].bitcast(dt.uint8), [XQ], [])
+    for k in range(4):
+        dma("a" if k % 2 else "s", T.osc[4 * k:4 * k + 4, :], T.XS[32 * k:32 * k + 4, :], [XS], [])
+    mm(S, V("vq"), V("vs"), XQ, XS)
+    copy(V("yb"), S)
+    dma("s", T.y[:, :], T.yb[:, :], [V("yb")], [])
+    finish()

@@ -7,16 +7,18 @@ C, K, R = 256, 64, 3
 STEP = [1, 2, 4]
 F32, B16, I32, U16, U8, MX = "float32", "bfloat16", "int32", "uint16", "uint8", "float8_e4m3fn_x4"
 INIT = float(2 ** 20 + 256)
+CYCLE, FIXED, WAKE = 0.83, 60.0, 100.0
 
 _SB = {
-    F32: {"cf": 256, "jc": 128, "iw": 776, "col": 256, "sm": 64, "Sw": 1032, "M": 128, "VV": 128, "PK": 128, "tm": 128, "tsV": 128, "tsM": 128,
-          "tsN": 128, "tsK": 128, "JL": 128, "JR": 128, "nkL": 128, "nkR": 128, "RL": 128, "RR": 128, "sad": 128, "Gp": 128, "np": 128, "cm": 128,
-          "yk": 128, "CG": 256, "ct": 256, "g64": 64, "s64": 64, "H": 256, "G3": 256, "rmx": 136, "rm": 256, "lm": 256, "out": 256, "yb": 256},
-    B16: {"X0": 1024, "X1": 1024, "ut": 512, "vt": 512, "et": 2048, "rbt": 512, "idn": 128, "mk": 256, "sg": 256, "ng": 128, "A": 272, "pk": 256,
-          "npk": 256, "np2": 256, "ni": 256, "nf": 256, "th": 256, "hp": 128, "FV": 1024, "UL": 1024, "UR": 1024, "eqf": 128, "pe": 128, "kept": 128,
-          "K": 256, "pcw": 272, "ed": 256, "Tf": 768, "Th": 1024, "TE": 256, "F": 512, "NR": 128, "rec": 128, "rnk": 128, "nPL": 128, "tmb": 256,
-          "tsb": 256, "vLR": 128, "z": 128, "wl": 128, "uu": 256, "Bar": 256, "bv": 256, "BB1": 256, "BB2": 256, "D": 256, "nW": 256, "vl": 256,
-          "hv": 256},
+    F32: {"cf": 256, "jc": 128, "iw": 776, "col": 256, "sm": 64, "Sw": 1032, "M": 128, "VV": 128, "PK": 128, "tm": 128, "tmM": 128, "tmK": 128,
+          "tmN": 128, "tsV": 128, "tsM": 128, "tsN": 128, "tsK": 128, "JL": 128, "nkL": 128, "nkR": 128, "RL": 128, "RR": 128, "sad": 128, "Gp": 128,
+          "np": 128, "cm": 128, "yk": 128, "ct": 256, "g64": 64, "s64": 64, "H": 256, "G3": 512, "rmx": 136, "rm": 256, "lm": 256, "out": 256,
+          "yb": 256},
+    B16: {"X0": 1024, "X1": 1024, "ut": 512, "vt": 512, "et": 2048, "rbt": 512, "idn": 128, "mk": 256, "sg": 256, "ng": 128, "A": 272, "A2": 272,
+          "du": 256, "pk": 256, "npk": 256, "np2": 256, "ni": 256, "nf": 256, "th": 256, "hp": 128, "FV": 1024, "UL": 1024, "UR": 1024, "eqf": 128,
+          "pe": 128, "kept": 128, "K": 256, "pcw": 272, "ed": 256, "Tf": 512, "Th": 2048, "TE": 256, "F": 512, "NR": 128, "rec": 128, "rnk": 128,
+          "nPL": 128, "tmb": 256, "tsb": 256, "vLR": 128, "z": 128, "wl": 128, "uu": 256, "Bar": 256, "bv": 256, "BB1": 256, "BB2": 256, "D": 256,
+          "D2": 256, "nW": 256, "vl": 256, "hv": 256},
     I32: {"ci": 256, "cj": 256, "si": 32},
     U16: {"su": 64},
     MX: {"uq0": 128, "uq": 128, "vq": 128, "wq": 512, "eq": 512, "rbq": 128, "zq": 128, "FVq": 256, "XQ": 256},
@@ -33,9 +35,9 @@ _PS = ("pss", "psr", "pst")
 SEMAPHORES = ["qv", "qa", "qt", "qg"] + ["d%d" % i for i in range(24)] + ["arr%d" % t for t in range(R)] + ["snt"]
 
 
-def maker(g, T):
+def planner(g, T):
     eng = {"v": g.vector, "a": g.scalar, "t": g.tensor, "g": g, "s": g.sync}
-    count, known, snap, log, nd = {}, {q: {} for q in eng}, {}, {}, [0]
+    ops, log = [], {}
 
     def span(v):
         n, a, b, s = v
@@ -52,56 +54,83 @@ def maker(g, T):
             return False
         return not (s == r and s > 1 and (a - c) % s)
 
-    def need(q, reads, writes):
-        want = {}
+    def add(q, call, reads, writes, cost, hold=None, sem=None, inc=1):
+        i, pre = len(ops), set()
         for kind, vs in (("r", reads), ("w", writes)):
             for v in vs:
                 x = span(v)
-                for (y, k2, q2, n2) in log.get(x[0], []):
-                    if meet(x, y) and (kind == "w" or k2 == "w" or (x[0] in _PS and q2 != q)):
-                        want[q2] = max(want.get(q2, 0), n2)
-        return want
-
-    def wait(q, want):
-        for q2, n in sorted(want.items()):
-            if known[q].get(q2, 0) >= n:
-                continue
-            eng[q].wait_ge(T.sem[q2], n)
-            known[q][q2] = n
-            for k, m in snap.get((q2, n), {}).items():
-                known[q][k] = max(known[q].get(k, 0), m)
-
-    def note(q2, n, reads, writes):
+                for (y, k2, j) in log.get(x[0], []):
+                    if meet(x, y) and (kind == "w" or k2 == "w" or (x[0] in _PS and ops[j]["q"] != q)):
+                        pre.add(j)
         for kind, vs in (("r", reads), ("w", writes)):
             for v in vs:
                 x = span(v)
                 l = log.setdefault(x[0], [])
                 if kind == "w" and x[3] == 1:
                     l[:] = [e for e in l if not (x[1] <= e[0][1] and e[0][2] <= x[2])]
-                l.append((x, kind, q2, n))
+                l.append((x, kind, i))
+        ops.append({"q": q, "call": call, "pre": pre, "cost": cost, "hold": cost if hold is None else hold, "sem": sem or "q" + q, "inc": inc})
 
-    def do(q, call, reads, writes):
-        wait(q, need(q, reads, writes))
-        s = "q" + q
-        count[s] = count.get(s, 0) + 1
-        call(eng[q]).then_inc(T.sem[s], 1)
-        snap[(s, count[s])] = dict(known[q])
-        note(s, count[s], reads, writes)
+    def order():
+        n = len(ops)
+        succ, left, rank = [[] for _ in range(n)], [len(o["pre"]) for o in ops], [0.0] * n
+        for i, o in enumerate(ops):
+            for j in o["pre"]:
+                succ[j].append(i)
+        for i in range(n - 1, -1, -1):
+            rank[i] = ops[i]["cost"] + max([rank[k] + WAKE for k in succ[i]], default=0.0)
+        ready, free, cand, out = [0.0] * n, {}, {}, []
+        for i in range(n):
+            if not left[i]:
+                cand.setdefault(ops[i]["q"], []).append(i)
+        while any(cand.values()):
+            best = None
+            for q, l in cand.items():
+                if not l:
+                    continue
+                f = free.get(q, 0.0)
+                t = min(max(f, ready[i]) for i in l)
+                i = max([i for i in l if max(f, ready[i]) <= t + 15.0], key=lambda i: (rank[i], -i))
+                t = max(f, ready[i])
+                if best is None or (t, -rank[i]) < best[0]:
+                    best = ((t, -rank[i]), q, i)
+            (t, _), q, i = best
+            cand[q].remove(i)
+            out.append(i)
+            free[q] = t + ops[i]["hold"]
+            for k in succ[i]:
+                ready[k] = max(ready[k], t + ops[i]["cost"] + WAKE)
+                left[k] -= 1
+                if not left[k]:
+                    cand.setdefault(ops[k]["q"], []).append(k)
+        return out
 
-    def dma(q, out, in_, reads, writes):
-        wait(q, need(q, reads, writes))
-        s = "d%d" % nd[0]
-        nd[0] += 1
-        eng[q].dma_start(out, in_).then_inc(T.sem[s], 16)
-        count[s] = 16
-        snap[(s, 16)] = dict(known[q])
-        note(s, 16, reads, writes)
-
-    def finish():
+    def issue():
+        count, at, known, snap = {}, {}, {q: {} for q in eng}, {}
+        for i in order():
+            o = ops[i]
+            q, s = o["q"], o["sem"]
+            kn = known.setdefault(q, {})
+            if q in eng:
+                want = {}
+                for j in o["pre"]:
+                    want[ops[j]["sem"]] = max(want.get(ops[j]["sem"], 0), at[j])
+                for s2, m in sorted(want.items()):
+                    if kn.get(s2, 0) >= m:
+                        continue
+                    eng[q].wait_ge(T.sem[s2], m)
+                    kn[s2] = m
+                    for k, x in snap.get((s2, m), {}).items():
+                        kn[k] = max(kn.get(k, 0), x)
+            count[s] = count.get(s, 0) + o["inc"]
+            at[i] = count[s]
+            if o["call"]:
+                o["call"](eng[q])
+            snap[(s, at[i])] = dict(kn) if q in eng else {}
         for s in sorted(count):
             if known["g"].get(s, 0) < count[s]:
                 g.wait_ge(T.sem[s], count[s])
-    return do, dma, need, wait, note, count, finish
+    return add, issue
 
 
 def rank_program(g, core, T, topo):
@@ -109,7 +138,8 @@ def rank_program(g, core, T, topo):
     if rank is None:
         return
     OP, AF, AX = AluOpType, ActivationFunctionType, AxisListType.X
-    do, dma, need, wait, note, count, finish = maker(g, T)
+    add, issue = planner(g, T)
+    nd = [0]
 
     def V(n, a=None, b=None, s=1):
         if a is None:
@@ -131,23 +161,42 @@ def rank_program(g, core, T, topo):
     def scr(*xs):
         return [x for x in xs if isinstance(x, tuple)]
 
+    def width(v):
+        return len(range(v[1], v[2], v[3]))
+
+    def short(*vs):
+        return all(SCRATCH[v[0]][2] in (B16, U16) for v in vs)
+
+    def do(q, call, reads, writes, cycles):
+        add(q, lambda e: call(e).then_inc(T.sem["q" + q], 1), reads, writes, max(64, cycles) * CYCLE + FIXED)
+
+    def dma(q, out, in_, reads, writes):
+        s = "d%d" % nd[0]
+        nd[0] += 1
+        add(q, lambda e: e.dma_start(out, in_).then_inc(T.sem[s], 16), reads, writes, 2500.0, 100.0, s, 16)
+
     def tt(out, a, b, op, l=None):
-        do("v", lambda e: e.tensor_tensor(ap(out), ind(a, l) if l else ap(a), ap(b), op), [a, b] + scr(l), [out])
+        n = width(out)
+        n = 60 + 1.5 * n if l else n if a[0] in _PS or b[0] in _PS else 2 * n
+        do("v", lambda e: e.tensor_tensor(ap(out), ind(a, l) if l else ap(a), ap(b), op), [a, b] + scr(l), [out], n)
+
+    def half(out, *a):
+        return width(out) * (0.5 if short(out, *a) else 1.0)
 
     def ts(out, a, s1, s2, op0, op1=None):
         if op1 is None:
-            do("v", lambda e: e.tensor_scalar(ap(out), ap(a), sc(s1), None, op0), [a] + scr(s1), [out])
+            do("v", lambda e: e.tensor_scalar(ap(out), ap(a), sc(s1), None, op0), [a] + scr(s1), [out], half(out, a))
         else:
-            do("v", lambda e: e.tensor_scalar(ap(out), ap(a), sc(s1), sc(s2), op0, op1), [a] + scr(s1, s2), [out])
+            do("v", lambda e: e.tensor_scalar(ap(out), ap(a), sc(s1), sc(s2), op0, op1), [a] + scr(s1, s2), [out], half(out, a))
 
     def scan(out, d0, d1, init, op0, op1):
-        do("v", lambda e: e.tensor_tensor_scan(ap(out), ap(d0), ap(d1), init, op0, op1), [d0, d1], [out])
+        do("v", lambda e: e.tensor_tensor_scan(ap(out), ap(d0), ap(d1), init, op0, op1), [d0, d1], [out], half(out, d0, d1))
 
     def copy(out, a):
-        do("v", lambda e: e.tensor_copy(ap(out), ap(a)), [a], [out])
+        do("v", lambda e: e.tensor_copy(ap(out), ap(a)), [a], [out], half(out, a))
 
     def fill(v, c):
-        do("v", lambda e: e.memset(ap(v), c), [], [v])
+        do("v", lambda e: e.memset(ap(v), c), [], [v], half(v))
 
     def act(out, a, f, bias=0.0, scale=1.0, l=None, acc=None):
         def call(e):
@@ -159,23 +208,24 @@ def rank_program(g, core, T, topo):
             if acc:
                 kw["accum_out"] = ap(acc)
             return e.activation(ap(out), ind(a, l) if l else ap(a), f, **kw)
-        do("a", call, [a] + scr(bias, scale, l), [out] + scr(acc))
+        n = width(out)
+        do("a", call, [a] + scr(bias, scale, l), [out] + scr(acc), 78 + 1.5 * n if l else n + (24 if acc else 0))
 
     def quant(q, s, x):
-        do("v", lambda e: e.quantize_mx(ap(q), ap(s), ap(x)), [x], [q, s])
+        do("v", lambda e: e.quantize_mx(ap(q), ap(s), ap(x)), [x], [q, s], 14 + 0.265 * width(x))
 
     def mm(out, l, ls, r, rs, start=True, stop=True):
-        do("t", lambda e: e.matmul_mx(ap(out), ap(l), ap(ls), ap(r), ap(rs), start, stop), [l, ls, r, rs], [out])
+        do("t", lambda e: e.matmul_mx(ap(out), ap(l), ap(ls), ap(r), ap(rs), start, stop), [l, ls, r, rs], [out], width(r) + 16)
 
     def iota(v, pat, base, cm):
         kw = {} if v[0] in ("ci", "cj") else {"allow_small_or_imprecise_dtypes": True}
-        do("g", lambda e: e.iota(ap(v), pat, base, cm, **kw), [], [v])
+        do("g", lambda e: e.iota(ap(v), pat, base, cm, **kw), [], [v], 160 + 2 * width(v))
 
     def select(v, pat, op, base, cm):
-        do("g", lambda e: e.affine_select(ap(v), ap(v), pat, op, 0.0, base, cm), [v], [v])
+        do("g", lambda e: e.affine_select(ap(v), ap(v), pat, op, 0.0, base, cm), [v], [v], 200 + 2 * width(v))
 
     def bits(out, a, n):
-        do("v", lambda e: e.tensor_scalar(ap(out), ap(a), n, None, OP.bitwise_and), [a], [out])
+        do("v", lambda e: e.tensor_scalar(ap(out), ap(a), n, None, OP.bitwise_and), [a], [out], width(out))
 
     def diag(out, src, tmp, n):
         tt(tmp, src, V("mk", 0, n), OP.mult)
@@ -198,48 +248,55 @@ def rank_program(g, core, T, topo):
     ts(V("mk"), V("cf"), 0.0, None, OP.is_equal)
     iota(V("col"), [[0, 16], [1, 16]], 0, 0)
     ts(V("sg"), V("col"), 1.0, None, OP.min)
+    fill(V("Sw"), -1e25)
+    quant(V("uq0"), V("us0"), V("ut"))
+    do("v", lambda e: e.tensor_copy(T.uq[:, 0:128].bitcast(dt.uint32), T.uq0[:, 0:128].bitcast(dt.uint32).indirect(ap(UO))), [V("uq0"), UO], [V("uq")], 250)
+    do("v", lambda e: e.tensor_copy(T.us[:, 0:128], T.us0[:, 0:128].indirect(ap(UO))), [V("us0"), UO], [V("us")], 250)
     fill(V("idn"), 1.0)
     fill(V("rbt"), 1024.0)
     select(V("idn"), [[-1, 128]], OP.is_equal, 0, 1)
     select(V("rbt"), [[-16, 8], [0, 64]], OP.is_ge, 0, 1)
     select(V("rbt"), [[16, 8], [0, 64]], OP.is_ge, 15, -1)
-    fill(V("Sw"), -1e25)
-    fill(V("et"), 0.0)
-    quant(V("uq0"), V("us0"), V("ut"))
-    do("v", lambda e: e.tensor_copy(T.uq[:, 0:128].bitcast(dt.uint32), T.uq0[:, 0:128].bitcast(dt.uint32).indirect(ap(UO))), [V("uq0"), UO], [V("uq")])
-    do("v", lambda e: e.tensor_copy(T.us[:, 0:128], T.us0[:, 0:128].indirect(ap(UO))), [V("us0"), UO], [V("us")])
     iota(V("ci"), [[0, 256]], 0, 1)
     iota(V("jc"), [[2, 128]], 131072, 0)
     iota(V("ng"), [[-1, 128]], 128, 0)
+    fill(V("iw"), 0.0)
+    iota(V("iw", 0, 256), [[1, 256]], 256, 0)
+    iota(V("iw", 512, 768), [[1, 256]], 256, 0)
     iota(V("col"), [[1, 256]], 0, 0)
-    iota(V("iw"), [[1, 776]], 1024, 0)
-
-    def late():
-        for b in range(4):
-            copy(V("et", 512 * b + b, 512 * b + 512, 4), V("idn"))
-        quant(V("eq"), V("es"), V("et"))
-        quant(V("rbq"), V("rbs"), V("rbt"))
-        bits(V("cj"), V("ci"), 15)
-        copy(V("cf", 0, 8), V("cj", 0, 8))
-        for m in range(4):
-            ts(V("sm", m, m + 1), V("cf", 0, 1), 16.0 * m + 0.5, None, OP.add)
-        for n, c in (("A", 0.0), ("D", 1.0), ("nW", 1.0), ("RL", INIT), ("RR", INIT), ("nPL", 200.0), ("rmx", 1e25), ("F", 0.0), ("UL", 0.0), ("pcw", 0.0)):
-            fill(V(n), c)
-        fill(V("iw", 256, 257), 0.0)
-
-    def later():
-        fill(V("rbt"), 0.0)
-        quant(V("zq"), V("zs"), V("rbt"))
-        for t in range(R):
-            dma("s", T["lc%d" % t][:, 64:128].bitcast(dt.uint8), T.zq[:, 64:128].bitcast(dt.uint8), [V("zq")], [V("lc%d" % t, 64, 128)])
-            dma("s", T["ls%d" % t][:, 64:128], T.zs[:, 64:128], [V("zs")], [V("ls%d" % t, 64, 128)])
-        quant(V("vq"), V("vs"), V("vt"))
+    fill(V("et"), 0.0)
+    for b in range(4):
+        copy(V("et", 512 * b + b, 512 * b + 512, 4), V("idn"))
+    quant(V("eq"), V("es"), V("et"))
+    quant(V("rbq"), V("rbs"), V("rbt"))
+    bits(V("cj", 0, 8), V("ci", 0, 8), 15)
+    copy(V("cf", 0, 8), V("cj", 0, 8))
+    for m in range(4):
+        ts(V("sm", m, m + 1), V("cf", 0, 1), 16.0 * m + 0.5, None, OP.add)
+    for n, c in (("A", 0.0), ("nW", 1.0), ("RL", INIT), ("RR", INIT), ("nPL", 200.0), ("rmx", 1e25), ("F", 0.0), ("UL", 0.0), ("pcw", 0.0)):
+        fill(V(n), c)
+    fill(V("rbt"), 0.0)
+    quant(V("zq"), V("zs"), V("rbt"))
+    for t in range(R):
+        dma("s", T["lc%d" % t][:, 64:128].bitcast(dt.uint8), T.zq[:, 64:128].bitcast(dt.uint8), [V("zq")], [V("lc%d" % t, 64, 128)])
+        dma("s", T["ls%d" % t][:, 64:128], T.zs[:, 64:128], [V("zs")], [V("ls%d" % t, 64, 128)])
+    quant(V("vq"), V("vs"), V("vt"))
 
     far = [T.cores[rank ^ s] for s in STEP]
     engs = topo.engines(core, far[1])
     mask = 0
     for e in engs:
         mask |= 1 << e
+
+    def send(t):
+        rid, pid, _ = topo.addr(far[t])
+        arr = T.sem["arr%d" % t]
+
+        def call(e):
+            e.remote_dma(T["lc%d" % t][:, 0:64].bitcast(dt.uint8), T["Fq%d" % t][:, 0:64].bitcast(dt.uint8), arr, T.sem.snt, pid, rid, mask)
+            e.remote_dma(T["ls%d" % t][:, 0:64], T["Fs%d" % t][:, 0:64], arr, T.sem.snt, pid, rid, mask)
+        add("g", call, [V("Fq%d" % t), V("Fs%d" % t)], [], 1500.0, 1500.0, "snt", 2 * len(engs))
+        add("in", None, [V("Fq%d" % t)], [V("lc%d" % t, 0, 64), V("ls%d" % t, 0, 64)], 4000.0, 0.0, "arr%d" % t, 2 * len(engs))
 
     S, XQ, XS, P = V("pss", 0, 256), V("XQ"), V("XS"), V("psr", 0, 128)
     pc = V("pcw", 16, 272)
@@ -261,46 +318,46 @@ def rank_program(g, core, T, topo):
         diag(V("tsV"), V("VV"), V("tm"), 128)
         for m in range(8):
             act(slot(m), V("VV"), AF.Sign, bias=V("tsV", 16 * m + 15, 16 * m + 16), scale=-1.0)
+        tt(V("A", 0, 256), S, V("Sw", 7, 263), OP.is_gt)
         tt(V("M"), V("pss", 0, 256, 2), V("Sw", 9, 264, 2), OP.max)
-        if t == 0:
-            late()
         for b in range(4):
             mm(V("pst", 512 * b, 512 * b + 256), V("eq", 128 * b, 128 * b + 128), V("es", 128 * b, 128 * b + 128), XQ, XS)
-        tt(V("A", 0, 256), S, V("Sw", 7, 263), OP.is_gt)
-        tt(V("nW", 1, 256), V("pss", 0, 255), V("Sw", 10, 265), OP.is_ge)
-        tt(V("pk"), V("A", 0, 256), V("A", 1, 257), OP.is_gt)
-        tt(V("hp"), V("pk", 0, 256, 2), V("pk", 1, 256, 2), OP.max)
+        act(V("A2", 0, 257), V("A", 0, 257), AF.Copy, bias=2.0)
+        scan(V("du"), V("A2", 0, 256), V("A2", 1, 257), 0.0, OP.max, OP.subtract)
+        tt(V("hp"), V("du", 0, 256, 2), V("du", 1, 256, 2), OP.max)
         ts(V("hp"), V("hp"), 1.0, 1e29, OP.subtract, OP.mult)
         tt(V("PK"), V("M"), V("hp"), OP.add)
-        diag(V("tsM"), V("PK"), V("tm"), 128)
+        diag(V("tsM"), V("PK"), V("tmM"), 128)
+        tt(V("nW", 1, 256), V("pss", 0, 255), V("Sw", 10, 265), OP.is_ge)
         for m in range(7, -1, -1):
             act(V("UL", 128 * m, 128 * m + 16 * m + 16), V("M", 0, 16 * m + 16), AF.Relu, bias=V("tsM", 16 * m + 15, 16 * m + 16), scale=-1.0)
         act(V("UL"), V("UL"), AF.Sign)
         ranks()
         tt(V("JL"), V("jc"), V("A", 0, 256, 2), OP.subtract)
-        act(V("JR"), V("JL"), AF.Copy, bias=512.0)
         for m in range(8):
             ts(V("UR", 128 * m + 16 * m, 128 * m + 128), V("M", 16 * m, 128), V("tsM", 16 * m + 15, 16 * m + 16), None, OP.is_le)
         act(V("Sw", 520, 776), V("Sw", 8, 264), AF.Copy)
+        act(V("pk"), V("du"), AF.Relu)
         act(V("npk"), V("pk"), AF.Copy, bias=1.0, scale=-1.0)
         act(V("np2"), V("pk"), AF.Copy, bias=2.0, scale=-1.0)
         for b in range(4):
-            act(V("Th", 256 * b, 256 * b + 256), V("pst", 512 * b, 512 * b + 256), AF.Copy, scale=0.5)
-        tt(V("nkR"), P, V("JR"), OP.add)
+            act(V("Th", 512 * b, 512 * b + 256), V("pst", 512 * b, 512 * b + 256), AF.Copy, scale=0.5)
+            act(V("Th", 512 * b + 256, 512 * b + 512), V("Th", 512 * b, 512 * b + 256), AF.Copy)
         tt(V("nkL"), P, V("JL"), OP.add)
-        for m in range(8):
-            a = 16 * m
-            scan(V("RR", 126, a - 1, -1), V("UR", 128 * m + 127, 128 * m + a, -1), V("nkR", 127, a, -1), INIT, OP.mult, OP.max)
+        act(V("nkR"), V("nkL"), AF.Copy, bias=512.0)
         for m in range(7, -1, -1):
             n = 16 * m + 15
             scan(V("RL", 1, n + 1), V("UL", 128 * m, 128 * m + n), V("nkL", 1, n + 1), INIT, OP.mult, OP.max)
+        for m in range(8):
+            a = 16 * m
+            scan(V("RR", 126, a - 1, -1), V("UR", 128 * m + 127, 128 * m + a, -1), V("nkR", 127, a, -1), INIT, OP.mult, OP.max)
         tt(V("sad"), V("RL"), V("RR"), OP.min)
-        diag(V("tsK"), V("sad"), V("tm"), 128)
+        diag(V("tsK"), V("sad"), V("tmK"), 128)
         copy(V("si", 0, 8), V("tsK", 15, 128, 16))
         bits(V("si", 8, 16), V("si", 0, 8), 1023)
         copy(LI, V("si", 8, 16))
         tt(V("np"), V("Sw", 8, 784), V("PK"), OP.subtract, l=LI)
-        diag(V("tsN"), V("np"), V("tm"), 128)
+        diag(V("tsN"), V("np"), V("tmN"), 128)
         for m in range(5, 8):
             act(slot(m), V("np"), AF.Relu, bias=V("tsN", 16 * m + 15, 16 * m + 16), scale=-1.0)
             act(slot(m), slot(m), AF.Sign)
@@ -309,56 +366,43 @@ def rank_program(g, core, T, topo):
         ranks()
         act(V("Gp"), V("iw"), AF.Copy, l=LI)
         scan(V("ni"), V("npk"), V("npk"), 0.0, OP.add, OP.max)
-        ts(V("sm", 10, 11), V("ni", 255, 256), -1.0, 192.0, OP.mult, OP.add)
-        act(V("nf"), V("ni"), AF.Relu, bias=V("sm", 10, 11))
-        act(V("nf"), V("nf"), AF.Sign)
+        ts(V("sm", 10, 11), V("ni", 255, 256), -4.0, 768.0, OP.mult, OP.add)
+        act(V("nf"), V("ni"), AF.Relu, bias=V("sm", 10, 11), scale=4.0)
+        scan(V("th"), V("nf"), V("np2"), 0.0, OP.max, OP.min)
         for m in range(7, -1, -1):
             n = 16 * m + 15
             scan(V("nPL", 1, n + 1), V("UL", 128 * m, 128 * m + n), V("ng", 0, n), 200.0, OP.mult, OP.max)
         ts(V("eqf"), P, 65536.0, None, OP.is_lt)
         tt(V("cm"), P, V("eqf"), OP.mult)
-        do("v", lambda e: e.tensor_reduce(ap(CS), T.cm[:, 0:128], AX, OP.max), [V("cm")], [CS])
+        do("v", lambda e: e.tensor_reduce(ap(CS), T.cm[:, 0:128], AX, OP.max), [V("cm")], [CS], 128)
         ts(V("eqf"), P, CS, None, OP.is_equal)
         ts(TH, CS, 1.0 - 1.0 / 1024, 65.0, OP.mult, OP.add)
         scan(V("pe", 127, -1, -1), V("eqf", 127, -1, -1), V("eqf", 127, -1, -1), 0.0, OP.add, OP.max)
         tt(V("yk"), P, V("pe"), OP.add)
         ts(V("kept"), V("yk"), TH, None, OP.is_ge)
         act(V("NR"), V("kept"), AF.Copy, scale=-1e29)
-        tt(V("th"), V("np2"), V("nf"), OP.mult)
         for p in range(2):
             tt(V("K", p, 256, 2), V("kept"), V("th", p, 256, 2), OP.is_ge)
         scan(pc, V("K"), V("K"), 0.0, OP.add, OP.max)
         for m in range(4):
             act(V("ed"), pc, AF.Sign, bias=V("sm", m, m + 1), scale=-1.0, acc=V("sm", 16 + m, 17 + m))
-        if t < R - 1:
-            for b in range(3):
-                act(V("Tf", 256 * b, 256 * b + 256), V("pst", 512 * b, 512 * b + 256), AF.Copy)
+        for b in range(2):
+            act(V("Tf", 256 * b, 256 * b + 256), V("pst", 512 * b, 512 * b + 256), AF.Copy)
         for p in range(2):
             tt(V("ct", p, 256, 2), V("Gp"), V("pk", p, 256, 2), OP.mult)
-        tt(V("CG"), V("ct"), V("col"), OP.max)
-        scan(V("rmx", 1, 129), V("NR"), V("M"), 1e25, OP.add, OP.max)
         ts(EL, V("sm", 16, 20), 0.5, 128.0, OP.mult, OP.add)
+        act(V("sm", 40, 44), V("sm", 16, 20), AF.Copy, bias=128.0, scale=0.5)
         for b in range(4):
-            act(V("TE", 64 * b, 64 * b + 64), V("Th", 256 * b, 256 * b + 256), AF.Copy, l=EL)
-        tt(V("g64"), V("CG"), V("mk", 0, 64), OP.mult, l=EL)
+            act(V("TE", 64 * b, 64 * b + 64), V("Th", 512 * b, 512 * b + 256), AF.Copy, l=EL)
+        tt(V("g64"), V("ct"), V("mk", 0, 64), OP.mult, l=EL)
         scan(V("s64"), V("sg", 0, 64), V("g64"), 0.0, OP.mult, OP.add)
-        copy(V("si", 16, 20), V("s64", 15, 64, 16))
-        bits(V("si", 20, 24), V("si", 16, 20), 255)
-        copy(QL, V("si", 20, 24))
+        tt(V("sm", 44, 48), V("s64", 15, 64, 16), V("sm", 40, 44), OP.max)
+        copy(QL, V("sm", 44, 48))
         for b in range(4):
-            tt(V("F", b, 256, 4), V("Th", 256 * b, 256 * b + 256), V("TE", 64 * b, 64 * b + 64), OP.add, l=QL)
-        FQ, FS = V("Fq%d" % t), V("Fs%d" % t)
-        quant(FQ, FS, V("F"))
-        rid, pid, _ = topo.addr(far[t])
-        wait("g", need("g", [FQ, FS], []))
-        arr = T.sem["arr%d" % t]
-        g.remote_dma(T["lc%d" % t][:, 0:64].bitcast(dt.uint8), T["Fq%d" % t][:, 0:64].bitcast(dt.uint8), arr, T.sem.snt, pid, rid, mask)
-        g.remote_dma(T["ls%d" % t][:, 0:64], T["Fs%d" % t][:, 0:64], arr, T.sem.snt, pid, rid, mask)
-        count["snt"] = count.get("snt", 0) + 2 * len(engs)
-        count["arr%d" % t] = 2 * len(engs)
-        note("arr%d" % t, 2 * len(engs), [], [V("lc%d" % t, 0, 64), V("ls%d" % t, 0, 64)])
-        if t == 0:
-            later()
+            tt(V("F", b, 256, 4), V("Th", 512 * b, 512 * b + 512), V("TE", 64 * b, 64 * b + 64), OP.add, l=QL)
+        quant(V("Fq%d" % t), V("Fs%d" % t), V("F"))
+        send(t)
+        scan(V("rmx", 1, 129), V("NR"), V("M"), 1e25, OP.add, OP.max)
         diag(V("tsb", 0, 128), V("nPL"), V("tmb", 0, 128), 128)
         ts(V("sm", 24, 32), V("tsb", 15, 128, 16), -2.0, 273.0, OP.mult, OP.add)
         ts(V("sm", 32, 40), V("si", 8, 16), 512.0, None, OP.is_lt)
@@ -380,8 +424,8 @@ def rank_program(g, core, T, topo):
         scan(V("rm"), V("Sw", 8, 264), V("BB1"), -1e26, OP.min, OP.max)
         scan(V("lm", 255, -1, -1), V("Sw", 263, 7, -1), V("BB2", 255, -1, -1), -1e25, OP.min, OP.max)
         tt(V("D"), V("rm"), V("lm"), OP.is_ge)
-        scan(V("D", 255, -1, -1), V("nW", 255, -1, -1), V("D", 255, -1, -1), 1.0, OP.max, OP.min)
-        scan(V("vl"), V("D"), V("bv"), 0.0, OP.mult, OP.add)
+        scan(V("D2", 255, -1, -1), V("nW", 255, -1, -1), V("D", 255, -1, -1), 1.0, OP.max, OP.min)
+        scan(V("vl"), V("D2"), V("bv"), 0.0, OP.mult, OP.add)
         ts(V("uu"), V("vl"), 0.0, None, OP.is_equal)
         scan(V("hv", 255, -1, -1), V("uu", 255, -1, -1), V("vl", 255, -1, -1), 0.0, OP.mult, OP.add)
         diag(V("tsb"), V("hv"), V("tmb"), 256)
@@ -390,23 +434,22 @@ def rank_program(g, core, T, topo):
             act(V("s64"), V("col"), AF.Copy, l=EL)
             act(V("out"), V("s64"), AF.Copy, l=HL)
             dma("s", T.ol[:, :], T.out[0:128:16, :], [V("out")], [])
-            for b in range(3):
-                act(V("Tf", 256 * b, 256 * b + 256), V("pst", 512 * b, 512 * b + 256), AF.Copy)
         X = "X%d" % ((t + 1) % 2)
-        for b in (3, 0, 1, 2):
-            o = "psr" if b == 3 else "pst"
-            k = 0 if b == 3 else 512 * b
+        for b in (3, 2, 0, 1):
+            o, k = {3: ("psr", 0), 2: ("pss", 0)}.get(b, ("pst", 512 * b))
             mm(V(o, k, k + 128), V("wq", 128 * b, 128 * b + 128), V("wp", 128 * b, 128 * b + 128), V("lc%d" % t), V("ls%d" % t))
             act(V("H", 64 * b, 64 * b + 64), V(o, k, k + 64), AF.Relu, scale=0.03125)
-        act(V("G3"), V("H", 192, 256), AF.Copy, l=HL)
-        for b in range(3):
+        for b in (3, 2):
+            act(V("G3", 256 * (b - 2), 256 * (b - 1)), V("H", 64 * b, 64 * b + 64), AF.Copy, l=HL)
+        for b in range(2):
             tt(V(X, b, 1024, 4), V("H", 64 * b, 64 * b + 64), V("Tf", 256 * b, 256 * b + 256), OP.add, l=HL)
-        tt(V(X, 3, 1024, 4), V("pst", 1536, 1792), V("G3"), OP.add)
+        for b in (3, 2):
+            tt(V(X, b, 1024, 4), V("pst", 512 * b, 512 * b + 256), V("G3", 256 * (b - 2), 256 * (b - 1)), OP.add)
     quant(XQ, XS, V("X%d" % (R % 2)))
+    mm(S, V("vq"), V("vs"), XQ, XS)
     dma("s", T.oc[:, :], T.XQ[:, :].bitcast(dt.uint8), [XQ], [])
     for k in range(4):
         dma("a" if k % 2 else "s", T.osc[4 * k:4 * k + 4, :], T.XS[32 * k:32 * k + 4, :], [XS], [])
-    mm(S, V("vq"), V("vs"), XQ, XS)
     copy(V("yb"), S)
     dma("s", T.y[:, :], T.yb[:, :], [V("yb")], [])
-    finish()
+    issue()

@@ -7,22 +7,22 @@ C, K, R = 256, 64, 3
 STEP = [1, 2, 4]
 F32, B16, I32, U16, U8, MX = "float32", "bfloat16", "int32", "uint16", "uint8", "float8_e4m3fn_x4"
 INIT = float(2 ** 20 + 256)
-CYCLE, FIXED, WAKE = 0.83, 60.0, 100.0
+CYCLE, FIXED, WAKE, NET = 0.83, 0.0, 190.0, 3500.0
 
 _SB = {
     F32: {"cf": 256, "jc": 128, "iw": 776, "col": 256, "sm": 64, "Sw": 1032, "M": 128, "VV": 128, "PK": 128, "tm": 128, "tmM": 128, "tmK": 128,
-          "tmN": 128, "tsV": 128, "tsM": 128, "tsN": 128, "tsK": 128, "JL": 128, "nkL": 128, "nkR": 128, "RL": 128, "RR": 128, "sad": 128, "Gp": 128,
-          "np": 128, "cm": 128, "yk": 128, "ct": 256, "g64": 64, "s64": 64, "H": 256, "G3": 512, "rmx": 136, "rm": 256, "lm": 256, "out": 256,
+          "tmN": 128, "tsV": 128, "tsM": 128, "tsN": 128, "tsK": 128, "JL": 128, "nkL": 128, "nkR": 128, "RL": 128, "RR": 128, "Gp": 128,
+          "np": 128, "SR": 128, "ct": 256, "CG": 256, "g64": 64, "s64": 64, "H": 256, "G3": 512, "rmx": 136, "rm": 256, "lm": 256, "out": 256,
           "yb": 256},
     B16: {"X0": 1024, "X1": 1024, "ut": 512, "vt": 512, "et": 2048, "rbt": 512, "idn": 128, "mk": 256, "sg": 256, "ng": 128, "A": 272, "A2": 272,
-          "du": 256, "pk": 256, "npk": 256, "np2": 256, "ni": 256, "nf": 256, "th": 256, "hp": 128, "FV": 1024, "UL": 1024, "UR": 1024, "eqf": 128,
-          "pe": 128, "kept": 128, "K": 256, "pcw": 272, "ed": 256, "Tf": 512, "Th": 2048, "TE": 256, "F": 512, "NR": 128, "rec": 128, "rnk": 128,
-          "nPL": 128, "tmb": 256, "tsb": 256, "vLR": 128, "z": 128, "wl": 128, "uu": 256, "Bar": 256, "bv": 256, "BB1": 256, "BB2": 256, "D": 256,
-          "D2": 256, "nW": 256, "vl": 256, "hv": 256},
-    I32: {"ci": 256, "cj": 256, "si": 32},
+          "du": 256, "pk": 256, "npk": 256, "np2": 256, "ni": 256, "nf": 256, "th": 256, "th2": 256, "hp": 128, "FV": 1024, "FE": 512, "UL": 1024,
+          "UR": 1024, "kept": 128, "K": 256, "pcw": 272, "ed": 256, "ec": 256, "Tf": 512, "Th": 2048, "TE": 256, "F": 512, "NR": 128, "rec": 128,
+          "rnk": 128, "nPL": 128, "tmb": 256, "tsb": 256, "vLR": 128, "z": 128, "wl": 128, "uu": 256, "Bar": 256, "bv": 256, "BB1": 256, "BB2": 256,
+          "D": 256, "D2": 256, "nW": 256, "vl": 256, "hv": 256},
+    I32: {"ci": 256, "cj": 256},
     U16: {"su": 64},
-    MX: {"uq0": 128, "uq": 128, "vq": 128, "wq": 512, "eq": 512, "rbq": 128, "zq": 128, "FVq": 256, "XQ": 256},
-    U8: {"us0": 128, "us": 128, "vs": 128, "wp": 512, "es": 512, "rbs": 128, "zs": 128, "FVs": 256, "XS": 256},
+    MX: {"uq0": 128, "uq": 128, "vq": 128, "wq": 512, "eq": 512, "rbq": 128, "zq": 128, "FVq": 256, "FEq": 128, "XQ": 256},
+    U8: {"us0": 128, "us": 128, "vs": 128, "wp": 512, "es": 512, "rbs": 128, "zs": 128, "FVs": 256, "FEs": 128, "XS": 256},
 }
 SCRATCH = {n: ("sbuf", [128, w], d) for d, l in _SB.items() for n, w in l.items()}
 for _t in range(R):
@@ -54,14 +54,14 @@ def planner(g, T):
             return False
         return not (s == r and s > 1 and (a - c) % s)
 
-    def add(q, call, reads, writes, cost, hold=None, sem=None, inc=1):
-        i, pre = len(ops), set()
+    def add(q, call, reads, writes, cost, hold=None, sem=None, inc=1, adds=False):
+        i, pre = len(ops), {}
         for kind, vs in (("r", reads), ("w", writes)):
             for v in vs:
                 x = span(v)
                 for (y, k2, j) in log.get(x[0], []):
                     if meet(x, y) and (kind == "w" or k2 == "w" or (x[0] in _PS and ops[j]["q"] != q)):
-                        pre.add(j)
+                        pre[j] = pre.get(j, False) or not (adds and x[0] in _PS and ops[j]["q"] == q)
         for kind, vs in (("r", reads), ("w", writes)):
             for v in vs:
                 x = span(v)
@@ -78,7 +78,7 @@ def planner(g, T):
             for j in o["pre"]:
                 succ[j].append(i)
         for i in range(n - 1, -1, -1):
-            rank[i] = ops[i]["cost"] + max([rank[k] + WAKE for k in succ[i]], default=0.0)
+            rank[i] = ops[i]["cost"] + max([rank[k] + (WAKE if ops[k]["pre"][i] else 0.0) for k in succ[i]], default=0.0)
         ready, free, cand, out = [0.0] * n, {}, {}, []
         for i in range(n):
             if not left[i]:
@@ -99,7 +99,7 @@ def planner(g, T):
             out.append(i)
             free[q] = t + ops[i]["hold"]
             for k in succ[i]:
-                ready[k] = max(ready[k], t + ops[i]["cost"] + WAKE)
+                ready[k] = max(ready[k], t + ops[i]["cost"] + (WAKE if ops[k]["pre"][i] else 0.0))
                 left[k] -= 1
                 if not left[k]:
                     cand.setdefault(ops[k]["q"], []).append(k)
@@ -113,8 +113,9 @@ def planner(g, T):
             kn = known.setdefault(q, {})
             if q in eng:
                 want = {}
-                for j in o["pre"]:
-                    want[ops[j]["sem"]] = max(want.get(ops[j]["sem"], 0), at[j])
+                for j, w in o["pre"].items():
+                    if w:
+                        want[ops[j]["sem"]] = max(want.get(ops[j]["sem"], 0), at[j])
                 for s2, m in sorted(want.items()):
                     if kn.get(s2, 0) >= m:
                         continue
@@ -167,8 +168,8 @@ def rank_program(g, core, T, topo):
     def short(*vs):
         return all(SCRATCH[v[0]][2] in (B16, U16) for v in vs)
 
-    def do(q, call, reads, writes, cycles):
-        add(q, lambda e: call(e).then_inc(T.sem["q" + q], 1), reads, writes, max(64, cycles) * CYCLE + FIXED)
+    def do(q, call, reads, writes, cycles, adds=False):
+        add(q, lambda e: call(e).then_inc(T.sem["q" + q], 1), reads, writes, max(64, cycles) * CYCLE + FIXED, adds=adds)
 
     def dma(q, out, in_, reads, writes):
         s = "d%d" % nd[0]
@@ -215,7 +216,7 @@ def rank_program(g, core, T, topo):
         do("v", lambda e: e.quantize_mx(ap(q), ap(s), ap(x)), [x], [q, s], 14 + 0.265 * width(x))
 
     def mm(out, l, ls, r, rs, start=True, stop=True):
-        do("t", lambda e: e.matmul_mx(ap(out), ap(l), ap(ls), ap(r), ap(rs), start, stop), [l, ls, r, rs], [out], width(r) + 16)
+        do("t", lambda e: e.matmul_mx(ap(out), ap(l), ap(ls), ap(r), ap(rs), start, stop), [l, ls, r, rs], [out], width(r) + 16, not start)
 
     def iota(v, pat, base, cm):
         kw = {} if v[0] in ("ci", "cj") else {"allow_small_or_imprecise_dtypes": True}
@@ -232,7 +233,6 @@ def rank_program(g, core, T, topo):
         scan(out, V("sg", 0, n), tmp, 0.0, OP.mult, OP.add)
 
     LI, EL, QL, PL, HL, UO = V("su", 0, 8), V("su", 8, 12), V("su", 12, 16), V("su", 16, 24), V("su", 24, 40), V("su", 40, 48)
-    CS, TH = V("sm", 8, 9), V("sm", 9, 10)
 
     dma("s", ap(V("X0")), T.x[:, :], [], [V("X0")])
     dma("a", ap(V("ut")), T.u[:, :], [], [V("ut")])
@@ -273,7 +273,8 @@ def rank_program(g, core, T, topo):
     copy(V("cf", 0, 8), V("cj", 0, 8))
     for m in range(4):
         ts(V("sm", m, m + 1), V("cf", 0, 1), 16.0 * m + 0.5, None, OP.add)
-    for n, c in (("A", 0.0), ("nW", 1.0), ("RL", INIT), ("RR", INIT), ("nPL", 200.0), ("rmx", 1e25), ("F", 0.0), ("UL", 0.0), ("pcw", 0.0)):
+    ts(V("sm", 48, 64), V("col", 0, 16), V("cf", 0, 1), -5e29, OP.is_ge, OP.mult)
+    for n, c in (("A", 0.0), ("nW", 1.0), ("RL", INIT), ("RR", INIT), ("nPL", 200.0), ("rmx", 1e25), ("F", 0.0), ("FE", 0.0), ("pcw", 0.0)):
         fill(V(n), c)
     fill(V("rbt"), 0.0)
     quant(V("zq"), V("zs"), V("rbt"))
@@ -295,20 +296,24 @@ def rank_program(g, core, T, topo):
         def call(e):
             e.remote_dma(T["lc%d" % t][:, 0:64].bitcast(dt.uint8), T["Fq%d" % t][:, 0:64].bitcast(dt.uint8), arr, T.sem.snt, pid, rid, mask)
             e.remote_dma(T["ls%d" % t][:, 0:64], T["Fs%d" % t][:, 0:64], arr, T.sem.snt, pid, rid, mask)
-        add("g", call, [V("Fq%d" % t), V("Fs%d" % t)], [], 1500.0, 1500.0, "snt", 2 * len(engs))
-        add("in", None, [V("Fq%d" % t)], [V("lc%d" % t, 0, 64), V("ls%d" % t, 0, 64)], 4000.0, 0.0, "arr%d" % t, 2 * len(engs))
+        add("g", call, [V("Fq%d" % t), V("Fs%d" % t)], [], NET, NET, "snt", 2 * len(engs))
+        add("in", None, [V("Fq%d" % t)], [V("lc%d" % t, 0, 64), V("ls%d" % t, 0, 64)], NET, 0.0, "arr%d" % t, 2 * len(engs))
 
     S, XQ, XS, P = V("pss", 0, 256), V("XQ"), V("XS"), V("psr", 0, 128)
     pc = V("pcw", 16, 272)
 
-    def ranks():
+    def ranks(more=False):
+        if more:
+            quant(V("FEq"), V("FEs"), V("FE"))
         quant(V("FVq"), V("FVs"), V("FV"))
         for h in range(2):
-            mm(P, V("rbq"), V("rbs"), V("FVq", 128 * h, 128 * h + 128), V("FVs", 128 * h, 128 * h + 128), h == 0, h == 1)
+            mm(P, V("rbq"), V("rbs"), V("FVq", 128 * h, 128 * h + 128), V("FVs", 128 * h, 128 * h + 128), h == 0, h == 1 and not more)
+        if more:
+            mm(P, V("rbq"), V("rbs"), V("FEq"), V("FEs"), False, True)
 
-    def slot(m):
-        b = 512 * (m // 4) + m % 4
-        return V("FV", b, 512 * (m // 4) + 512, 4)
+    def slot(m, a=0, b=128):
+        o = 512 * (m // 4) + m % 4
+        return V("FV", o + 4 * a, 512 * (m // 4) + 4 * b, 4)
 
     for t in range(R):
         quant(XQ, XS, V("X%d" % (t % 2)))
@@ -318,101 +323,99 @@ def rank_program(g, core, T, topo):
         diag(V("tsV"), V("VV"), V("tm"), 128)
         for m in range(8):
             act(slot(m), V("VV"), AF.Sign, bias=V("tsV", 16 * m + 15, 16 * m + 16), scale=-1.0)
-        tt(V("A", 0, 256), S, V("Sw", 7, 263), OP.is_gt)
         tt(V("M"), V("pss", 0, 256, 2), V("Sw", 9, 264, 2), OP.max)
+        diag(V("tsM"), V("M"), V("tmM"), 128)
+        tt(V("A", 0, 256), S, V("Sw", 7, 263), OP.is_gt)
         for b in range(4):
             mm(V("pst", 512 * b, 512 * b + 256), V("eq", 128 * b, 128 * b + 128), V("es", 128 * b, 128 * b + 128), XQ, XS)
+        tt(V("JL"), V("jc"), V("A", 0, 256, 2), OP.subtract)
+        for m in range(8):
+            s = V("tsM", 16 * m + 15, 16 * m + 16)
+            ts(V("UL", 128 * m, 128 * m + 16 * m + 16), V("M", 0, 16 * m + 16), s, None, OP.is_lt)
+            ts(V("UR", 128 * m + 16 * m, 128 * m + 128), V("M", 16 * m, 128), s, None, OP.is_le)
+        ranks()
+        tt(V("nkL"), P, V("JL"), OP.add)
+        act(V("nkR"), V("nkL"), AF.Copy, bias=512.0)
         act(V("A2", 0, 257), V("A", 0, 257), AF.Copy, bias=2.0)
         scan(V("du"), V("A2", 0, 256), V("A2", 1, 257), 0.0, OP.max, OP.subtract)
         tt(V("hp"), V("du", 0, 256, 2), V("du", 1, 256, 2), OP.max)
         ts(V("hp"), V("hp"), 1.0, 1e29, OP.subtract, OP.mult)
         tt(V("PK"), V("M"), V("hp"), OP.add)
-        diag(V("tsM"), V("PK"), V("tmM"), 128)
         tt(V("nW", 1, 256), V("pss", 0, 255), V("Sw", 10, 265), OP.is_ge)
-        for m in range(7, -1, -1):
-            act(V("UL", 128 * m, 128 * m + 16 * m + 16), V("M", 0, 16 * m + 16), AF.Relu, bias=V("tsM", 16 * m + 15, 16 * m + 16), scale=-1.0)
-        act(V("UL"), V("UL"), AF.Sign)
-        ranks()
-        tt(V("JL"), V("jc"), V("A", 0, 256, 2), OP.subtract)
-        for m in range(8):
-            ts(V("UR", 128 * m + 16 * m, 128 * m + 128), V("M", 16 * m, 128), V("tsM", 16 * m + 15, 16 * m + 16), None, OP.is_le)
         act(V("Sw", 520, 776), V("Sw", 8, 264), AF.Copy)
         act(V("pk"), V("du"), AF.Relu)
         act(V("npk"), V("pk"), AF.Copy, bias=1.0, scale=-1.0)
-        act(V("np2"), V("pk"), AF.Copy, bias=2.0, scale=-1.0)
+        act(V("np2"), V("pk"), AF.Copy, bias=131072.0, scale=-65536.0)
         for b in range(4):
             act(V("Th", 512 * b, 512 * b + 256), V("pst", 512 * b, 512 * b + 256), AF.Copy, scale=0.5)
             act(V("Th", 512 * b + 256, 512 * b + 512), V("Th", 512 * b, 512 * b + 256), AF.Copy)
-        tt(V("nkL"), P, V("JL"), OP.add)
-        act(V("nkR"), V("nkL"), AF.Copy, bias=512.0)
         for m in range(7, -1, -1):
             n = 16 * m + 15
             scan(V("RL", 1, n + 1), V("UL", 128 * m, 128 * m + n), V("nkL", 1, n + 1), INIT, OP.mult, OP.max)
         for m in range(8):
             a = 16 * m
             scan(V("RR", 126, a - 1, -1), V("UR", 128 * m + 127, 128 * m + a, -1), V("nkR", 127, a, -1), INIT, OP.mult, OP.max)
-        tt(V("sad"), V("RL"), V("RR"), OP.min)
-        diag(V("tsK"), V("sad"), V("tmK"), 128)
-        copy(V("si", 0, 8), V("tsK", 15, 128, 16))
-        bits(V("si", 8, 16), V("si", 0, 8), 1023)
-        copy(LI, V("si", 8, 16))
+        tt(V("ci", 0, 128), V("RL"), V("RR"), OP.min)
+        bits(V("cj", 0, 128), V("ci", 0, 128), 1023)
+        diag(V("tsK"), V("cj", 0, 128), V("tmK"), 128)
+        copy(LI, V("tsK", 15, 128, 16))
         tt(V("np"), V("Sw", 8, 784), V("PK"), OP.subtract, l=LI)
         diag(V("tsN"), V("np"), V("tmN"), 128)
-        for m in range(5, 8):
-            act(slot(m), V("np"), AF.Relu, bias=V("tsN", 16 * m + 15, 16 * m + 16), scale=-1.0)
-            act(slot(m), slot(m), AF.Sign)
-        for m in range(5):
-            ts(slot(m), V("np"), V("tsN", 16 * m + 15, 16 * m + 16), None, OP.is_lt)
-        ranks()
+        for m in range(8):
+            act(V("SR", 16 * m, 16 * m + 16), V("sm", 48, 64), AF.Identity, bias=V("tsN", 16 * m + 15, 16 * m + 16))
+        act(slot(0), V("np"), AF.Relu, bias=V("tsN", 15, 16), scale=-1.0)
+        act(slot(0), slot(0), AF.Sign)
+        for m in range(1, 8):
+            s = V("tsN", 16 * m + 15, 16 * m + 16)
+            ts(slot(m, 0, 16 * m), V("np", 0, 16 * m), s, None, OP.is_le)
+            ts(slot(m, 16 * m, 128), V("np", 16 * m, 128), s, None, OP.is_lt)
+        tt(V("FE", 0, 512, 4), V("np"), V("SR"), OP.is_equal)
+        ranks(True)
         act(V("Gp"), V("iw"), AF.Copy, l=LI)
         scan(V("ni"), V("npk"), V("npk"), 0.0, OP.add, OP.max)
-        ts(V("sm", 10, 11), V("ni", 255, 256), -4.0, 768.0, OP.mult, OP.add)
-        act(V("nf"), V("ni"), AF.Relu, bias=V("sm", 10, 11), scale=4.0)
+        ts(V("sm", 10, 11), V("ni", 255, 256), -float(2 ** 20), 192.0 * 2 ** 20, OP.mult, OP.add)
+        act(V("nf"), V("ni"), AF.Relu, bias=V("sm", 10, 11), scale=float(2 ** 20))
         scan(V("th"), V("nf"), V("np2"), 0.0, OP.max, OP.min)
+        act(V("th2"), V("th"), AF.Copy, scale=2.0 ** -16)
         for m in range(7, -1, -1):
             n = 16 * m + 15
             scan(V("nPL", 1, n + 1), V("UL", 128 * m, 128 * m + n), V("ng", 0, n), 200.0, OP.mult, OP.max)
-        ts(V("eqf"), P, 65536.0, None, OP.is_lt)
-        tt(V("cm"), P, V("eqf"), OP.mult)
-        do("v", lambda e: e.tensor_reduce(ap(CS), T.cm[:, 0:128], AX, OP.max), [V("cm")], [CS], 128)
-        ts(V("eqf"), P, CS, None, OP.is_equal)
-        ts(TH, CS, 1.0 - 1.0 / 1024, 65.0, OP.mult, OP.add)
-        scan(V("pe", 127, -1, -1), V("eqf", 127, -1, -1), V("eqf", 127, -1, -1), 0.0, OP.add, OP.max)
-        tt(V("yk"), P, V("pe"), OP.add)
-        ts(V("kept"), V("yk"), TH, None, OP.is_ge)
-        act(V("NR"), V("kept"), AF.Copy, scale=-1e29)
         for p in range(2):
-            tt(V("K", p, 256, 2), V("kept"), V("th", p, 256, 2), OP.is_ge)
+            tt(V("K", p, 256, 2), P, V("th", p, 256, 2), OP.is_ge)
         scan(pc, V("K"), V("K"), 0.0, OP.add, OP.max)
-        for m in range(4):
+        ts(V("ec"), pc, V("sm", 0, 1), None, OP.is_le)
+        do("v", lambda e: e.tensor_reduce(T.sm[:, 16:17], T.ec[:, :], AX, OP.add), [V("ec")], [V("sm", 16, 17)], 256)
+        for m in range(1, 4):
             act(V("ed"), pc, AF.Sign, bias=V("sm", m, m + 1), scale=-1.0, acc=V("sm", 16 + m, 17 + m))
+        copy(V("su", 8, 9), V("sm", 16, 17))
+        ts(V("su", 9, 12), V("sm", 17, 20), 0.5, 128.0, OP.mult, OP.add)
         for b in range(2):
             act(V("Tf", 256 * b, 256 * b + 256), V("pst", 512 * b, 512 * b + 256), AF.Copy)
-        for p in range(2):
-            tt(V("ct", p, 256, 2), V("Gp"), V("pk", p, 256, 2), OP.mult)
-        ts(EL, V("sm", 16, 20), 0.5, 128.0, OP.mult, OP.add)
-        act(V("sm", 40, 44), V("sm", 16, 20), AF.Copy, bias=128.0, scale=0.5)
         for b in range(4):
             act(V("TE", 64 * b, 64 * b + 64), V("Th", 512 * b, 512 * b + 256), AF.Copy, l=EL)
-        tt(V("g64"), V("ct"), V("mk", 0, 64), OP.mult, l=EL)
+        for p in range(2):
+            tt(V("ct", p, 256, 2), V("Gp"), V("pk", p, 256, 2), OP.mult)
+        tt(V("CG"), V("ct"), V("col"), OP.max)
+        tt(V("g64"), V("CG"), V("mk", 0, 64), OP.mult, l=EL)
         scan(V("s64"), V("sg", 0, 64), V("g64"), 0.0, OP.mult, OP.add)
-        tt(V("sm", 44, 48), V("s64", 15, 64, 16), V("sm", 40, 44), OP.max)
-        copy(QL, V("sm", 44, 48))
+        copy(QL, V("s64", 15, 64, 16))
         for b in range(4):
             tt(V("F", b, 256, 4), V("Th", 512 * b, 512 * b + 512), V("TE", 64 * b, 64 * b + 64), OP.add, l=QL)
         quant(V("Fq%d" % t), V("Fs%d" % t), V("F"))
         send(t)
+        ts(V("kept"), P, 65536.0, None, OP.is_ge)
+        act(V("NR"), V("kept"), AF.Copy, scale=-1e29)
         scan(V("rmx", 1, 129), V("NR"), V("M"), 1e25, OP.add, OP.max)
         diag(V("tsb", 0, 128), V("nPL"), V("tmb", 0, 128), 128)
         ts(V("sm", 24, 32), V("tsb", 15, 128, 16), -2.0, 273.0, OP.mult, OP.add)
-        ts(V("sm", 32, 40), V("si", 8, 16), 512.0, None, OP.is_lt)
+        ts(V("sm", 32, 40), V("tsK", 15, 128, 16), 512.0, None, OP.is_lt)
         tt(V("sm", 24, 32), V("sm", 24, 32), V("sm", 32, 40), OP.mult)
         copy(PL, V("sm", 24, 32))
         act(V("vLR"), V("pcw"), AF.Copy, l=PL)
         tt(V("rec"), V("PK"), V("rmx", 0, 128), OP.is_gt)
         tt(V("z"), V("rec"), V("kept"), OP.max)
         for p in range(2):
-            tt(V("Bar", p, 256, 2), V("z"), V("th", p, 256, 2), OP.is_ge)
+            tt(V("Bar", p, 256, 2), V("z"), V("th2", p, 256, 2), OP.is_ge)
         act(V("BB1"), V("Bar"), AF.Copy, bias=-1e29, scale=1.1e29)
         act(V("BB2"), V("Bar"), AF.Copy, bias=-1e29, scale=2e29)
         tt(V("rnk"), V("rec"), V("kept"), OP.is_gt)

@@ -7,17 +7,17 @@ C, K, R = 256, 64, 3
 STEP = [1, 2, 4]
 F32, B16, I32, U16, U8, MX = "float32", "bfloat16", "int32", "uint16", "uint8", "float8_e4m3fn_x4"
 INIT = float(2 ** 20 + 256)
-CYCLE, FIXED, WAKE, NET = 0.83, 0.0, 190.0, 3500.0
+CYCLE, FIXED, WAKE, NET, TRIES = 0.83, 0.0, 190.0, 3500.0, 48
 
 _SB = {
     F32: {"cf": 256, "jc": 128, "iw": 776, "col": 256, "sm": 64, "Sw": 1032, "M": 128, "VV": 128, "PK": 128, "tm": 128, "tmM": 128, "tmK": 128,
-          "tmN": 128, "tsV": 128, "tsM": 128, "tsN": 128, "tsK": 128, "JL": 128, "nkL": 128, "nkR": 128, "RL": 128, "RR": 128, "Gp": 128,
+          "tmN": 128, "tsV": 128, "tsM": 128, "tsN": 128, "tsK": 128, "JL": 128, "nkL": 128, "nkR": 128, "Gp": 128,
           "np": 128, "SR": 128, "ct": 256, "CG": 256, "g64": 64, "s64": 64, "H": 256, "G3": 512, "rmx": 136, "rm": 256, "lm": 256, "out": 256,
           "yb": 256},
     B16: {"X0": 1024, "X1": 1024, "ut": 512, "vt": 512, "et": 2048, "rbt": 512, "idn": 128, "mk": 256, "sg": 256, "ng": 128, "A": 272, "A2": 272,
           "du": 256, "pk": 256, "npk": 256, "np2": 256, "ni": 256, "nf": 256, "th": 256, "th2": 256, "hp": 128, "FV": 1024, "FE": 512, "UL": 1024,
           "UR": 1024, "kept": 128, "K": 256, "pcw": 272, "ed": 256, "ec": 256, "Tf": 512, "Th": 2048, "TE": 256, "F": 512, "NR": 128, "rec": 128,
-          "rnk": 128, "nPL": 128, "tmb": 256, "tsb": 256, "vLR": 128, "z": 128, "wl": 128, "uu": 256, "Bar": 256, "bv": 256, "BB1": 256, "BB2": 256,
+          "rnk": 128, "tmb": 256, "tsb": 256, "vLR": 128, "z": 128, "wl": 128, "uu": 256, "Bar": 256, "bv": 256, "BB1": 256, "BB2": 256,
           "D": 256, "D2": 256, "nW": 256, "vl": 256, "hv": 256},
     I32: {"ci": 256, "cj": 256},
     U16: {"su": 64},
@@ -28,6 +28,10 @@ SCRATCH = {n: ("sbuf", [128, w], d) for d, l in _SB.items() for n, w in l.items(
 for _t in range(R):
     for _n, _d in (("Fq", MX), ("Fs", U8), ("lc", MX), ("ls", U8)):
         SCRATCH["%s%d" % (_n, _t)] = ("sbuf", [128, 128], _d)
+BW = 136
+_BLOCKS = ("RL", "RR", "NP")
+for _n, _d in (("RL", F32), ("RR", F32), ("NP", B16)):
+    SCRATCH[_n] = ("sbuf", [128, 8, BW], _d)
 SCRATCH["pss"] = ("psum", [128, 512], F32)
 SCRATCH["psr"] = ("psum", [128, 512], F32)
 SCRATCH["pst"] = ("psum", [128, 2048], F32)
@@ -43,6 +47,8 @@ def planner(g, T):
         n, a, b, s = v
         if n in _PS:
             return n, a // 512 * 512, (b + 511) // 512 * 512, 1
+        if s == 0:
+            return n, 0, 8 * BW, 1
         if s < 0:
             k = (a - b + (-s) - 1) // (-s)
             return n, a + s * (k - 1), a + 1, -s
@@ -71,15 +77,10 @@ def planner(g, T):
                 l.append((x, kind, i))
         ops.append({"q": q, "call": call, "pre": pre, "cost": cost, "hold": cost if hold is None else hold, "sem": sem or "q" + q, "inc": inc})
 
-    def order():
+    def order(succ, rank, patience):
         n = len(ops)
-        succ, left, rank = [[] for _ in range(n)], [len(o["pre"]) for o in ops], [0.0] * n
-        for i, o in enumerate(ops):
-            for j in o["pre"]:
-                succ[j].append(i)
-        for i in range(n - 1, -1, -1):
-            rank[i] = ops[i]["cost"] + max([rank[k] + (WAKE if ops[k]["pre"][i] else 0.0) for k in succ[i]], default=0.0)
-        ready, free, cand, out = [0.0] * n, {}, {}, []
+        left = [len(o["pre"]) for o in ops]
+        ready, free, cand, out, end = [0.0] * n, {}, {}, [], 0.0
         for i in range(n):
             if not left[i]:
                 cand.setdefault(ops[i]["q"], []).append(i)
@@ -89,8 +90,8 @@ def planner(g, T):
                 if not l:
                     continue
                 f = free.get(q, 0.0)
-                t = min(max(f, ready[i]) for i in l)
-                i = max([i for i in l if max(f, ready[i]) <= t + 15.0], key=lambda i: (rank[i], -i))
+                t = max(f, min(ready[i] for i in l)) + patience
+                i = max([i for i in l if ready[i] <= t], key=lambda i: rank[i])
                 t = max(f, ready[i])
                 if best is None or (t, -rank[i]) < best[0]:
                     best = ((t, -rank[i]), q, i)
@@ -98,16 +99,35 @@ def planner(g, T):
             cand[q].remove(i)
             out.append(i)
             free[q] = t + ops[i]["hold"]
-            for k in succ[i]:
-                ready[k] = max(ready[k], t + ops[i]["cost"] + (WAKE if ops[k]["pre"][i] else 0.0))
+            done = t + ops[i]["cost"]
+            end = max(end, done)
+            for k, w in succ[i]:
+                ready[k] = max(ready[k], done + w)
                 left[k] -= 1
                 if not left[k]:
                     cand.setdefault(ops[k]["q"], []).append(k)
-        return out
+        return end, out
+
+    def best_order():
+        n = len(ops)
+        succ, rank = [[] for _ in range(n)], [0.0] * n
+        for i, o in enumerate(ops):
+            for j, w in o["pre"].items():
+                succ[j].append((i, WAKE if w else 0.0))
+        for i in range(n - 1, -1, -1):
+            rank[i] = ops[i]["cost"] + max([rank[k] + w for k, w in succ[i]], default=0.0)
+        best = None
+        for k in range(TRIES):
+            rng = np.random.default_rng(k)
+            noise = [float(x) for x in rng.random(n) * (0.0, 100.0, 300.0, 800.0)[k // 4 % 4]]
+            got = order(succ, [r + x for r, x in zip(rank, noise)], (0.0, 20.0, 50.0, 100.0)[k % 4])
+            if best is None or got[0] < best[0]:
+                best = got
+        return best[1]
 
     def issue():
         count, at, known, snap = {}, {}, {q: {} for q in eng}, {}
-        for i in order():
+        for i in best_order():
             o = ops[i]
             q, s = o["q"], o["sem"]
             kn = known.setdefault(q, {})
@@ -147,8 +167,17 @@ def rank_program(g, core, T, topo):
             return (n, 0, SCRATCH[n][1][1], 1)
         return (n, a, b, s)
 
+    def B(n, m, a, b, s=1):
+        return (n, BW * m + a, BW * m + b, s)
+
     def ap(v):
         n, a, b, s = v
+        if n in _BLOCKS:
+            if s == 0:
+                return T[n][:, :, a:b]
+            m = a // BW
+            a, b = a - BW * m, b - BW * m
+            return T[n][:, m, a:b] if s == 1 else T[n][:, m, a:(b if b >= 0 else None):s]
         if s < 0:
             return T[n][:, a:(b if b >= 0 else None):s]
         return T[n][:, a:b:s] if s != 1 else T[n][:, a:b]
@@ -163,7 +192,7 @@ def rank_program(g, core, T, topo):
         return [x for x in xs if isinstance(x, tuple)]
 
     def width(v):
-        return len(range(v[1], v[2], v[3]))
+        return len(range(v[1], v[2], v[3])) if v[3] else 8 * (v[2] - v[1])
 
     def short(*vs):
         return all(SCRATCH[v[0]][2] in (B16, U16) for v in vs)
@@ -274,8 +303,9 @@ def rank_program(g, core, T, topo):
     for m in range(4):
         ts(V("sm", m, m + 1), V("cf", 0, 1), 16.0 * m + 0.5, None, OP.add)
     ts(V("sm", 48, 64), V("col", 0, 16), V("cf", 0, 1), -5e29, OP.is_ge, OP.mult)
-    for n, c in (("A", 0.0), ("nW", 1.0), ("RL", INIT), ("RR", INIT), ("nPL", 200.0), ("rmx", 1e25), ("F", 0.0), ("FE", 0.0), ("pcw", 0.0)):
-        fill(V(n), c)
+    for v, c in ((V("A"), 0.0), (V("nW"), 1.0), (B("RL", 0, 120, 121), INIT), (B("RR", 7, 15, 16), INIT), (B("NP", 0, 120, 121), 200.0),
+                 (V("rmx"), 1e25), (V("F"), 0.0), (V("FE"), 0.0), (V("pcw"), 0.0)):
+        fill(v, c)
     fill(V("rbt"), 0.0)
     quant(V("zq"), V("zs"), V("rbt"))
     for t in range(R):
@@ -318,7 +348,8 @@ def rank_program(g, core, T, topo):
     for t in range(R):
         quant(XQ, XS, V("X%d" % (t % 2)))
         mm(S, V("uq"), V("us"), XQ, XS)
-        copy(V("Sw", 8, 264), S)
+        copy(V("Sw", 9, 264, 2), V("pss", 1, 256, 2))
+        copy(V("Sw", 8, 264, 2), V("pss", 0, 256, 2))
         tt(V("VV"), V("pss", 0, 256, 2), V("Sw", 7, 263, 2), OP.min)
         diag(V("tsV"), V("VV"), V("tm"), 128)
         for m in range(8):
@@ -331,7 +362,7 @@ def rank_program(g, core, T, topo):
         tt(V("JL"), V("jc"), V("A", 0, 256, 2), OP.subtract)
         for m in range(8):
             s = V("tsM", 16 * m + 15, 16 * m + 16)
-            ts(V("UL", 128 * m, 128 * m + 16 * m + 16), V("M", 0, 16 * m + 16), s, None, OP.is_lt)
+            act(V("UL", 128 * m, 128 * m + 16 * m + 16), V("M", 0, 16 * m + 16), AF.Sign, bias=s, scale=-1.0)
             ts(V("UR", 128 * m + 16 * m, 128 * m + 128), V("M", 16 * m, 128), s, None, OP.is_le)
         ranks()
         tt(V("nkL"), P, V("JL"), OP.add)
@@ -351,11 +382,11 @@ def rank_program(g, core, T, topo):
             act(V("Th", 512 * b + 256, 512 * b + 512), V("Th", 512 * b, 512 * b + 256), AF.Copy)
         for m in range(7, -1, -1):
             n = 16 * m + 15
-            scan(V("RL", 1, n + 1), V("UL", 128 * m, 128 * m + n), V("nkL", 1, n + 1), INIT, OP.mult, OP.max)
+            scan(B("RL", m, BW - n, BW), V("UL", 128 * m, 128 * m + n), V("nkL", 1, n + 1), INIT, OP.mult, OP.max)
         for m in range(8):
             a = 16 * m
-            scan(V("RR", 126, a - 1, -1), V("UR", 128 * m + 127, 128 * m + a, -1), V("nkR", 127, a, -1), INIT, OP.mult, OP.max)
-        tt(V("ci", 0, 128), V("RL"), V("RR"), OP.min)
+            scan(B("RR", m, 126 - a, -1, -1), V("UR", 128 * m + 127, 128 * m + a, -1), V("nkR", 127, a, -1), INIT, OP.mult, OP.max)
+        tt(V("ci", 0, 128), V("RL", BW - 16, BW, 0), V("RR", 0, 16, 0), OP.min)
         bits(V("cj", 0, 128), V("ci", 0, 128), 1023)
         diag(V("tsK"), V("cj", 0, 128), V("tmK"), 128)
         copy(LI, V("tsK", 15, 128, 16))
@@ -379,7 +410,7 @@ def rank_program(g, core, T, topo):
         act(V("th2"), V("th"), AF.Copy, scale=2.0 ** -16)
         for m in range(7, -1, -1):
             n = 16 * m + 15
-            scan(V("nPL", 1, n + 1), V("UL", 128 * m, 128 * m + n), V("ng", 0, n), 200.0, OP.mult, OP.max)
+            scan(B("NP", m, BW - n, BW), V("UL", 128 * m, 128 * m + n), V("ng", 0, n), 200.0, OP.mult, OP.max)
         for p in range(2):
             tt(V("K", p, 256, 2), P, V("th", p, 256, 2), OP.is_ge)
         scan(pc, V("K"), V("K"), 0.0, OP.add, OP.max)
@@ -406,7 +437,7 @@ def rank_program(g, core, T, topo):
         ts(V("kept"), P, 65536.0, None, OP.is_ge)
         act(V("NR"), V("kept"), AF.Copy, scale=-1e29)
         scan(V("rmx", 1, 129), V("NR"), V("M"), 1e25, OP.add, OP.max)
-        diag(V("tsb", 0, 128), V("nPL"), V("tmb", 0, 128), 128)
+        diag(V("tsb", 0, 128), V("NP", BW - 16, BW, 0), V("tmb", 0, 128), 128)
         ts(V("sm", 24, 32), V("tsb", 15, 128, 16), -2.0, 273.0, OP.mult, OP.add)
         ts(V("sm", 32, 40), V("tsK", 15, 128, 16), 512.0, None, OP.is_lt)
         tt(V("sm", 24, 32), V("sm", 24, 32), V("sm", 32, 40), OP.mult)

@@ -7,36 +7,54 @@ C, K, R = 256, 64, 3
 STEP = [1, 2, 4]
 F32, B16, I32, U16, U8, MX = "float32", "bfloat16", "int32", "uint16", "uint8", "float8_e4m3fn_x4"
 INIT = float(2 ** 20 + 256)
-CYCLE, FIXED, WAKE, NET, TRIES = 0.83, 0.0, 190.0, 3500.0, 48
+LIFT, LIFT2 = float(2 ** 21), 128.0
+SPAN = C - K + 16
+CYCLE, FIXED, WAKE, NET = 0.83, 0.0, 190.0, 3500.0
+TRIES = 5000
+ORDERS = {}
 
 _SB = {
-    F32: {"cf": 256, "jc": 128, "iw": 776, "col": 256, "sm": 64, "Sw": 1032, "M": 128, "VV": 128, "PK": 128, "tm": 128, "tmM": 128, "tmK": 128,
-          "tmN": 128, "tsV": 128, "tsM": 128, "tsN": 128, "tsK": 128, "JL": 128, "nkL": 128, "nkR": 128, "Gp": 128,
-          "np": 128, "SR": 128, "ct": 256, "CG": 256, "g64": 64, "s64": 64, "H": 256, "G3": 512, "rmx": 136, "rm": 256, "lm": 256, "out": 256,
+    F32: {"sm": 64, "c8": 8, "Sw": 784, "M": 128, "VV": 128, "PK": 128, "tmV": 256,
+          "tmM": 128, "tmN": 128, "tsV": 256, "tsM": 128, "tsN": 128, "tRL": 128, "tRR": 128, "tNP": 128, "NJ": 128, "nkL": 128, "nkR": 136,
+          "Gp": 128, "np": 128, "ct": 256, "CG": 256, "g64": 64, "s64": 64, "H": 256, "G3": 512, "rmx": 136, "rm": 256, "lm": 256, "out": 256,
           "yb": 256},
-    B16: {"X0": 1024, "X1": 1024, "ut": 512, "vt": 512, "et": 2048, "rbt": 512, "idn": 128, "mk": 256, "sg": 256, "ng": 128, "A": 272, "A2": 272,
-          "du": 256, "pk": 256, "npk": 256, "np2": 256, "ni": 256, "nf": 256, "th": 256, "th2": 256, "hp": 128, "FV": 1024, "FE": 512, "UL": 1024,
-          "UR": 1024, "kept": 128, "K": 256, "pcw": 272, "ed": 256, "ec": 256, "Tf": 512, "Th": 2048, "TE": 256, "F": 512, "NR": 128, "rec": 128,
-          "rnk": 128, "tmb": 256, "tsb": 256, "vLR": 128, "z": 128, "wl": 128, "uu": 256, "Bar": 256, "bv": 256, "BB1": 256, "BB2": 256,
-          "D": 256, "D2": 256, "nW": 256, "vl": 256, "hv": 256},
-    I32: {"ci": 256, "cj": 256},
+    B16: {"X0": 1024, "X1": 1024, "ut": 512, "vt": 512, "et": 2048, "rbt": 512, "zt": 512, "one": 64, "idn": 128, "A": 272, "A2": 272,
+          "du": 256, "pk": 256, "npk": 256, "np2": 256, "ni": 256, "nf": 256, "th": 256, "th2": 256, "hp": 128, "FV": 1024, "FE": 512, "UL": 1040,
+          "UR": 1040, "K": 256, "pcw": 272, "ed": 416, "ec": 416, "cn": 416, "Tf": 512, "Th": 2048, "TE": 256, "F": 512,
+          "tsb": 256, "vLR": 128, "nW": 256, "vl": 256, "hv": 256},
     U16: {"su": 64},
     MX: {"uq0": 128, "uq": 128, "vq": 128, "wq": 512, "eq": 512, "rbq": 128, "zq": 128, "FVq": 256, "FEq": 128, "XQ": 256},
     U8: {"us0": 128, "us": 128, "vs": 128, "wp": 512, "es": 512, "rbs": 128, "zs": 128, "FVs": 256, "FEs": 128, "XS": 256},
 }
-SCRATCH = {n: ("sbuf", [128, w], d) for d, l in _SB.items() for n, w in l.items()}
+for _n, _d in (("RL", F32), ("RR", F32), ("NP", B16)):
+    for _h in "01":
+        _SB[_d][_n + _h] = 128
 for _t in range(R):
     for _n, _d in (("Fq", MX), ("Fs", U8), ("lc", MX), ("ls", U8)):
-        SCRATCH["%s%d" % (_n, _t)] = ("sbuf", [128, 128], _d)
-BW = 136
-_BLOCKS = ("RL", "RR", "NP")
-for _n, _d in (("RL", F32), ("RR", F32), ("NP", B16)):
-    SCRATCH[_n] = ("sbuf", [128, 8, BW], _d)
-SCRATCH["pss"] = ("psum", [128, 512], F32)
-SCRATCH["psr"] = ("psum", [128, 512], F32)
-SCRATCH["pst"] = ("psum", [128, 2048], F32)
-_PS = ("pss", "psr", "pst")
-SEMAPHORES = ["qv", "qa", "qt", "qg"] + ["d%d" % i for i in range(24)] + ["arr%d" % t for t in range(R)] + ["snt"]
+        _SB[_d]["%s%d" % (_n, _t)] = 128
+_JOINT = {
+    "kf": (F32, {"iw": 776, "cf": 256, "jc": 128, "col": 256, "cq": 8}),
+    "kb": (B16, {"mk": 256, "sg": 256, "ng": 144, "mP": 128, "rst": 128, "mkV": 256, "rstV": 256, "dL": 128, "dL2": 256, "mt": 256, "mu": 256}),
+    "ki": (I32, {"ci": 256, "cj": 256, "c0": 8, "c1": 8, "c2": 8}),
+    "rb": (B16, {"kept": 128, "NR": 128, "rec": 128, "rnk": 128, "z": 128, "wl": 128, "uu": 256, "u2": 256, "Bar": 256, "bv": 256, "BB1": 256,
+                 "BB2": 256, "D": 256, "D2": 256}),
+    "l8s": (I32, {"k8": 8, "l8": 8}),
+}
+WIDTH = {n: w for l in _SB.values() for n, w in l.items()}
+TYPE = {n: d for d, l in _SB.items() for n in l}
+PLACE = {}
+SCRATCH = {n: ("sbuf", [128, WIDTH[n]], TYPE[n]) for n in WIDTH}
+for _b, (_d, _l) in _JOINT.items():
+    _o = 0
+    for _n, _w in _l.items():
+        PLACE[_n], WIDTH[_n], TYPE[_n] = (_b, _o), _w, _d
+        _o += (_w + 31) // 32 * 32
+    SCRATCH[_b] = ("sbuf", [128, _o], _d)
+_PS = ("ps0", "ps1", "psr", "pst")
+for _n in _PS:
+    SCRATCH[_n] = ("psum", [128, 2048 if _n == "pst" else 512], F32)
+    TYPE[_n] = F32
+SEMAPHORES = ["qv", "qa", "qt", "qg"] + ["d%d" % i for i in range(48)] + ["arr%d" % t for t in range(R)] + ["snt"]
 
 
 def planner(g, T):
@@ -47,8 +65,6 @@ def planner(g, T):
         n, a, b, s = v
         if n in _PS:
             return n, a // 512 * 512, (b + 511) // 512 * 512, 1
-        if s == 0:
-            return n, 0, 8 * BW, 1
         if s < 0:
             k = (a - b + (-s) - 1) // (-s)
             return n, a + s * (k - 1), a + 1, -s
@@ -77,37 +93,6 @@ def planner(g, T):
                 l.append((x, kind, i))
         ops.append({"q": q, "call": call, "pre": pre, "cost": cost, "hold": cost if hold is None else hold, "sem": sem or "q" + q, "inc": inc})
 
-    def order(succ, rank, patience):
-        n = len(ops)
-        left = [len(o["pre"]) for o in ops]
-        ready, free, cand, out, end = [0.0] * n, {}, {}, [], 0.0
-        for i in range(n):
-            if not left[i]:
-                cand.setdefault(ops[i]["q"], []).append(i)
-        while any(cand.values()):
-            best = None
-            for q, l in cand.items():
-                if not l:
-                    continue
-                f = free.get(q, 0.0)
-                t = max(f, min(ready[i] for i in l)) + patience
-                i = max([i for i in l if ready[i] <= t], key=lambda i: rank[i])
-                t = max(f, ready[i])
-                if best is None or (t, -rank[i]) < best[0]:
-                    best = ((t, -rank[i]), q, i)
-            (t, _), q, i = best
-            cand[q].remove(i)
-            out.append(i)
-            free[q] = t + ops[i]["hold"]
-            done = t + ops[i]["cost"]
-            end = max(end, done)
-            for k, w in succ[i]:
-                ready[k] = max(ready[k], done + w)
-                left[k] -= 1
-                if not left[k]:
-                    cand.setdefault(ops[k]["q"], []).append(k)
-        return end, out
-
     def best_order():
         n = len(ops)
         succ, rank = [[] for _ in range(n)], [0.0] * n
@@ -116,18 +101,65 @@ def planner(g, T):
                 succ[j].append((i, WAKE if w else 0.0))
         for i in range(n - 1, -1, -1):
             rank[i] = ops[i]["cost"] + max([rank[k] + w for k, w in succ[i]], default=0.0)
-        best = None
+        names = sorted({o["q"] for o in ops})
+        qs = [names.index(o["q"]) for o in ops]
+        cost, hold, need = [o["cost"] for o in ops], [o["hold"] for o in ops], [len(o["pre"]) for o in ops]
+
+        def order(rk, patience):
+            left, ready, free, cand = need[:], [0.0] * n, [0.0] * len(names), [[] for _ in names]
+            pick, out, end = [None] * len(names), [], 0.0
+            for i in range(n):
+                if not left[i]:
+                    cand[qs[i]].append(i)
+            while True:
+                best = None
+                for q, l in enumerate(cand):
+                    if not l:
+                        continue
+                    if pick[q] is None:
+                        t = max(free[q], min([ready[i] for i in l])) + patience
+                        top, r = -1, -1e18
+                        for i in l:
+                            if ready[i] <= t and rk[i] > r:
+                                top, r = i, rk[i]
+                        pick[q] = (max(free[q], ready[top]), -r, top)
+                    if best is None or pick[q] < best[0]:
+                        best = (pick[q], q)
+                if best is None:
+                    return end, out
+                (t, _, i), q = best
+                cand[q].remove(i)
+                pick[q] = None
+                out.append(i)
+                free[q] = t + hold[i]
+                done = t + cost[i]
+                end = max(end, done)
+                for k, w in succ[i]:
+                    ready[k] = max(ready[k], done + w)
+                    left[k] -= 1
+                    if not left[k]:
+                        cand[qs[k]].append(k)
+                        pick[qs[k]] = None
+
+        rng, at, best = np.random.default_rng(0), np.arange(n), None
         for k in range(TRIES):
-            rng = np.random.default_rng(k)
-            noise = [float(x) for x in rng.random(n) * (0.0, 100.0, 300.0, 800.0)[k // 4 % 4]]
-            got = order(succ, [r + x for r, x in zip(rank, noise)], (0.0, 20.0, 50.0, 100.0)[k % 4])
-            if best is None or got[0] < best[0]:
-                best = got
+            if k < 200:
+                noise, patience = rng.random(n) * (0.0, 100.0, 300.0, 800.0)[k // 4 % 4], (0.0, 20.0, 50.0, 100.0)[k % 4]
+            else:
+                noise, patience = best[2].copy(), best[3] if k % 5 else 10.0 * (k // 5 % 11)
+                some = (np.abs(at - rng.integers(0, n)) < (5, 20, 60, 200)[k % 4]) & (rng.random(n) < (0.6, 0.3, 0.15, 0.1)[k % 4])
+                noise[some] += rng.normal(0.0, (100.0, 300.0, 800.0)[k % 3], int(some.sum()))
+            end, out = order([r + x for r, x in zip(rank, noise.tolist())], patience)
+            if best is None or end <= best[0]:
+                best = (end, out, noise, patience)
         return best[1]
 
     def issue():
+        key = str([(o["q"], o["cost"], sorted(o["pre"].items())) for o in ops])
+        if key not in ORDERS:
+            ORDERS[key] = best_order()
         count, at, known, snap = {}, {}, {q: {} for q in eng}, {}
-        for i in best_order():
+        for i in ORDERS[key]:
             o = ops[i]
             q, s = o["q"], o["sem"]
             kn = known.setdefault(q, {})
@@ -158,26 +190,20 @@ def rank_program(g, core, T, topo):
     rank = T.rank_of(core)
     if rank is None:
         return
-    OP, AF, AX = AluOpType, ActivationFunctionType, AxisListType.X
+    OP, AF = AluOpType, ActivationFunctionType
     add, issue = planner(g, T)
     nd = [0]
 
     def V(n, a=None, b=None, s=1):
         if a is None:
-            return (n, 0, SCRATCH[n][1][1], 1)
+            return (n, 0, WIDTH[n], 1)
         return (n, a, b, s)
-
-    def B(n, m, a, b, s=1):
-        return (n, BW * m + a, BW * m + b, s)
 
     def ap(v):
         n, a, b, s = v
-        if n in _BLOCKS:
-            if s == 0:
-                return T[n][:, :, a:b]
-            m = a // BW
-            a, b = a - BW * m, b - BW * m
-            return T[n][:, m, a:b] if s == 1 else T[n][:, m, a:(b if b >= 0 else None):s]
+        if n in PLACE:
+            n, o = PLACE[n]
+            a, b = a + o, b + o
         if s < 0:
             return T[n][:, a:(b if b >= 0 else None):s]
         return T[n][:, a:b:s] if s != 1 else T[n][:, a:b]
@@ -192,10 +218,10 @@ def rank_program(g, core, T, topo):
         return [x for x in xs if isinstance(x, tuple)]
 
     def width(v):
-        return len(range(v[1], v[2], v[3])) if v[3] else 8 * (v[2] - v[1])
+        return len(range(v[1], v[2], v[3]))
 
     def short(*vs):
-        return all(SCRATCH[v[0]][2] in (B16, U16) for v in vs)
+        return all(TYPE[v[0]] in (B16, U16) for v in vs)
 
     def do(q, call, reads, writes, cycles, adds=False):
         add(q, lambda e: call(e).then_inc(T.sem["q" + q], 1), reads, writes, max(64, cycles) * CYCLE + FIXED, adds=adds)
@@ -248,7 +274,7 @@ def rank_program(g, core, T, topo):
         do("t", lambda e: e.matmul_mx(ap(out), ap(l), ap(ls), ap(r), ap(rs), start, stop), [l, ls, r, rs], [out], width(r) + 16, not start)
 
     def iota(v, pat, base, cm):
-        kw = {} if v[0] in ("ci", "cj") else {"allow_small_or_imprecise_dtypes": True}
+        kw = {} if TYPE[v[0]] == I32 else {"allow_small_or_imprecise_dtypes": True}
         do("g", lambda e: e.iota(ap(v), pat, base, cm, **kw), [], [v], 160 + 2 * width(v))
 
     def select(v, pat, op, base, cm):
@@ -257,9 +283,8 @@ def rank_program(g, core, T, topo):
     def bits(out, a, n):
         do("v", lambda e: e.tensor_scalar(ap(out), ap(a), n, None, OP.bitwise_and), [a], [out], width(out))
 
-    def diag(out, src, tmp, n):
-        tt(tmp, src, V("mk", 0, n), OP.mult)
-        scan(out, V("sg", 0, n), tmp, 0.0, OP.mult, OP.add)
+    def dscan(out, src, lift):
+        scan(out, lift, src, 0.0, OP.add, OP.max)
 
     LI, EL, QL, PL, HL, UO = V("su", 0, 8), V("su", 8, 12), V("su", 12, 16), V("su", 16, 24), V("su", 24, 40), V("su", 40, 48)
 
@@ -269,45 +294,62 @@ def rank_program(g, core, T, topo):
     dma("a", ap(V("wp")), T.ws[:, :], [], [V("wp")])
     dma("s", ap(V("vt")), T.v[:, :], [], [V("vt")])
 
-    iota(V("ci", 0, 8), [[16, 8]], 0, 0)
-    copy(UO, V("ci", 0, 8))
     iota(V("ci"), [[1, 256]], 256, -1)
     bits(V("cj"), V("ci"), 15)
     copy(V("cf"), V("cj"))
     ts(V("mk"), V("cf"), 0.0, None, OP.is_equal)
-    iota(V("col"), [[0, 16], [1, 16]], 0, 0)
-    ts(V("sg"), V("col"), 1.0, None, OP.min)
-    fill(V("Sw"), -1e25)
+    iota(V("c0"), [[16, 8]], 0, 0)
+    copy(UO, V("c0"))
+    for n, w, k, c0, c in (("sg", 256, 16, 0.0, 1.0), ("rst", 128, 16, -4.95e29, 4.95e29), ("rstV", 256, 32, 4.95e29, -4.95e29)):
+        fill(V(n, 0, w), c)
+        fill(V(n, 0, w, k), c0)
+    for a, b in ((0, 8), (264, 520), (776, 784)):
+        fill(V("Sw", a, b), -1e25)
+    for p in range(2):
+        ts(V("mkV", p, 256, 2), V("mk", 0, 128), 0.5, -9.9e29, OP.subtract, OP.mult)
+    ts(V("tmV", 0, 1), V("mkV", 0, 1), -1e25, None, OP.max)
+    ts(V("mP"), V("mk", 0, 128), 0.5, 9.9e29, OP.subtract, OP.mult)
+    for d, n, c in (("dL", 128, LIFT), ("dL2", 256, LIFT2)):
+        ts(V("mt", 0, n), V("mk", 0, n), c, None, OP.mult)
+        ts(V("mu", 0, n), V("mk", 0, n), -1e29, None, OP.mult)
+        copy(V(d, 0, 1), V("mu", 0, 1))
+        tt(V(d, 1, n), V("mu", 1, n), V("mt", 0, n - 1), OP.add)
     quant(V("uq0"), V("us0"), V("ut"))
     do("v", lambda e: e.tensor_copy(T.uq[:, 0:128].bitcast(dt.uint32), T.uq0[:, 0:128].bitcast(dt.uint32).indirect(ap(UO))), [V("uq0"), UO], [V("uq")], 250)
-    do("v", lambda e: e.tensor_copy(T.us[:, 0:128], T.us0[:, 0:128].indirect(ap(UO))), [V("us0"), UO], [V("us")], 250)
+    act(V("us"), V("us0", 0, 128), AF.Copy, l=UO)
     fill(V("idn"), 1.0)
-    fill(V("rbt"), 1024.0)
+    fill(V("one"), 1.0)
+    fill(V("c8"), 1024.0)
+    select(V("c8"), [[-16, 8]], OP.is_ge, 0, 1)
+    select(V("c8"), [[16, 8]], OP.is_ge, 15, -1)
+    for m in range(8):
+        act(V("rbt", 64 * m, 64 * m + 64), V("one"), AF.Copy, scale=V("c8", m, m + 1))
     select(V("idn"), [[-1, 128]], OP.is_equal, 0, 1)
-    select(V("rbt"), [[-16, 8], [0, 64]], OP.is_ge, 0, 1)
-    select(V("rbt"), [[16, 8], [0, 64]], OP.is_ge, 15, -1)
-    iota(V("ci"), [[0, 256]], 0, 1)
+    iota(V("c1"), [[0, 8]], 0, 1)
     iota(V("jc"), [[2, 128]], 131072, 0)
-    iota(V("ng"), [[-1, 128]], 128, 0)
-    fill(V("iw"), 0.0)
+    iota(V("ng", 16, 144), [[-1, 128]], 128, 0)
     iota(V("iw", 0, 256), [[1, 256]], 256, 0)
+    fill(V("iw", 256, 512), 0.0)
     iota(V("iw", 512, 768), [[1, 256]], 256, 0)
+    fill(V("iw", 768, 776), 0.0)
     iota(V("col"), [[1, 256]], 0, 0)
-    fill(V("et"), 0.0)
     for b in range(4):
-        copy(V("et", 512 * b + b, 512 * b + 512, 4), V("idn"))
+        fill(V("et", 512 * b, 512 * b + 512), 0.0)
+        act(V("et", 512 * b + b, 512 * b + 512, 4), V("idn"), AF.Copy)
     quant(V("eq"), V("es"), V("et"))
     quant(V("rbq"), V("rbs"), V("rbt"))
-    bits(V("cj", 0, 8), V("ci", 0, 8), 15)
-    copy(V("cf", 0, 8), V("cj", 0, 8))
+    bits(V("c2"), V("c1"), 15)
+    copy(V("cq"), V("c2"))
     for m in range(4):
-        ts(V("sm", m, m + 1), V("cf", 0, 1), 16.0 * m + 0.5, None, OP.add)
-    ts(V("sm", 48, 64), V("col", 0, 16), V("cf", 0, 1), -5e29, OP.is_ge, OP.mult)
-    for v, c in ((V("A"), 0.0), (V("nW"), 1.0), (B("RL", 0, 120, 121), INIT), (B("RR", 7, 15, 16), INIT), (B("NP", 0, 120, 121), 200.0),
+        ts(V("sm", m, m + 1), V("cq", 0, 1), 16.0 * m + 0.5, None, OP.add)
+    ts(V("sm", 11, 12), V("cq", 0, 1), 15.0, None, OP.is_lt)
+    ts(V("sm", 8, 9), V("sm", 11, 12), 2.0 * LIFT, 273.0, OP.mult, OP.add)
+    ts(V("sm", 9, 10), V("sm", 11, 12), -LIFT2, -1.0, OP.mult, OP.add)
+    for v, c in ((V("A"), 0.0), (V("nW"), 1.0), (V("UL", 15, 16), 1.0), (V("UR", 1024, 1025), 1.0), (V("nkR", 128, 129), 0.0), (V("ng", 15, 16), 0.0),
                  (V("rmx"), 1e25), (V("F"), 0.0), (V("FE"), 0.0), (V("pcw"), 0.0)):
         fill(v, c)
-    fill(V("rbt"), 0.0)
-    quant(V("zq"), V("zs"), V("rbt"))
+    fill(V("zt"), 0.0)
+    quant(V("zq"), V("zs"), V("zt"))
     for t in range(R):
         dma("s", T["lc%d" % t][:, 64:128].bitcast(dt.uint8), T.zq[:, 64:128].bitcast(dt.uint8), [V("zq")], [V("lc%d" % t, 64, 128)])
         dma("s", T["ls%d" % t][:, 64:128], T.zs[:, 64:128], [V("zs")], [V("ls%d" % t, 64, 128)])
@@ -329,104 +371,135 @@ def rank_program(g, core, T, topo):
         add("g", call, [V("Fq%d" % t), V("Fs%d" % t)], [], NET, NET, "snt", 2 * len(engs))
         add("in", None, [V("Fq%d" % t)], [V("lc%d" % t, 0, 64), V("ls%d" % t, 0, 64)], NET, 0.0, "arr%d" % t, 2 * len(engs))
 
-    S, XQ, XS, P = V("pss", 0, 256), V("XQ"), V("XS"), V("psr", 0, 128)
+    XQ, XS, P = V("XQ"), V("XS"), V("psr", 0, 128)
     pc = V("pcw", 16, 272)
 
-    def ranks(more=False):
-        if more:
-            quant(V("FEq"), V("FEs"), V("FE"))
-        quant(V("FVq"), V("FVs"), V("FV"))
+    def product(l, ls, X):
         for h in range(2):
-            mm(P, V("rbq"), V("rbs"), V("FVq", 128 * h, 128 * h + 128), V("FVs", 128 * h, 128 * h + 128), h == 0, h == 1 and not more)
-        if more:
-            mm(P, V("rbq"), V("rbs"), V("FEq"), V("FEs"), False, True)
+            q, s = V("XQ", 128 * h, 128 * h + 128), V("XS", 128 * h, 128 * h + 128)
+            quant(q, s, V(X, 512 * h, 512 * h + 512))
+            mm(V("ps%d" % h, 0, 128), V(l), V(ls), q, s)
+
+    def ranks(tiles):
+        for i, h in enumerate(tiles):
+            x, q, s = (V("FE"), V("FEq"), V("FEs")) if h == 2 else (V("FV", 512 * h, 512 * h + 512), V("FVq", 128 * h, 128 * h + 128),
+                                                                    V("FVs", 128 * h, 128 * h + 128))
+            quant(q, s, x)
+            mm(P, V("rbq"), V("rbs"), q, s, i == 0, i == len(tiles) - 1)
 
     def slot(m, a=0, b=128):
         o = 512 * (m // 4) + m % 4
         return V("FV", o + 4 * a, 512 * (m // 4) + 4 * b, 4)
 
+    def climb(n, d, o, init, w):
+        for m in range(7, -1, -1):
+            k = 16 * m + 15 + (m == 0)
+            scan(V("%s%d" % (n, m // 4), 80 + 16 * (m % 4) - k, 80 + 16 * (m % 4)), V("UL", 144 * m + 31 - k, 144 * m + 31),
+                 V(d, o + 16 * m + 15 - k, o + 16 * m + 15), init, OP.mult, OP.max)
+        for h in range(2):
+            dscan(V(w, 64 * h, 64 * h + 64), V("%s%d" % (n, h), 64, 128), V("dL", 0, 64))
+
     for t in range(R):
-        quant(XQ, XS, V("X%d" % (t % 2)))
-        mm(S, V("uq"), V("us"), XQ, XS)
-        copy(V("Sw", 9, 264, 2), V("pss", 1, 256, 2))
-        copy(V("Sw", 8, 264, 2), V("pss", 0, 256, 2))
-        tt(V("VV"), V("pss", 0, 256, 2), V("Sw", 7, 263, 2), OP.min)
-        diag(V("tsV"), V("VV"), V("tm"), 128)
-        for m in range(8):
-            act(slot(m), V("VV"), AF.Sign, bias=V("tsV", 16 * m + 15, 16 * m + 16), scale=-1.0)
-        tt(V("M"), V("pss", 0, 256, 2), V("Sw", 9, 264, 2), OP.max)
-        diag(V("tsM"), V("M"), V("tmM"), 128)
-        tt(V("A", 0, 256), S, V("Sw", 7, 263), OP.is_gt)
+        product("uq", "us", "X%d" % (t % 2))
         for b in range(4):
             mm(V("pst", 512 * b, 512 * b + 256), V("eq", 128 * b, 128 * b + 128), V("es", 128 * b, 128 * b + 128), XQ, XS)
-        tt(V("JL"), V("jc"), V("A", 0, 256, 2), OP.subtract)
+        for h in range(2):
+            S, o, e = "ps%d" % h, 128 * h, 128 - h
+            copy(V("Sw", o + 9, o + 136, 2), V(S, 1, 128, 2))
+            tt(V("tmV", o + 1, o + 1 + e), V(S, 0, e), V("mkV", o + 1, o + 1 + e), OP.max)
+            tt(V("VV", o // 2, o // 2 + 64), V(S, 0, 128, 2), V("Sw", o + 7, o + 135, 2), OP.min)
+            scan(V("tsV", o, o + 128), V("rstV", o, o + 128), V("tmV", o, o + 128), 0.0, OP.max, OP.min)
+            tt(V("M", o // 2, o // 2 + 64), V(S, 0, 128, 2), V("Sw", o + 9, o + 137, 2), OP.max)
+            copy(V("Sw", o + 8, o + 136, 2), V(S, 0, 128, 2))
+            tt(V("A", o, o + 128), V(S, 0, 128), V("Sw", o + 7, o + 135), OP.is_gt)
+        for h in range(2):
+            o, e = 128 * h, 128 - h
+            tt(V("nW", o + 1, o + 1 + e), V("ps%d" % h, 0, e), V("Sw", o + 10, o + 10 + e), OP.is_ge)
+        for m in range(8):
+            s = V("tsV", 32 * m + 31, 32 * m + 32)
+            if m < 2:
+                ts(slot(m), V("VV"), s, None, OP.is_lt)
+            else:
+                act(slot(m), V("VV"), AF.Sign, bias=s, scale=-1.0)
+        scan(V("tmM"), V("M"), V("mP"), -4e29, OP.max, OP.min)
+        scan(V("tsM"), V("rst"), V("tmM"), 0.0, OP.min, OP.max)
+        dma("s", T.Sw[:, 520:776], T.Sw[:, 8:264], [V("Sw", 8, 264)], [V("Sw", 520, 776)])
+        scan(V("NJ"), V("A", 0, 256, 2), V("jc"), 0.0, OP.max, OP.subtract)
         for m in range(8):
             s = V("tsM", 16 * m + 15, 16 * m + 16)
-            act(V("UL", 128 * m, 128 * m + 16 * m + 16), V("M", 0, 16 * m + 16), AF.Sign, bias=s, scale=-1.0)
-            ts(V("UR", 128 * m + 16 * m, 128 * m + 128), V("M", 16 * m, 128), s, None, OP.is_le)
-        ranks()
-        tt(V("nkL"), P, V("JL"), OP.add)
-        act(V("nkR"), V("nkL"), AF.Copy, bias=512.0)
+            act(V("UL", 16 + 128 * m, 16 + 128 * m + 16 * m + 16), V("M", 0, 16 * m + 16), AF.Sign, bias=s, scale=-1.0)
+            r = V("UR", 128 * m + 16 * m, 128 * m + 128)
+            if m < 4:
+                ts(r, V("M", 16 * m, 128), s, None, OP.is_le)
+            else:
+                act(r, V("M", 16 * m, 128), AF.Sign, bias=s, scale=-1.0)
+                act(r, r, AF.Sign, bias=0.5)
+        ranks((0, 1))
+        tt(V("nkL"), P, V("NJ"), OP.subtract)
+        act(V("nkR", 0, 128), V("nkL"), AF.Copy, bias=512.0)
         act(V("A2", 0, 257), V("A", 0, 257), AF.Copy, bias=2.0)
         scan(V("du"), V("A2", 0, 256), V("A2", 1, 257), 0.0, OP.max, OP.subtract)
         tt(V("hp"), V("du", 0, 256, 2), V("du", 1, 256, 2), OP.max)
         ts(V("hp"), V("hp"), 1.0, 1e29, OP.subtract, OP.mult)
         tt(V("PK"), V("M"), V("hp"), OP.add)
-        tt(V("nW", 1, 256), V("pss", 0, 255), V("Sw", 10, 265), OP.is_ge)
-        act(V("Sw", 520, 776), V("Sw", 8, 264), AF.Copy)
         act(V("pk"), V("du"), AF.Relu)
         act(V("npk"), V("pk"), AF.Copy, bias=1.0, scale=-1.0)
-        act(V("np2"), V("pk"), AF.Copy, bias=131072.0, scale=-65536.0)
+        act(V("np2"), V("pk"), AF.Copy, bias=132096.0, scale=-65536.0)
         for b in range(4):
             act(V("Th", 512 * b, 512 * b + 256), V("pst", 512 * b, 512 * b + 256), AF.Copy, scale=0.5)
-            act(V("Th", 512 * b + 256, 512 * b + 512), V("Th", 512 * b, 512 * b + 256), AF.Copy)
-        for m in range(7, -1, -1):
-            n = 16 * m + 15
-            scan(B("RL", m, BW - n, BW), V("UL", 128 * m, 128 * m + n), V("nkL", 1, n + 1), INIT, OP.mult, OP.max)
+            dma("s", T.Th[:, 512 * b + 256:512 * b + 512], T.Th[:, 512 * b:512 * b + 256], [V("Th", 512 * b, 512 * b + 256)],
+                [V("Th", 512 * b + 256, 512 * b + 512)])
+        climb("RL", "nkL", 1, INIT, "tRL")
         for m in range(8):
-            a = 16 * m
-            scan(B("RR", m, 126 - a, -1, -1), V("UR", 128 * m + 127, 128 * m + a, -1), V("nkR", 127, a, -1), INIT, OP.mult, OP.max)
-        tt(V("ci", 0, 128), V("RL", BW - 16, BW, 0), V("RR", 0, 16, 0), OP.min)
-        bits(V("cj", 0, 128), V("ci", 0, 128), 1023)
-        diag(V("tsK"), V("cj", 0, 128), V("tmK"), 128)
-        copy(LI, V("tsK", 15, 128, 16))
+            a, e = 16 * m, 127 + m // 7
+            scan(V("RR%d" % (m // 4), e - 1 - a + a % 64, a % 64 - 1, -1), V("UR", 128 * m + e, 128 * m + a, -1), V("nkR", e, a, -1), INIT, OP.mult,
+                 OP.max)
+        for h in range(2):
+            dscan(V("tRR", 64 * h, 64 * h + 64), V("RR%d" % h, 0, 64), V("dL", 0, 64))
+        tt(V("k8"), V("tRL", 15, 128, 16), V("tRR", 15, 128, 16), OP.min)
+        bits(V("l8"), V("k8"), 1023)
+        copy(LI, V("l8"))
         tt(V("np"), V("Sw", 8, 784), V("PK"), OP.subtract, l=LI)
-        diag(V("tsN"), V("np"), V("tmN"), 128)
+        scan(V("tmN"), V("np"), V("mP"), -4e29, OP.max, OP.min)
+        scan(V("tsN", 127, -1, -1), V("rst"), V("tmN", 127, -1, -1), 0.0, OP.min, OP.max)
         for m in range(8):
-            act(V("SR", 16 * m, 16 * m + 16), V("sm", 48, 64), AF.Identity, bias=V("tsN", 16 * m + 15, 16 * m + 16))
-        act(slot(0), V("np"), AF.Relu, bias=V("tsN", 15, 16), scale=-1.0)
-        act(slot(0), slot(0), AF.Sign)
-        for m in range(1, 8):
-            s = V("tsN", 16 * m + 15, 16 * m + 16)
-            ts(slot(m, 0, 16 * m), V("np", 0, 16 * m), s, None, OP.is_le)
-            ts(slot(m, 16 * m, 128), V("np", 16 * m, 128), s, None, OP.is_lt)
-        tt(V("FE", 0, 512, 4), V("np"), V("SR"), OP.is_equal)
-        ranks(True)
+            s = V("tsN", 16 * m, 16 * m + 1)
+            if m < 5:
+                act(slot(m, 16 * m, 128), V("np", 16 * m, 128), AF.Relu, bias=s, scale=-1.0)
+                act(slot(m, 16 * m, 128), slot(m, 16 * m, 128), AF.Sign)
+            else:
+                ts(slot(m, 16 * m, 128), V("np", 16 * m, 128), s, None, OP.is_lt)
+            if m:
+                ts(slot(m, 0, 16 * m), V("np", 0, 16 * m), s, None, OP.is_le)
+        tt(V("FE", 0, 512, 4), V("np"), V("tsN"), OP.is_equal)
+        ranks((2, 1, 0))
         act(V("Gp"), V("iw"), AF.Copy, l=LI)
         scan(V("ni"), V("npk"), V("npk"), 0.0, OP.add, OP.max)
         ts(V("sm", 10, 11), V("ni", 255, 256), -float(2 ** 20), 192.0 * 2 ** 20, OP.mult, OP.add)
         act(V("nf"), V("ni"), AF.Relu, bias=V("sm", 10, 11), scale=float(2 ** 20))
         scan(V("th"), V("nf"), V("np2"), 0.0, OP.max, OP.min)
-        act(V("th2"), V("th"), AF.Copy, scale=2.0 ** -16)
-        for m in range(7, -1, -1):
-            n = 16 * m + 15
-            scan(B("NP", m, BW - n, BW), V("UL", 128 * m, 128 * m + n), V("ng", 0, n), 200.0, OP.mult, OP.max)
+        act(V("th2"), V("th"), AF.Copy, scale=1.5 * 2.0 ** -16)
+        climb("NP", "ng", 16, 200.0, "tNP")
         for p in range(2):
             tt(V("K", p, 256, 2), P, V("th", p, 256, 2), OP.is_ge)
         scan(pc, V("K"), V("K"), 0.0, OP.add, OP.max)
-        ts(V("ec"), pc, V("sm", 0, 1), None, OP.is_le)
-        do("v", lambda e: e.tensor_reduce(T.sm[:, 16:17], T.ec[:, :], AX, OP.add), [V("ec")], [V("sm", 16, 17)], 256)
-        for m in range(1, 4):
-            act(V("ed"), pc, AF.Sign, bias=V("sm", m, m + 1), scale=-1.0, acc=V("sm", 16 + m, 17 + m))
-        copy(V("su", 8, 9), V("sm", 16, 17))
-        ts(V("su", 9, 12), V("sm", 17, 20), 0.5, 128.0, OP.mult, OP.add)
+        for m in range(4):
+            w, o = V("pcw", 16 + 16 * m, 16 + 16 * m + SPAN), SPAN * (m % 2)
+            if m < 2:
+                ts(V("ec", o, o + SPAN), w, V("sm", m, m + 1), None, OP.is_le)
+                scan(V("cn", o, o + SPAN), V("ec", o, o + SPAN), V("ec", o, o + SPAN), 16.0 * m, OP.add, OP.max)
+            else:
+                act(V("ed", o, o + SPAN), w, AF.Sign, bias=V("sm", m, m + 1), scale=-1.0, acc=V("sm", 16 + m, 17 + m))
+                ts(V("su", 8 + m, 9 + m), V("sm", 16 + m, 17 + m), 0.5, SPAN / 2.0 + 16.0 * m, OP.mult, OP.add)
+        copy(V("su", 8, 10), V("cn", SPAN - 1, 2 * SPAN, SPAN))
         for b in range(2):
             act(V("Tf", 256 * b, 256 * b + 256), V("pst", 512 * b, 512 * b + 256), AF.Copy)
         for b in range(4):
             act(V("TE", 64 * b, 64 * b + 64), V("Th", 512 * b, 512 * b + 256), AF.Copy, l=EL)
         for p in range(2):
             tt(V("ct", p, 256, 2), V("Gp"), V("pk", p, 256, 2), OP.mult)
-        tt(V("CG"), V("ct"), V("col"), OP.max)
+        for p in range(2):
+            tt(V("CG", 128 * p, 128 * p + 128), V("ct", 128 * p, 128 * p + 128), V("col", 128 * p, 128 * p + 128), OP.max)
         tt(V("g64"), V("CG"), V("mk", 0, 64), OP.mult, l=EL)
         scan(V("s64"), V("sg", 0, 64), V("g64"), 0.0, OP.mult, OP.add)
         copy(QL, V("s64", 15, 64, 16))
@@ -434,56 +507,60 @@ def rank_program(g, core, T, topo):
             tt(V("F", b, 256, 4), V("Th", 512 * b, 512 * b + 512), V("TE", 64 * b, 64 * b + 64), OP.add, l=QL)
         quant(V("Fq%d" % t), V("Fs%d" % t), V("F"))
         send(t)
-        ts(V("kept"), P, 65536.0, None, OP.is_ge)
-        act(V("NR"), V("kept"), AF.Copy, scale=-1e29)
+        ts(V("kept"), P, 66560.0, 1.0, OP.is_ge, OP.add)
+        act(V("NR"), V("kept"), AF.Copy, bias=1e29, scale=-1e29)
         scan(V("rmx", 1, 129), V("NR"), V("M"), 1e25, OP.add, OP.max)
-        diag(V("tsb", 0, 128), V("NP", BW - 16, BW, 0), V("tmb", 0, 128), 128)
-        ts(V("sm", 24, 32), V("tsb", 15, 128, 16), -2.0, 273.0, OP.mult, OP.add)
-        ts(V("sm", 32, 40), V("tsK", 15, 128, 16), 512.0, None, OP.is_lt)
+        ts(V("sm", 24, 32), V("tNP", 15, 128, 16), -2.0, V("sm", 8, 9), OP.mult, OP.add)
+        ts(V("sm", 32, 40), V("l8"), 512.0, None, OP.is_lt)
         tt(V("sm", 24, 32), V("sm", 24, 32), V("sm", 32, 40), OP.mult)
         copy(PL, V("sm", 24, 32))
         act(V("vLR"), V("pcw"), AF.Copy, l=PL)
         tt(V("rec"), V("PK"), V("rmx", 0, 128), OP.is_gt)
-        tt(V("z"), V("rec"), V("kept"), OP.max)
+        scan(V("z"), V("rec"), V("kept"), 5.0, OP.min, OP.add)
         for p in range(2):
             tt(V("Bar", p, 256, 2), V("z"), V("th2", p, 256, 2), OP.is_ge)
         act(V("BB1"), V("Bar"), AF.Copy, bias=-1e29, scale=1.1e29)
         act(V("BB2"), V("Bar"), AF.Copy, bias=-1e29, scale=2e29)
-        tt(V("rnk"), V("rec"), V("kept"), OP.is_gt)
+        tt(V("rnk"), V("rec"), V("kept"), OP.is_ge)
         tt(V("wl"), V("pcw", 17, 272, 2), V("vLR"), OP.subtract)
         tt(V("wl"), V("wl"), V("rnk"), OP.mult)
         for p in range(2):
             tt(V("uu", p, 256, 2), V("pcw", 16 + p, 272, 2), V("wl"), OP.subtract)
-        tt(V("bv"), V("Bar"), V("uu"), OP.mult)
+        for p in range(2):
+            tt(V("bv", 128 * p, 128 * p + 128), V("Bar", 128 * p, 128 * p + 128), V("uu", 128 * p, 128 * p + 128), OP.mult)
         scan(V("rm"), V("Sw", 8, 264), V("BB1"), -1e26, OP.min, OP.max)
         scan(V("lm", 255, -1, -1), V("Sw", 263, 7, -1), V("BB2", 255, -1, -1), -1e25, OP.min, OP.max)
-        tt(V("D"), V("rm"), V("lm"), OP.is_ge)
+        for p in range(2):
+            tt(V("D", 128 * p, 128 * p + 128), V("rm", 128 * p, 128 * p + 128), V("lm", 128 * p, 128 * p + 128), OP.is_ge)
         scan(V("D2", 255, -1, -1), V("nW", 255, -1, -1), V("D", 255, -1, -1), 1.0, OP.max, OP.min)
         scan(V("vl"), V("D2"), V("bv"), 0.0, OP.mult, OP.add)
-        ts(V("uu"), V("vl"), 0.0, None, OP.is_equal)
-        scan(V("hv", 255, -1, -1), V("uu", 255, -1, -1), V("vl", 255, -1, -1), 0.0, OP.mult, OP.add)
-        diag(V("tsb"), V("hv"), V("tmb"), 256)
-        ts(HL, V("tsb", 15, 256, 16), -1.0, None, OP.add)
+        ts(V("u2"), V("vl"), 0.0, None, OP.is_equal)
+        scan(V("hv", 255, -1, -1), V("u2", 255, -1, -1), V("vl", 255, -1, -1), 0.0, OP.mult, OP.add)
+        dscan(V("tsb"), V("hv"), V("dL2"))
+        ts(HL, V("tsb", 15, 256, 16), V("sm", 9, 10), None, OP.add)
         if t == R - 1:
             act(V("s64"), V("col"), AF.Copy, l=EL)
             act(V("out"), V("s64"), AF.Copy, l=HL)
             dma("s", T.ol[:, :], T.out[0:128:16, :], [V("out")], [])
         X = "X%d" % ((t + 1) % 2)
-        for b in (3, 2, 0, 1):
-            o, k = {3: ("psr", 0), 2: ("pss", 0)}.get(b, ("pst", 512 * b))
+        for b in (0, 3, 1, 2):
+            o, k = {3: ("psr", 0), 2: ("ps0", 0)}.get(b, ("pst", 512 * b))
             mm(V(o, k, k + 128), V("wq", 128 * b, 128 * b + 128), V("wp", 128 * b, 128 * b + 128), V("lc%d" % t), V("ls%d" % t))
             act(V("H", 64 * b, 64 * b + 64), V(o, k, k + 64), AF.Relu, scale=0.03125)
-        for b in (3, 2):
-            act(V("G3", 256 * (b - 2), 256 * (b - 1)), V("H", 64 * b, 64 * b + 64), AF.Copy, l=HL)
-        for b in range(2):
-            tt(V(X, b, 1024, 4), V("H", 64 * b, 64 * b + 64), V("Tf", 256 * b, 256 * b + 256), OP.add, l=HL)
-        for b in (3, 2):
-            tt(V(X, b, 1024, 4), V("pst", 512 * b, 512 * b + 256), V("G3", 256 * (b - 2), 256 * (b - 1)), OP.add)
-    quant(XQ, XS, V("X%d" % (R % 2)))
-    mm(S, V("vq"), V("vs"), XQ, XS)
-    dma("s", T.oc[:, :], T.XQ[:, :].bitcast(dt.uint8), [XQ], [])
+        for h in range(2):
+            hl = V("su", 24 + 8 * h, 32 + 8 * h)
+            for b in range(2):
+                o = 256 * b + 128 * h
+                tt(V(X, 512 * h + b, 512 * h + 512, 4), V("H", 64 * b, 64 * b + 64), V("Tf", o, o + 128), OP.add, l=hl)
+            for b in (3, 2):
+                o = 256 * (b - 2) + 128 * h
+                act(V("G3", o, o + 128), V("H", 64 * b, 64 * b + 64), AF.Copy, l=hl)
+                tt(V(X, 512 * h + b, 512 * h + 512, 4), V("pst", 512 * b + 128 * h, 512 * b + 128 * h + 128), V("G3", o, o + 128), OP.add)
+    product("vq", "vs", "X%d" % (R % 2))
+    dma("a", T.oc[:, :], T.XQ[:, :].bitcast(dt.uint8), [XQ], [])
     for k in range(4):
         dma("a" if k % 2 else "s", T.osc[4 * k:4 * k + 4, :], T.XS[32 * k:32 * k + 4, :], [XS], [])
-    copy(V("yb"), S)
+    copy(V("yb", 0, 128), V("ps0", 0, 128))
+    copy(V("yb", 128, 256), V("ps1", 0, 128))
     dma("s", T.y[:, :], T.yb[:, :], [V("yb")], [])
     issue()

@@ -8,20 +8,23 @@ STEP = [1, 2, 4]
 F32, B16, I32, U16, U8, MX = "float32", "bfloat16", "int32", "uint16", "uint8", "float8_e4m3fn_x4"
 INIT = float(2 ** 20 + 256)
 LIFT, LIFT2 = float(2 ** 21), 128.0
+BASE = 192.0
+ALL = 66560
 SPAN = C - K + 16
-CYCLE, FIXED, WAKE, NET = 0.83, 0.0, 190.0, 3500.0
-TRIES = 5000
+CYCLE, FIXED, WAKE, NET = 0.83, 0.0, 220.0, 2500.0
+CASES = ((1.0, 190.0, 3500.0), (1.0, 240.0, 2500.0), (1.25, 210.0, 2500.0))
+TRIES = 7000
 ORDERS = {}
 
 _SB = {
     F32: {"sm": 64, "c8": 8, "Sw": 784, "M": 128, "VV": 128, "PK": 128, "tmV": 256,
-          "tmM": 128, "tmN": 128, "tsV": 256, "tsM": 128, "tsN": 128, "tRL": 128, "tRR": 128, "tNP": 128, "NJ": 128, "nkL": 128, "nkR": 136,
-          "Gp": 128, "np": 128, "ct": 256, "CG": 256, "g64": 64, "s64": 64, "H": 256, "G3": 512, "rmx": 136, "rm": 256, "lm": 256, "out": 256,
+          "tmM": 128, "tmN": 128, "tsV": 256, "tsM": 128, "tsN": 128, "tRL": 128, "tRR": 128, "tNP": 128, "NJ": 128, "nkL": 136,
+          "Gp": 128, "np": 128, "CT": 256, "g128": 128, "s128": 128, "s64": 64, "H": 256, "G3": 640, "lm": 256, "out": 256,
           "yb": 256},
-    B16: {"X0": 1024, "X1": 1024, "ut": 512, "vt": 512, "et": 2048, "rbt": 512, "zt": 512, "one": 64, "idn": 128, "A": 272, "A2": 272,
-          "du": 256, "pk": 256, "npk": 256, "np2": 256, "ni": 256, "nf": 256, "th": 256, "th2": 256, "hp": 128, "FV": 1024, "FE": 512, "UL": 1040,
-          "UR": 1040, "K": 256, "pcw": 272, "ed": 416, "ec": 416, "cn": 416, "Tf": 512, "Th": 2048, "TE": 256, "F": 512,
-          "tsb": 256, "vLR": 128, "nW": 256, "vl": 256, "hv": 256},
+    B16: {"X0": 1024, "X1": 1024, "ut": 512, "vt": 512, "et": 520, "et1": 520, "rbt": 512, "zt": 512, "one": 64, "idn": 128, "A": 272, "A2": 272,
+          "du": 256, "pk": 256, "npk": 256, "np2": 256, "ni": 256, "nf": 256, "th": 256, "thB": 256, "hpx": 256, "hp": 128, "FV": 1024, "FE": 512,
+          "UL": 1040, "UR": 1040, "K": 256, "pcw": 272, "ed": 416, "ec": 416, "cn": 416, "Tf": 512, "Th": 2048, "TE": 256, "F": 512,
+          "tsb": 256, "vL": 128, "nW": 256, "vl": 256, "hv": 256, "WM": 384, "WD": 384, "WO": 384, "r": 272},
     U16: {"su": 64},
     MX: {"uq0": 128, "uq": 128, "vq": 128, "wq": 512, "eq": 512, "rbq": 128, "zq": 128, "FVq": 256, "FEq": 128, "XQ": 256},
     U8: {"us0": 128, "us": 128, "vs": 128, "wp": 512, "es": 512, "rbs": 128, "zs": 128, "FVs": 256, "FEs": 128, "XS": 256},
@@ -34,10 +37,10 @@ for _t in range(R):
         _SB[_d]["%s%d" % (_n, _t)] = 128
 _JOINT = {
     "kf": (F32, {"iw": 776, "cf": 256, "jc": 128, "col": 256, "cq": 8}),
-    "kb": (B16, {"mk": 256, "sg": 256, "ng": 144, "mP": 128, "rst": 128, "mkV": 256, "rstV": 256, "dL": 128, "dL2": 256, "mt": 256, "mu": 256}),
+    "kb": (B16, {"mk": 256, "sgb": 128, "par": 256, "mkS": 64, "dg": 776, "ng": 144, "mP": 128, "rst": 128, "mkV": 256, "rstV": 256, "dL": 128,
+                 "dL2": 256, "mt": 256, "mu": 256}),
     "ki": (I32, {"ci": 256, "cj": 256, "c0": 8, "c1": 8, "c2": 8}),
-    "rb": (B16, {"kept": 128, "NR": 128, "rec": 128, "rnk": 128, "z": 128, "wl": 128, "uu": 256, "u2": 256, "Bar": 256, "bv": 256, "BB1": 256,
-                 "BB2": 256, "D": 256, "D2": 256}),
+    "rb": (B16, {"uu": 256, "u2": 256, "bv": 256, "BB2": 256, "nE": 256, "Sg": 256, "pen": 256, "D": 256, "D2": 256}),
     "l8s": (I32, {"k8": 8, "l8": 8}),
 }
 WIDTH = {n: w for l in _SB.values() for n, w in l.items()}
@@ -74,7 +77,7 @@ def planner(g, T):
         (_, a, b, s), (_, c, d, r) = x, y
         if a >= d or c >= b:
             return False
-        return not (s == r and s > 1 and (a - c) % s)
+        return not (a - c) % math.gcd(s, r)
 
     def add(q, call, reads, writes, cost, hold=None, sem=None, inc=1, adds=False):
         i, pre = len(ops), {}
@@ -141,7 +144,32 @@ def planner(g, T):
                         cand[qs[k]].append(k)
                         pick[qs[k]] = None
 
-        rng, at, best = np.random.default_rng(0), np.arange(n), None
+        cases = []
+        for f, wake, net in CASES:
+            pre = [[(j, wake if w else 0.0) for j, w in o["pre"].items()] for o in ops]
+            sent = [o["cost"] == NET for o in ops]
+            c = [net if s else x if x > 2000.0 else f * x for s, x in zip(sent, cost)]
+            cases.append((pre, c, [net if s and h else h if x > 2000.0 else f * h for s, x, h in zip(sent, cost, hold)]))
+
+        def judge(out):
+            total = 0.0
+            for pre, c, h in cases:
+                fin, free, end = [0.0] * n, [0.0] * len(names), 0.0
+                for i in out:
+                    q = qs[i]
+                    t = free[q]
+                    for j, w in pre[i]:
+                        x = fin[j] + w
+                        if x > t:
+                            t = x
+                    free[q] = t + h[i]
+                    fin[i] = t = t + c[i]
+                    if t > end:
+                        end = t
+                total += end
+            return total
+
+        rng, at, best, least = np.random.default_rng(0), np.arange(n), None, 1e18
         for k in range(TRIES):
             if k < 200:
                 noise, patience = rng.random(n) * (0.0, 100.0, 300.0, 800.0)[k // 4 % 4], (0.0, 20.0, 50.0, 100.0)[k % 4]
@@ -150,6 +178,9 @@ def planner(g, T):
                 some = (np.abs(at - rng.integers(0, n)) < (5, 20, 60, 200)[k % 4]) & (rng.random(n) < (0.6, 0.3, 0.15, 0.1)[k % 4])
                 noise[some] += rng.normal(0.0, (100.0, 300.0, 800.0)[k % 3], int(some.sum()))
             end, out = order([r + x for r, x in zip(rank, noise.tolist())], patience)
+            if end > least + 500.0:
+                continue
+            least, end = min(least, end), judge(out)
             if best is None or end <= best[0]:
                 best = (end, out, noise, patience)
         return best[1]
@@ -229,7 +260,7 @@ def rank_program(g, core, T, topo):
     def dma(q, out, in_, reads, writes):
         s = "d%d" % nd[0]
         nd[0] += 1
-        add(q, lambda e: e.dma_start(out, in_).then_inc(T.sem[s], 16), reads, writes, 2500.0, 100.0, s, 16)
+        add(q, lambda e: e.dma_start(out, in_).then_inc(T.sem[s], 16), reads, writes, 2501.0, 100.0, s, 16)
 
     def tt(out, a, b, op, l=None):
         n = width(out)
@@ -277,6 +308,9 @@ def rank_program(g, core, T, topo):
         kw = {} if TYPE[v[0]] == I32 else {"allow_small_or_imprecise_dtypes": True}
         do("g", lambda e: e.iota(ap(v), pat, base, cm, **kw), [], [v], 160 + 2 * width(v))
 
+    def level(n, a, b, c):
+        iota(V(n, a, b), [[0, b - a]], c, 0)
+
     def select(v, pat, op, base, cm):
         do("g", lambda e: e.affine_select(ap(v), ap(v), pat, op, 0.0, base, cm), [v], [v], 200 + 2 * width(v))
 
@@ -286,7 +320,10 @@ def rank_program(g, core, T, topo):
     def dscan(out, src, lift):
         scan(out, lift, src, 0.0, OP.add, OP.max)
 
-    LI, EL, QL, PL, HL, UO = V("su", 0, 8), V("su", 8, 12), V("su", 12, 16), V("su", 16, 24), V("su", 24, 40), V("su", 40, 48)
+    def less(out, a, b):
+        scan(out, a, b, 0.0, OP.max, OP.subtract)
+
+    LI, EL, QL, NL, HL, UO = V("su", 0, 8), V("su", 8, 12), V("su", 12, 16), V("su", 16, 24), V("su", 24, 40), V("su", 40, 48)
 
     dma("s", ap(V("X0")), T.x[:, :], [], [V("X0")])
     dma("a", ap(V("ut")), T.u[:, :], [], [V("ut")])
@@ -300,7 +337,7 @@ def rank_program(g, core, T, topo):
     ts(V("mk"), V("cf"), 0.0, None, OP.is_equal)
     iota(V("c0"), [[16, 8]], 0, 0)
     copy(UO, V("c0"))
-    for n, w, k, c0, c in (("sg", 256, 16, 0.0, 1.0), ("rst", 128, 16, -4.95e29, 4.95e29), ("rstV", 256, 32, 4.95e29, -4.95e29)):
+    for n, w, k, c0, c in (("sgb", 128, 32, 0.0, 1.0), ("par", 256, 2, 0.0, 1.0), ("rst", 128, 16, -4.95e29, 4.95e29), ("rstV", 256, 32, 4.95e29, -4.95e29)):
         fill(V(n, 0, w), c)
         fill(V(n, 0, w, k), c0)
     for a, b in ((0, 8), (264, 520), (776, 784)):
@@ -314,6 +351,12 @@ def rank_program(g, core, T, topo):
         ts(V("mu", 0, n), V("mk", 0, n), -1e29, None, OP.mult)
         copy(V(d, 0, 1), V("mu", 0, 1))
         tt(V(d, 1, n), V("mu", 1, n), V("mt", 0, n - 1), OP.add)
+    ts(V("mkS"), V("mk", 0, 64), -2.0 ** 20, 2.0 ** 20, OP.mult, OP.add)
+    fill(V("dg"), -65.0)
+    fill(V("dg", 512, 768), -1.0)
+    for k, c in enumerate((0.0, 1.0)):
+        fill(V("WM", k, 384, 3), c)
+    fill(V("WD", 2, 384, 3), 64.0)
     quant(V("uq0"), V("us0"), V("ut"))
     do("v", lambda e: e.tensor_copy(T.uq[:, 0:128].bitcast(dt.uint32), T.uq0[:, 0:128].bitcast(dt.uint32).indirect(ap(UO))), [V("uq0"), UO], [V("uq")], 250)
     act(V("us"), V("us0", 0, 128), AF.Copy, l=UO)
@@ -328,27 +371,32 @@ def rank_program(g, core, T, topo):
     iota(V("c1"), [[0, 8]], 0, 1)
     iota(V("jc"), [[2, 128]], 131072, 0)
     iota(V("ng", 16, 144), [[-1, 128]], 128, 0)
-    iota(V("iw", 0, 256), [[1, 256]], 256, 0)
-    fill(V("iw", 256, 512), 0.0)
-    iota(V("iw", 512, 768), [[1, 256]], 256, 0)
-    fill(V("iw", 768, 776), 0.0)
+    iota(V("iw", 0, 256), [[1, 256]], ALL + 256, 0)
+    level("iw", 256, 512, ALL)
+    iota(V("iw", 512, 768), [[1, 256]], ALL + 256, 0)
+    level("iw", 768, 776, ALL)
     iota(V("col"), [[1, 256]], 0, 0)
+    for n, o in (("et", 4), ("et1", 5)):
+        fill(V(n), 0.0)
+        act(V(n, o, o + 509, 4), V("idn"), AF.Copy)
     for b in range(4):
-        fill(V("et", 512 * b, 512 * b + 512), 0.0)
-        act(V("et", 512 * b + b, 512 * b + 512, 4), V("idn"), AF.Copy)
-    quant(V("eq"), V("es"), V("et"))
+        o = (4, 4, 2, 2)[b]
+        quant(V("eq", 128 * b, 128 * b + 128), V("es", 128 * b, 128 * b + 128), V(("et", "et1")[b % 2], o, o + 512))
     quant(V("rbq"), V("rbs"), V("rbt"))
     bits(V("c2"), V("c1"), 15)
     copy(V("cq"), V("c2"))
     for m in range(4):
-        ts(V("sm", m, m + 1), V("cq", 0, 1), 16.0 * m + 0.5, None, OP.add)
+        ts(V("sm", m, m + 1), V("cq", 0, 1), 16.0 * m + BASE + 0.5, None, OP.add)
     ts(V("sm", 11, 12), V("cq", 0, 1), 15.0, None, OP.is_lt)
     ts(V("sm", 8, 9), V("sm", 11, 12), 2.0 * LIFT, 273.0, OP.mult, OP.add)
     ts(V("sm", 9, 10), V("sm", 11, 12), -LIFT2, -1.0, OP.mult, OP.add)
-    for v, c in ((V("A"), 0.0), (V("nW"), 1.0), (V("UL", 15, 16), 1.0), (V("UR", 1024, 1025), 1.0), (V("nkR", 128, 129), 0.0), (V("ng", 15, 16), 0.0),
-                 (V("rmx"), 1e25), (V("F"), 0.0), (V("FE"), 0.0), (V("pcw"), 0.0)):
+    for v, c in ((V("A"), 0.0), (V("nW"), 1.0), (V("UL", 15, 16), 1.0), (V("UR", 1024, 1025), 1.0), (V("nkL", 128, 129), 0.0), (V("ng", 15, 16), 0.0),
+                 (V("pcw", 0, 16), BASE), (V("nE"), 1.0), (V("r", 0, 16), 0.0)):
         fill(v, c)
-    fill(V("zt"), 0.0)
+    level("FE", 0, 512, 0)
+    level("g128", 0, 128, 0)
+    level("F", 256, 512, 0)
+    level("zt", 0, 512, 0)
     quant(V("zq"), V("zs"), V("zt"))
     for t in range(R):
         dma("s", T["lc%d" % t][:, 64:128].bitcast(dt.uint8), T.zq[:, 64:128].bitcast(dt.uint8), [V("zq")], [V("lc%d" % t, 64, 128)])
@@ -374,11 +422,13 @@ def rank_program(g, core, T, topo):
     XQ, XS, P = V("XQ"), V("XS"), V("psr", 0, 128)
     pc = V("pcw", 16, 272)
 
-    def product(l, ls, X):
+    def product(l, ls, X, banks):
         for h in range(2):
             q, s = V("XQ", 128 * h, 128 * h + 128), V("XS", 128 * h, 128 * h + 128)
             quant(q, s, V(X, 512 * h, 512 * h + 512))
-            mm(V("ps%d" % h, 0, 128), V(l), V(ls), q, s)
+            for n in banks:
+                n, o = ("ps%d" % h, 0) if n == "ps" else (n, 512 * h)
+                mm(V(n, o, o + 128), V(l), V(ls), q, s)
 
     def ranks(tiles):
         for i, h in enumerate(tiles):
@@ -400,17 +450,17 @@ def rank_program(g, core, T, topo):
             dscan(V(w, 64 * h, 64 * h + 64), V("%s%d" % (n, h), 64, 128), V("dL", 0, 64))
 
     for t in range(R):
-        product("uq", "us", "X%d" % (t % 2))
+        product("uq", "us", "X%d" % (t % 2), ("ps", "pst"))
+        for h in range(2):
+            act(V("Sw", 128 * h + 8, 128 * h + 136), V("pst", 512 * h, 512 * h + 128), AF.Copy)
         for b in range(4):
             mm(V("pst", 512 * b, 512 * b + 256), V("eq", 128 * b, 128 * b + 128), V("es", 128 * b, 128 * b + 128), XQ, XS)
         for h in range(2):
             S, o, e = "ps%d" % h, 128 * h, 128 - h
-            copy(V("Sw", o + 9, o + 136, 2), V(S, 1, 128, 2))
             tt(V("tmV", o + 1, o + 1 + e), V(S, 0, e), V("mkV", o + 1, o + 1 + e), OP.max)
             tt(V("VV", o // 2, o // 2 + 64), V(S, 0, 128, 2), V("Sw", o + 7, o + 135, 2), OP.min)
             scan(V("tsV", o, o + 128), V("rstV", o, o + 128), V("tmV", o, o + 128), 0.0, OP.max, OP.min)
             tt(V("M", o // 2, o // 2 + 64), V(S, 0, 128, 2), V("Sw", o + 9, o + 137, 2), OP.max)
-            copy(V("Sw", o + 8, o + 136, 2), V(S, 0, 128, 2))
             tt(V("A", o, o + 128), V(S, 0, 128), V("Sw", o + 7, o + 135), OP.is_gt)
         for h in range(2):
             o, e = 128 * h, 128 - h
@@ -435,13 +485,12 @@ def rank_program(g, core, T, topo):
                 act(r, V("M", 16 * m, 128), AF.Sign, bias=s, scale=-1.0)
                 act(r, r, AF.Sign, bias=0.5)
         ranks((0, 1))
-        tt(V("nkL"), P, V("NJ"), OP.subtract)
-        act(V("nkR", 0, 128), V("nkL"), AF.Copy, bias=512.0)
+        tt(V("nkL", 0, 128), P, V("NJ"), OP.subtract)
         act(V("A2", 0, 257), V("A", 0, 257), AF.Copy, bias=2.0)
-        scan(V("du"), V("A2", 0, 256), V("A2", 1, 257), 0.0, OP.max, OP.subtract)
-        tt(V("hp"), V("du", 0, 256, 2), V("du", 1, 256, 2), OP.max)
-        ts(V("hp"), V("hp"), 1.0, 1e29, OP.subtract, OP.mult)
-        tt(V("PK"), V("M"), V("hp"), OP.add)
+        less(V("du"), V("A2", 0, 256), V("A2", 1, 257))
+        scan(V("hpx"), V("par"), V("du"), 0.0, OP.mult, OP.max)
+        ts(V("hp"), V("hpx", 1, 256, 2), 2e29, -1e27, OP.mult, OP.add)
+        scan(V("PK"), V("hp"), V("M"), 0.0, OP.add, OP.min)
         act(V("pk"), V("du"), AF.Relu)
         act(V("npk"), V("pk"), AF.Copy, bias=1.0, scale=-1.0)
         act(V("np2"), V("pk"), AF.Copy, bias=132096.0, scale=-65536.0)
@@ -452,11 +501,12 @@ def rank_program(g, core, T, topo):
         climb("RL", "nkL", 1, INIT, "tRL")
         for m in range(8):
             a, e = 16 * m, 127 + m // 7
-            scan(V("RR%d" % (m // 4), e - 1 - a + a % 64, a % 64 - 1, -1), V("UR", 128 * m + e, 128 * m + a, -1), V("nkR", e, a, -1), INIT, OP.mult,
+            scan(V("RR%d" % (m // 4), e - 1 - a + a % 64, a % 64 - 1, -1), V("UR", 128 * m + e, 128 * m + a, -1), V("nkL", e, a, -1), INIT, OP.mult,
                  OP.max)
         for h in range(2):
             dscan(V("tRR", 64 * h, 64 * h + 64), V("RR%d" % h, 0, 64), V("dL", 0, 64))
-        tt(V("k8"), V("tRL", 15, 128, 16), V("tRR", 15, 128, 16), OP.min)
+        ts(V("sm", 40, 48), V("tRR", 15, 128, 16), 512.0, None, OP.add)
+        tt(V("k8"), V("tRL", 15, 128, 16), V("sm", 40, 48), OP.min)
         bits(V("l8"), V("k8"), 1023)
         copy(LI, V("l8"))
         tt(V("np"), V("Sw", 8, 784), V("PK"), OP.subtract, l=LI)
@@ -474,15 +524,17 @@ def rank_program(g, core, T, topo):
         tt(V("FE", 0, 512, 4), V("np"), V("tsN"), OP.is_equal)
         ranks((2, 1, 0))
         act(V("Gp"), V("iw"), AF.Copy, l=LI)
+        act(V("WD", 1, 384, 3), V("dg"), AF.Copy, l=LI)
         scan(V("ni"), V("npk"), V("npk"), 0.0, OP.add, OP.max)
         ts(V("sm", 10, 11), V("ni", 255, 256), -float(2 ** 20), 192.0 * 2 ** 20, OP.mult, OP.add)
+        ts(V("sm", 12, 13), V("sm", 10, 11), float(ALL), float(ALL), OP.add, OP.min)
         act(V("nf"), V("ni"), AF.Relu, bias=V("sm", 10, 11), scale=float(2 ** 20))
         scan(V("th"), V("nf"), V("np2"), 0.0, OP.max, OP.min)
-        act(V("th2"), V("th"), AF.Copy, scale=1.5 * 2.0 ** -16)
+        ts(V("thB"), V("th"), float(ALL), 2.0 ** -10, OP.max, OP.mult)
         climb("NP", "ng", 16, 200.0, "tNP")
         for p in range(2):
             tt(V("K", p, 256, 2), P, V("th", p, 256, 2), OP.is_ge)
-        scan(pc, V("K"), V("K"), 0.0, OP.add, OP.max)
+        scan(pc, V("K"), V("K"), BASE, OP.add, OP.max)
         for m in range(4):
             w, o = V("pcw", 16 + 16 * m, 16 + 16 * m + SPAN), SPAN * (m % 2)
             if m < 2:
@@ -497,43 +549,35 @@ def rank_program(g, core, T, topo):
         for b in range(4):
             act(V("TE", 64 * b, 64 * b + 64), V("Th", 512 * b, 512 * b + 256), AF.Copy, l=EL)
         for p in range(2):
-            tt(V("ct", p, 256, 2), V("Gp"), V("pk", p, 256, 2), OP.mult)
-        for p in range(2):
-            tt(V("CG", 128 * p, 128 * p + 128), V("ct", 128 * p, 128 * p + 128), V("col", 128 * p, 128 * p + 128), OP.max)
-        tt(V("g64"), V("CG"), V("mk", 0, 64), OP.mult, l=EL)
-        scan(V("s64"), V("sg", 0, 64), V("g64"), 0.0, OP.mult, OP.add)
-        copy(QL, V("s64", 15, 64, 16))
+            less(V("CT", p, 256, 2), V("np2", p, 256, 2), V("Gp"))
+        ts(V("g128", 31, 128, 32), EL, -1.0, None, OP.mult)
+        tt(V("g128", 0, 128, 2), V("CT"), V("mkS"), OP.add, l=EL)
+        scan(V("s128"), V("sgb"), V("g128"), 0.0, OP.mult, OP.min)
+        ts(QL, V("s128", 31, 128, 32), -1.0, None, OP.mult)
         for b in range(4):
             tt(V("F", b, 256, 4), V("Th", 512 * b, 512 * b + 512), V("TE", 64 * b, 64 * b + 64), OP.add, l=QL)
         quant(V("Fq%d" % t), V("Fs%d" % t), V("F"))
         send(t)
-        ts(V("kept"), P, 66560.0, 1.0, OP.is_ge, OP.add)
-        act(V("NR"), V("kept"), AF.Copy, bias=1e29, scale=-1e29)
-        scan(V("rmx", 1, 129), V("NR"), V("M"), 1e25, OP.add, OP.max)
-        ts(V("sm", 24, 32), V("tNP", 15, 128, 16), -2.0, V("sm", 8, 9), OP.mult, OP.add)
-        ts(V("sm", 32, 40), V("l8"), 512.0, None, OP.is_lt)
-        tt(V("sm", 24, 32), V("sm", 24, 32), V("sm", 32, 40), OP.mult)
-        copy(PL, V("sm", 24, 32))
-        act(V("vLR"), V("pcw"), AF.Copy, l=PL)
-        tt(V("rec"), V("PK"), V("rmx", 0, 128), OP.is_gt)
-        scan(V("z"), V("rec"), V("kept"), 5.0, OP.min, OP.add)
+        ts(NL, V("tNP", 15, 128, 16), -2.0, V("sm", 8, 9), OP.mult, OP.add)
+        act(V("vL"), V("pcw"), AF.Copy, bias=-65.0, l=NL)
+        less(V("WD", 0, 384, 3), V("pcw", 17, 272, 2), V("vL"))
         for p in range(2):
-            tt(V("Bar", p, 256, 2), V("z"), V("th2", p, 256, 2), OP.is_ge)
-        act(V("BB1"), V("Bar"), AF.Copy, bias=-1e29, scale=1.1e29)
-        act(V("BB2"), V("Bar"), AF.Copy, bias=-1e29, scale=2e29)
-        tt(V("rnk"), V("rec"), V("kept"), OP.is_ge)
-        tt(V("wl"), V("pcw", 17, 272, 2), V("vLR"), OP.subtract)
-        tt(V("wl"), V("wl"), V("rnk"), OP.mult)
+            less(V("r", 16 + p, 272, 2), V("WD", 0, 384, 3), V("thB", p, 256, 2))
+        act(V("BB2"), V("r", 16, 272), AF.Copy, bias=-1e27, scale=2e27)
+        act(V("Sg"), V("r", 16, 272), AF.Sign, bias=0.5, scale=-1.0)
+        act(V("pen"), V("Sg"), AF.Copy, bias=192.0, scale=64.0)
+        ts(V("WM", 2, 384, 3), P, V("sm", 12, 13), None, OP.is_lt)
+        scan(V("WO"), V("WM"), V("WD"), 0.0, OP.mult, OP.add)
         for p in range(2):
-            tt(V("uu", p, 256, 2), V("pcw", 16 + p, 272, 2), V("wl"), OP.subtract)
-        for p in range(2):
-            tt(V("bv", 128 * p, 128 * p + 128), V("Bar", 128 * p, 128 * p + 128), V("uu", 128 * p, 128 * p + 128), OP.mult)
-        scan(V("rm"), V("Sw", 8, 264), V("BB1"), -1e26, OP.min, OP.max)
+            less(V("uu", p, 256, 2), V("pcw", 16 + p, 272, 2), V("WO", 2, 384, 3))
+        less(V("bv"), V("uu"), V("pen"))
         scan(V("lm", 255, -1, -1), V("Sw", 263, 7, -1), V("BB2", 255, -1, -1), -1e25, OP.min, OP.max)
-        for p in range(2):
-            tt(V("D", 128 * p, 128 * p + 128), V("rm", 128 * p, 128 * p + 128), V("lm", 128 * p, 128 * p + 128), OP.is_ge)
+        for h in range(2):
+            o, e = 128 * h + 1, 128 - h
+            tt(V("nE", o, o + e), V("ps%d" % h, 0, e), V("lm", o, o + e), OP.is_ge)
+        scan(V("D"), V("nE"), V("r", 15, 271), 0.0, OP.min, OP.max)
         scan(V("D2", 255, -1, -1), V("nW", 255, -1, -1), V("D", 255, -1, -1), 1.0, OP.max, OP.min)
-        scan(V("vl"), V("D2"), V("bv"), 0.0, OP.mult, OP.add)
+        scan(V("vl"), V("D2"), V("bv"), 0.0, OP.mult, OP.max)
         ts(V("u2"), V("vl"), 0.0, None, OP.is_equal)
         scan(V("hv", 255, -1, -1), V("u2", 255, -1, -1), V("vl", 255, -1, -1), 0.0, OP.mult, OP.add)
         dscan(V("tsb"), V("hv"), V("dL2"))
@@ -544,19 +588,24 @@ def rank_program(g, core, T, topo):
             dma("s", T.ol[:, :], T.out[0:128:16, :], [V("out")], [])
         X = "X%d" % ((t + 1) % 2)
         for b in (0, 3, 1, 2):
-            o, k = {3: ("psr", 0), 2: ("ps0", 0)}.get(b, ("pst", 512 * b))
-            mm(V(o, k, k + 128), V("wq", 128 * b, 128 * b + 128), V("wp", 128 * b, 128 * b + 128), V("lc%d" % t), V("ls%d" % t))
-            act(V("H", 64 * b, 64 * b + 64), V(o, k, k + 64), AF.Relu, scale=0.03125)
+            o = ("pst", "ps1", "ps0", "psr")[b]
+            mm(V(o, 0, 128), V("wq", 128 * b, 128 * b + 128), V("wp", 128 * b, 128 * b + 128), V("lc%d" % t), V("ls%d" % t))
+            if b == 0:
+                ts(V("H", 0, 64), V(o, 0, 64), 0.0, 0.03125, OP.max, OP.mult)
+            else:
+                act(V("H", 64 * b, 64 * b + 64), V(o, 0, 64), AF.Relu, scale=0.03125)
         for h in range(2):
             hl = V("su", 24 + 8 * h, 32 + 8 * h)
-            for b in range(2):
+            for b in (0, 1, 3, 2) if h == 0 else (0, 3, 2, 1):
                 o = 256 * b + 128 * h
-                tt(V(X, 512 * h + b, 512 * h + 512, 4), V("H", 64 * b, 64 * b + 64), V("Tf", o, o + 128), OP.add, l=hl)
-            for b in (3, 2):
-                o = 256 * (b - 2) + 128 * h
-                act(V("G3", o, o + 128), V("H", 64 * b, 64 * b + 64), AF.Copy, l=hl)
-                tt(V(X, 512 * h + b, 512 * h + 512, 4), V("pst", 512 * b + 128 * h, 512 * b + 128 * h + 128), V("G3", o, o + 128), OP.add)
-    product("vq", "vs", "X%d" % (R % 2))
+                x = V(X, 512 * h + b, 512 * h + 512, 4)
+                if b < 2 - h:
+                    tt(x, V("H", 64 * b, 64 * b + 64), V("Tf", o, o + 128), OP.add, l=hl)
+                else:
+                    k = 512 if b == 1 else o - 512
+                    act(V("G3", k, k + 128), V("H", 64 * b, 64 * b + 64), AF.Copy, l=hl)
+                    tt(x, V("pst", 512 * b + 128 * h, 512 * b + 128 * h + 128), V("G3", k, k + 128), OP.add)
+    product("vq", "vs", "X%d" % (R % 2), ("ps",))
     dma("a", T.oc[:, :], T.XQ[:, :].bitcast(dt.uint8), [XQ], [])
     for k in range(4):
         dma("a" if k % 2 else "s", T.osc[4 * k:4 * k + 4, :], T.XS[32 * k:32 * k + 4, :], [XS], [])

import numpy as np
import math
from concourse.mybir import dt, AluOpType, AxisListType, ActivationFunctionType
import comms_topo

C, K, R = 256, 64, 3
STEP = [1, 2, 4]
F32, B16, I32, U16, U8, MX = "float32", "bfloat16", "int32", "uint16", "uint8", "float8_e4m3fn_x4"
INIT = float(2 ** 20 + 256)
LIFT, LIFT2 = float(2 ** 21), 128.0
BASE = 192.0
ALL = 66560
SPAN = C - K + 16
CYCLE, FIXED, WAKE, NET = 0.83, 0.0, 220.0, 2500.0
CASES = ((1.0, 190.0, 3500.0), (1.0, 240.0, 2500.0), (1.25, 210.0, 2500.0))
TRIES = 7000
ORDERS = {}

_SB = {
    F32: {"sm": 64, "c8": 8, "Sw": 784, "M": 128, "VV": 128, "PK": 128, "tmV": 256,
          "tmM": 128, "tmN": 128, "tsV": 256, "tsM": 128, "tsN": 128, "tRL": 128, "tRR": 128, "tNP": 128, "NJ": 128, "nkL": 136,
          "Gp": 128, "np": 128, "CT": 256, "g128": 128, "s128": 128, "s64": 64, "H": 256, "G3": 640, "lm": 256, "out": 256,
          "yb": 256},
    B16: {"X0": 1024, "X1": 1024, "ut": 512, "vt": 512, "et": 520, "et1": 520, "rbt": 512, "zt": 512, "one": 64, "idn": 128, "A": 272, "A2": 272,
          "du": 256, "pk": 256, "npk": 256, "np2": 256, "ni": 256, "nf": 256, "th": 256, "thB": 256, "hpx": 256, "hp": 128, "FV": 1024, "FE": 512,
          "UL": 1040, "UR": 1040, "K": 256, "pcw": 272, "ed": 416, "ec": 416, "cn": 416, "Tf": 512, "Th": 2048, "TE": 256, "F": 512,
          "tsb": 256, "vL": 128, "nW": 256, "vl": 256, "hv": 256, "WM": 384, "WD": 384, "WO": 384, "r": 272},
    U16: {"su": 64},
    MX: {"uq0": 128, "uq": 128, "vq": 128, "wq": 512, "eq": 512, "rbq": 128, "zq": 128, "FVq": 256, "FEq": 128, "XQ": 256},
    U8: {"us0": 128, "us": 128, "vs": 128, "wp": 512, "es": 512, "rbs": 128, "zs": 128, "FVs": 256, "FEs": 128, "XS": 256},
}
for _n, _d in (("RL", F32), ("RR", F32), ("NP", B16)):
    for _h in "01":
        _SB[_d][_n + _h] = 128
for _t in range(R):
    for _n, _d in (("Fq", MX), ("Fs", U8), ("lc", MX), ("ls", U8)):
        _SB[_d]["%s%d" % (_n, _t)] = 128
_JOINT = {
    "kf": (F32, {"iw": 776, "cf": 256, "jc": 128, "col": 256, "cq": 8}),
    "kb": (B16, {"mk": 256, "sgb": 128, "par": 256, "mkS": 64, "dg": 776, "ng": 144, "mP": 128, "rst": 128, "mkV": 256, "rstV": 256, "dL": 128,
                 "dL2": 256, "mt": 256, "mu": 256}),
    "ki": (I32, {"ci": 256, "cj": 256, "c0": 8, "c1": 8, "c2": 8}),
    "rb": (B16, {"uu": 256, "u2": 256, "bv": 256, "BB2": 256, "nE": 256, "Sg": 256, "pen": 256, "D": 256, "D2": 256}),
    "l8s": (I32, {"k8": 8, "l8": 8}),
}
WIDTH = {n: w for l in _SB.values() for n, w in l.items()}
TYPE = {n: d for d, l in _SB.items() for n in l}
PLACE = {}
SCRATCH = {n: ("sbuf", [128, WIDTH[n]], TYPE[n]) for n in WIDTH}
for _b, (_d, _l) in _JOINT.items():
    _o = 0
    for _n, _w in _l.items():
        PLACE[_n], WIDTH[_n], TYPE[_n] = (_b, _o), _w, _d
        _o += (_w + 31) // 32 * 32
    SCRATCH[_b] = ("sbuf", [128, _o], _d)
_PS = ("ps0", "ps1", "psr", "pst")
for _n in _PS:
    SCRATCH[_n] = ("psum", [128, 2048 if _n == "pst" else 512], F32)
    TYPE[_n] = F32
SEMAPHORES = ["qv", "qa", "qt", "qg"] + ["d%d" % i for i in range(48)] + ["arr%d" % t for t in range(R)] + ["snt"]


def planner(g, T):
    eng = {"v": g.vector, "a": g.scalar, "t": g.tensor, "g": g, "s": g.sync}
    ops, log = [], {}

    def span(v):
        n, a, b, s = v
        if n in _PS:
            return n, a // 512 * 512, (b + 511) // 512 * 512, 1
        if s < 0:
            k = (a - b + (-s) - 1) // (-s)
            return n, a + s * (k - 1), a + 1, -s
        return n, a, b, s

    def meet(x, y):
        (_, a, b, s), (_, c, d, r) = x, y
        if a >= d or c >= b:
            return False
        return not (a - c) % math.gcd(s, r)

    def add(q, call, reads, writes, cost, hold=None, sem=None, inc=1, adds=False):
        i, pre = len(ops), {}
        for kind, vs in (("r", reads), ("w", writes)):
            for v in vs:
                x = span(v)
                for (y, k2, j) in log.get(x[0], []):
                    if meet(x, y) and (kind == "w" or k2 == "w" or (x[0] in _PS and ops[j]["q"] != q)):
                        pre[j] = pre.get(j, False) or not (adds and x[0] in _PS and ops[j]["q"] == q)
        for kind, vs in (("r", reads), ("w", writes)):
            for v in vs:
                x = span(v)
                l = log.setdefault(x[0], [])
                if kind == "w" and x[3] == 1:
                    l[:] = [e for e in l if not (x[1] <= e[0][1] and e[0][2] <= x[2])]
                l.append((x, kind, i))
        ops.append({"q": q, "call": call, "pre": pre, "cost": cost, "hold": cost if hold is None else hold, "sem": sem or "q" + q, "inc": inc})

    def best_order():
        n = len(ops)
        succ, rank = [[] for _ in range(n)], [0.0] * n
        for i, o in enumerate(ops):
            for j, w in o["pre"].items():
                succ[j].append((i, WAKE if w else 0.0))
        for i in range(n - 1, -1, -1):
            rank[i] = ops[i]["cost"] + max([rank[k] + w for k, w in succ[i]], default=0.0)
        names = sorted({o["q"] for o in ops})
        qs = [names.index(o["q"]) for o in ops]
        cost, hold, need = [o["cost"] for o in ops], [o["hold"] for o in ops], [len(o["pre"]) for o in ops]

        def order(rk, patience):
            left, ready, free, cand = need[:], [0.0] * n, [0.0] * len(names), [[] for _ in names]
            pick, out, end = [None] * len(names), [], 0.0
            for i in range(n):
                if not left[i]:
                    cand[qs[i]].append(i)
            while True:
                best = None
                for q, l in enumerate(cand):
                    if not l:
                        continue
                    if pick[q] is None:
                        t = max(free[q], min([ready[i] for i in l])) + patience
                        top, r = -1, -1e18
                        for i in l:
                            if ready[i] <= t and rk[i] > r:
                                top, r = i, rk[i]
                        pick[q] = (max(free[q], ready[top]), -r, top)
                    if best is None or pick[q] < best[0]:
                        best = (pick[q], q)
                if best is None:
                    return end, out
                (t, _, i), q = best
                cand[q].remove(i)
                pick[q] = None
                out.append(i)
                free[q] = t + hold[i]
                done = t + cost[i]
                end = max(end, done)
                for k, w in succ[i]:
                    ready[k] = max(ready[k], done + w)
                    left[k] -= 1
                    if not left[k]:
                        cand[qs[k]].append(k)
                        pick[qs[k]] = None

        cases = []
        for f, wake, net in CASES:
            pre = [[(j, wake if w else 0.0) for j, w in o["pre"].items()] for o in ops]
            sent = [o["cost"] == NET for o in ops]
            c = [net if s else x if x > 2000.0 else f * x for s, x in zip(sent, cost)]
            cases.append((pre, c, [net if s and h else h if x > 2000.0 else f * h for s, x, h in zip(sent, cost, hold)]))

        def judge(out):
            total = 0.0
            for pre, c, h in cases:
                fin, free, end = [0.0] * n, [0.0] * len(names), 0.0
                for i in out:
                    q = qs[i]
                    t = free[q]
                    for j, w in pre[i]:
                        x = fin[j] + w
                        if x > t:
                            t = x
                    free[q] = t + h[i]
                    fin[i] = t = t + c[i]
                    if t > end:
                        end = t
                total += end
            return total

        rng, at, best, least = np.random.default_rng(0), np.arange(n), None, 1e18
        for k in range(TRIES):
            if k < 200:
                noise, patience = rng.random(n) * (0.0, 100.0, 300.0, 800.0)[k // 4 % 4], (0.0, 20.0, 50.0, 100.0)[k % 4]
            else:
                noise, patience = best[2].copy(), best[3] if k % 5 else 10.0 * (k // 5 % 11)
                some = (np.abs(at - rng.integers(0, n)) < (5, 20, 60, 200)[k % 4]) & (rng.random(n) < (0.6, 0.3, 0.15, 0.1)[k % 4])
                noise[some] += rng.normal(0.0, (100.0, 300.0, 800.0)[k % 3], int(some.sum()))
            end, out = order([r + x for r, x in zip(rank, noise.tolist())], patience)
            if end > least + 500.0:
                continue
            least, end = min(least, end), judge(out)
            if best is None or end <= best[0]:
                best = (end, out, noise, patience)
        return best[1]

    def issue():
        key = str([(o["q"], o["cost"], sorted(o["pre"].items())) for o in ops])
        if key not in ORDERS:
            ORDERS[key] = best_order()
        count, at, known, snap = {}, {}, {q: {} for q in eng}, {}
        for i in ORDERS[key]:
            o = ops[i]
            q, s = o["q"], o["sem"]
            kn = known.setdefault(q, {})
            if q in eng:
                want = {}
                for j, w in o["pre"].items():
                    if w:
                        want[ops[j]["sem"]] = max(want.get(ops[j]["sem"], 0), at[j])
                for s2, m in sorted(want.items()):
                    if kn.get(s2, 0) >= m:
                        continue
                    eng[q].wait_ge(T.sem[s2], m)
                    kn[s2] = m
                    for k, x in snap.get((s2, m), {}).items():
                        kn[k] = max(kn.get(k, 0), x)
            count[s] = count.get(s, 0) + o["inc"]
            at[i] = count[s]
            if o["call"]:
                o["call"](eng[q])
            snap[(s, at[i])] = dict(kn) if q in eng else {}
        for s in sorted(count):
            if known["g"].get(s, 0) < count[s]:
                g.wait_ge(T.sem[s], count[s])
    return add, issue


def rank_program(g, core, T, topo):
    rank = T.rank_of(core)
    if rank is None:
        return
    OP, AF = AluOpType, ActivationFunctionType
    add, issue = planner(g, T)
    nd = [0]

    def V(n, a=None, b=None, s=1):
        if a is None:
            return (n, 0, WIDTH[n], 1)
        return (n, a, b, s)

    def ap(v):
        n, a, b, s = v
        if n in PLACE:
            n, o = PLACE[n]
            a, b = a + o, b + o
        if s < 0:
            return T[n][:, a:(b if b >= 0 else None):s]
        return T[n][:, a:b:s] if s != 1 else T[n][:, a:b]

    def ind(v, l):
        return ap(v).indirect(ap(l))

    def sc(x):
        return ap(x) if isinstance(x, tuple) else x

    def scr(*xs):
        return [x for x in xs if isinstance(x, tuple)]

    def width(v):
        return len(range(v[1], v[2], v[3]))

    def short(*vs):
        return all(TYPE[v[0]] in (B16, U16) for v in vs)

    def do(q, call, reads, writes, cycles, adds=False):
        add(q, lambda e: call(e).then_inc(T.sem["q" + q], 1), reads, writes, max(64, cycles) * CYCLE + FIXED, adds=adds)

    def dma(q, out, in_, reads, writes):
        s = "d%d" % nd[0]
        nd[0] += 1
        add(q, lambda e: e.dma_start(out, in_).then_inc(T.sem[s], 16), reads, writes, 2501.0, 100.0, s, 16)

    def tt(out, a, b, op, l=None):
        n = width(out)
        n = 60 + 1.5 * n if l else n if a[0] in _PS or b[0] in _PS else 2 * n
        do("v", lambda e: e.tensor_tensor(ap(out), ind(a, l) if l else ap(a), ap(b), op), [a, b] + scr(l), [out], n)

    def half(out, *a):
        return width(out) * (0.5 if short(out, *a) else 1.0)

    def ts(out, a, s1, s2, op0, op1=None):
        if op1 is None:
            do("v", lambda e: e.tensor_scalar(ap(out), ap(a), sc(s1), None, op0), [a] + scr(s1), [out], half(out, a))
        else:
            do("v", lambda e: e.tensor_scalar(ap(out), ap(a), sc(s1), sc(s2), op0, op1), [a] + scr(s1, s2), [out], half(out, a))

    def scan(out, d0, d1, init, op0, op1):
        do("v", lambda e: e.tensor_tensor_scan(ap(out), ap(d0), ap(d1), init, op0, op1), [d0, d1], [out], half(out, d0, d1))

    def copy(out, a):
        do("v", lambda e: e.tensor_copy(ap(out), ap(a)), [a], [out], half(out, a))

    def fill(v, c):
        do("v", lambda e: e.memset(ap(v), c), [], [v], half(v))

    def act(out, a, f, bias=0.0, scale=1.0, l=None, acc=None):
        def call(e):
            kw = {}
            if isinstance(bias, tuple) or bias != 0.0:
                kw["bias"] = sc(bias)
            if isinstance(scale, tuple) or scale != 1.0:
                kw["scale"] = sc(scale)
            if acc:
                kw["accum_out"] = ap(acc)
            return e.activation(ap(out), ind(a, l) if l else ap(a), f, **kw)
        n = width(out)
        do("a", call, [a] + scr(bias, scale, l), [out] + scr(acc), 78 + 1.5 * n if l else n + (24 if acc else 0))

    def quant(q, s, x):
        do("v", lambda e: e.quantize_mx(ap(q), ap(s), ap(x)), [x], [q, s], 14 + 0.265 * width(x))

    def mm(out, l, ls, r, rs, start=True, stop=True):
        do("t", lambda e: e.matmul_mx(ap(out), ap(l), ap(ls), ap(r), ap(rs), start, stop), [l, ls, r, rs], [out], width(r) + 16, not start)

    def iota(v, pat, base, cm):
        kw = {} if TYPE[v[0]] == I32 else {"allow_small_or_imprecise_dtypes": True}
        do("g", lambda e: e.iota(ap(v), pat, base, cm, **kw), [], [v], 160 + 2 * width(v))

    def level(n, a, b, c):
        iota(V(n, a, b), [[0, b - a]], c, 0)

    def select(v, pat, op, base, cm):
        do("g", lambda e: e.affine_select(ap(v), ap(v), pat, op, 0.0, base, cm), [v], [v], 200 + 2 * width(v))

    def bits(out, a, n):
        do("v", lambda e: e.tensor_scalar(ap(out), ap(a), n, None, OP.bitwise_and), [a], [out], width(out))

    def dscan(out, src, lift):
        scan(out, lift, src, 0.0, OP.add, OP.max)

    def less(out, a, b):
        scan(out, a, b, 0.0, OP.max, OP.subtract)

    LI, EL, QL, NL, HL, UO = V("su", 0, 8), V("su", 8, 12), V("su", 12, 16), V("su", 16, 24), V("su", 24, 40), V("su", 40, 48)

    dma("s", ap(V("X0")), T.x[:, :], [], [V("X0")])
    dma("a", ap(V("ut")), T.u[:, :], [], [V("ut")])
    dma("s", ap(V("wq")).bitcast(dt.uint8), T.wc[:, :], [], [V("wq")])
    dma("a", ap(V("wp")), T.ws[:, :], [], [V("wp")])
    dma("s", ap(V("vt")), T.v[:, :], [], [V("vt")])

    iota(V("ci"), [[1, 256]], 256, -1)
    bits(V("cj"), V("ci"), 15)
    copy(V("cf"), V("cj"))
    ts(V("mk"), V("cf"), 0.0, None, OP.is_equal)
    iota(V("c0"), [[16, 8]], 0, 0)
    copy(UO, V("c0"))
    for n, w, k, c0, c in (("sgb", 128, 32, 0.0, 1.0), ("par", 256, 2, 0.0, 1.0), ("rst", 128, 16, -4.95e29, 4.95e29), ("rstV", 256, 32, 4.95e29, -4.95e29)):
        fill(V(n, 0, w), c)
        fill(V(n, 0, w, k), c0)
    for a, b in ((0, 8), (264, 520), (776, 784)):
        fill(V("Sw", a, b), -1e25)
    for p in range(2):
        ts(V("mkV", p, 256, 2), V("mk", 0, 128), 0.5, -9.9e29, OP.subtract, OP.mult)
    ts(V("tmV", 0, 1), V("mkV", 0, 1), -1e25, None, OP.max)
    ts(V("mP"), V("mk", 0, 128), 0.5, 9.9e29, OP.subtract, OP.mult)
    for d, n, c in (("dL", 128, LIFT), ("dL2", 256, LIFT2)):
        ts(V("mt", 0, n), V("mk", 0, n), c, None, OP.mult)
        ts(V("mu", 0, n), V("mk", 0, n), -1e29, None, OP.mult)
        copy(V(d, 0, 1), V("mu", 0, 1))
        tt(V(d, 1, n), V("mu", 1, n), V("mt", 0, n - 1), OP.add)
    ts(V("mkS"), V("mk", 0, 64), -2.0 ** 20, 2.0 ** 20, OP.mult, OP.add)
    fill(V("dg"), -65.0)
    fill(V("dg", 512, 768), -1.0)
    for k, c in enumerate((0.0, 1.0)):
        fill(V("WM", k, 384, 3), c)
    fill(V("WD", 2, 384, 3), 64.0)
    quant(V("uq0"), V("us0"), V("ut"))
    do("v", lambda e: e.tensor_copy(T.uq[:, 0:128].bitcast(dt.uint32), T.uq0[:, 0:128].bitcast(dt.uint32).indirect(ap(UO))), [V("uq0"), UO], [V("uq")], 250)
    act(V("us"), V("us0", 0, 128), AF.Copy, l=UO)
    fill(V("idn"), 1.0)
    fill(V("one"), 1.0)
    fill(V("c8"), 1024.0)
    select(V("c8"), [[-16, 8]], OP.is_ge, 0, 1)
    select(V("c8"), [[16, 8]], OP.is_ge, 15, -1)
    for m in range(8):
        act(V("rbt", 64 * m, 64 * m + 64), V("one"), AF.Copy, scale=V("c8", m, m + 1))
    select(V("idn"), [[-1, 128]], OP.is_equal, 0, 1)
    iota(V("c1"), [[0, 8]], 0, 1)
    iota(V("jc"), [[2, 128]], 131072, 0)
    iota(V("ng", 16, 144), [[-1, 128]], 128, 0)
    iota(V("iw", 0, 256), [[1, 256]], ALL + 256, 0)
    level("iw", 256, 512, ALL)
    iota(V("iw", 512, 768), [[1, 256]], ALL + 256, 0)
    level("iw", 768, 776, ALL)
    iota(V("col"), [[1, 256]], 0, 0)
    for n, o in (("et", 4), ("et1", 5)):
        fill(V(n), 0.0)
        act(V(n, o, o + 509, 4), V("idn"), AF.Copy)
    for b in range(4):
        o = (4, 4, 2, 2)[b]
        quant(V("eq", 128 * b, 128 * b + 128), V("es", 128 * b, 128 * b + 128), V(("et", "et1")[b % 2], o, o + 512))
    quant(V("rbq"), V("rbs"), V("rbt"))
    bits(V("c2"), V("c1"), 15)
    copy(V("cq"), V("c2"))
    for m in range(4):
        ts(V("sm", m, m + 1), V("cq", 0, 1), 16.0 * m + BASE + 0.5, None, OP.add)
    ts(V("sm", 11, 12), V("cq", 0, 1), 15.0, None, OP.is_lt)
    ts(V("sm", 8, 9), V("sm", 11, 12), 2.0 * LIFT, 273.0, OP.mult, OP.add)
    ts(V("sm", 9, 10), V("sm", 11, 12), -LIFT2, -1.0, OP.mult, OP.add)
    for v, c in ((V("A"), 0.0), (V("nW"), 1.0), (V("UL", 15, 16), 1.0), (V("UR", 1024, 1025), 1.0), (V("nkL", 128, 129), 0.0), (V("ng", 15, 16), 0.0),
                 (V("pcw", 0, 16), BASE), (V("nE"), 1.0), (V("r", 0, 16), 0.0)):
        fill(v, c)
    level("FE", 0, 512, 0)
    level("g128", 0, 128, 0)
    level("F", 256, 512, 0)
    level("zt", 0, 512, 0)
    quant(V("zq"), V("zs"), V("zt"))
    for t in range(R):
        dma("s", T["lc%d" % t][:, 64:128].bitcast(dt.uint8), T.zq[:, 64:128].bitcast(dt.uint8), [V("zq")], [V("lc%d" % t, 64, 128)])
        dma("s", T["ls%d" % t][:, 64:128], T.zs[:, 64:128], [V("zs")], [V("ls%d" % t, 64, 128)])
    quant(V("vq"), V("vs"), V("vt"))

    far = [T.cores[rank ^ s] for s in STEP]
    engs = topo.engines(core, far[1])
    mask = 0
    for e in engs:
        mask |= 1 << e

    def send(t):
        rid, pid, _ = topo.addr(far[t])
        arr = T.sem["arr%d" % t]

        def call(e):
            e.remote_dma(T["lc%d" % t][:, 0:64].bitcast(dt.uint8), T["Fq%d" % t][:, 0:64].bitcast(dt.uint8), arr, T.sem.snt, pid, rid, mask)
            e.remote_dma(T["ls%d" % t][:, 0:64], T["Fs%d" % t][:, 0:64], arr, T.sem.snt, pid, rid, mask)
        add("g", call, [V("Fq%d" % t), V("Fs%d" % t)], [], NET, NET, "snt", 2 * len(engs))
        add("in", None, [V("Fq%d" % t)], [V("lc%d" % t, 0, 64), V("ls%d" % t, 0, 64)], NET, 0.0, "arr%d" % t, 2 * len(engs))

    XQ, XS, P = V("XQ"), V("XS"), V("psr", 0, 128)
    pc = V("pcw", 16, 272)

    def product(l, ls, X, banks):
        for h in range(2):
            q, s = V("XQ", 128 * h, 128 * h + 128), V("XS", 128 * h, 128 * h + 128)
            quant(q, s, V(X, 512 * h, 512 * h + 512))
            for n in banks:
                n, o = ("ps%d" % h, 0) if n == "ps" else (n, 512 * h)
                mm(V(n, o, o + 128), V(l), V(ls), q, s)

    def ranks(tiles):
        for i, h in enumerate(tiles):
            x, q, s = (V("FE"), V("FEq"), V("FEs")) if h == 2 else (V("FV", 512 * h, 512 * h + 512), V("FVq", 128 * h, 128 * h + 128),
                                                                    V("FVs", 128 * h, 128 * h + 128))
            quant(q, s, x)
            mm(P, V("rbq"), V("rbs"), q, s, i == 0, i == len(tiles) - 1)

    def slot(m, a=0, b=128):
        o = 512 * (m // 4) + m % 4
        return V("FV", o + 4 * a, 512 * (m // 4) + 4 * b, 4)

    def climb(n, d, o, init, w):
        for m in range(7, -1, -1):
            k = 16 * m + 15 + (m == 0)
            scan(V("%s%d" % (n, m // 4), 80 + 16 * (m % 4) - k, 80 + 16 * (m % 4)), V("UL", 144 * m + 31 - k, 144 * m + 31),
                 V(d, o + 16 * m + 15 - k, o + 16 * m + 15), init, OP.mult, OP.max)
        for h in range(2):
            dscan(V(w, 64 * h, 64 * h + 64), V("%s%d" % (n, h), 64, 128), V("dL", 0, 64))

    for t in range(R):
        product("uq", "us", "X%d" % (t % 2), ("ps", "pst"))
        for h in range(2):
            act(V("Sw", 128 * h + 8, 128 * h + 136), V("pst", 512 * h, 512 * h + 128), AF.Copy)
        for b in range(4):
            mm(V("pst", 512 * b, 512 * b + 256), V("eq", 128 * b, 128 * b + 128), V("es", 128 * b, 128 * b + 128), XQ, XS)
        for h in range(2):
            S, o, e = "ps%d" % h, 128 * h, 128 - h
            tt(V("tmV", o + 1, o + 1 + e), V(S, 0, e), V("mkV", o + 1, o + 1 + e), OP.max)
            tt(V("VV", o // 2, o // 2 + 64), V(S, 0, 128, 2), V("Sw", o + 7, o + 135, 2), OP.min)
            scan(V("tsV", o, o + 128), V("rstV", o, o + 128), V("tmV", o, o + 128), 0.0, OP.max, OP.min)
            tt(V("M", o // 2, o // 2 + 64), V(S, 0, 128, 2), V("Sw", o + 9, o + 137, 2), OP.max)
            tt(V("A", o, o + 128), V(S, 0, 128), V("Sw", o + 7, o + 135), OP.is_gt)
        for h in range(2):
            o, e = 128 * h, 128 - h
            tt(V("nW", o + 1, o + 1 + e), V("ps%d" % h, 0, e), V("Sw", o + 10, o + 10 + e), OP.is_ge)
        for m in range(8):
            s = V("tsV", 32 * m + 31, 32 * m + 32)
            if m < 2:
                ts(slot(m), V("VV"), s, None, OP.is_lt)
            else:
                act(slot(m), V("VV"), AF.Sign, bias=s, scale=-1.0)
        scan(V("tmM"), V("M"), V("mP"), -4e29, OP.max, OP.min)
        scan(V("tsM"), V("rst"), V("tmM"), 0.0, OP.min, OP.max)
        dma("s", T.Sw[:, 520:776], T.Sw[:, 8:264], [V("Sw", 8, 264)], [V("Sw", 520, 776)])
        scan(V("NJ"), V("A", 0, 256, 2), V("jc"), 0.0, OP.max, OP.subtract)
        for m in range(8):
            s = V("tsM", 16 * m + 15, 16 * m + 16)
            act(V("UL", 16 + 128 * m, 16 + 128 * m + 16 * m + 16), V("M", 0, 16 * m + 16), AF.Sign, bias=s, scale=-1.0)
            r = V("UR", 128 * m + 16 * m, 128 * m + 128)
            if m < 4:
                ts(r, V("M", 16 * m, 128), s, None, OP.is_le)
            else:
                act(r, V("M", 16 * m, 128), AF.Sign, bias=s, scale=-1.0)
                act(r, r, AF.Sign, bias=0.5)
        ranks((0, 1))
        tt(V("nkL", 0, 128), P, V("NJ"), OP.subtract)
        act(V("A2", 0, 257), V("A", 0, 257), AF.Copy, bias=2.0)
        less(V("du"), V("A2", 0, 256), V("A2", 1, 257))
        scan(V("hpx"), V("par"), V("du"), 0.0, OP.mult, OP.max)
        ts(V("hp"), V("hpx", 1, 256, 2), 2e29, -1e27, OP.mult, OP.add)
        scan(V("PK"), V("hp"), V("M"), 0.0, OP.add, OP.min)
        act(V("pk"), V("du"), AF.Relu)
        act(V("npk"), V("pk"), AF.Copy, bias=1.0, scale=-1.0)
        act(V("np2"), V("pk"), AF.Copy, bias=132096.0, scale=-65536.0)
        for b in range(4):
            act(V("Th", 512 * b, 512 * b + 256), V("pst", 512 * b, 512 * b + 256), AF.Copy, scale=0.5)
            dma("s", T.Th[:, 512 * b + 256:512 * b + 512], T.Th[:, 512 * b:512 * b + 256], [V("Th", 512 * b, 512 * b + 256)],
                [V("Th", 512 * b + 256, 512 * b + 512)])
        climb("RL", "nkL", 1, INIT, "tRL")
        for m in range(8):
            a, e = 16 * m, 127 + m // 7
            scan(V("RR%d" % (m // 4), e - 1 - a + a % 64, a % 64 - 1, -1), V("UR", 128 * m + e, 128 * m + a, -1), V("nkL", e, a, -1), INIT, OP.mult,
                 OP.max)
        for h in range(2):
            dscan(V("tRR", 64 * h, 64 * h + 64), V("RR%d" % h, 0, 64), V("dL", 0, 64))
        ts(V("sm", 40, 48), V("tRR", 15, 128, 16), 512.0, None, OP.add)
        tt(V("k8"), V("tRL", 15, 128, 16), V("sm", 40, 48), OP.min)
        bits(V("l8"), V("k8"), 1023)
        copy(LI, V("l8"))
        tt(V("np"), V("Sw", 8, 784), V("PK"), OP.subtract, l=LI)
        scan(V("tmN"), V("np"), V("mP"), -4e29, OP.max, OP.min)
        scan(V("tsN", 127, -1, -1), V("rst"), V("tmN", 127, -1, -1), 0.0, OP.min, OP.max)
        for m in range(8):
            s = V("tsN", 16 * m, 16 * m + 1)
            if m < 5:
                act(slot(m, 16 * m, 128), V("np", 16 * m, 128), AF.Relu, bias=s, scale=-1.0)
                act(slot(m, 16 * m, 128), slot(m, 16 * m, 128), AF.Sign)
            else:
                ts(slot(m, 16 * m, 128), V("np", 16 * m, 128), s, None, OP.is_lt)
            if m:
                ts(slot(m, 0, 16 * m), V("np", 0, 16 * m), s, None, OP.is_le)
        tt(V("FE", 0, 512, 4), V("np"), V("tsN"), OP.is_equal)
        ranks((2, 1, 0))
        act(V("Gp"), V("iw"), AF.Copy, l=LI)
        act(V("WD", 1, 384, 3), V("dg"), AF.Copy, l=LI)
        scan(V("ni"), V("npk"), V("npk"), 0.0, OP.add, OP.max)
        ts(V("sm", 10, 11), V("ni", 255, 256), -float(2 ** 20), 192.0 * 2 ** 20, OP.mult, OP.add)
        ts(V("sm", 12, 13), V("sm", 10, 11), float(ALL), float(ALL), OP.add, OP.min)
        act(V("nf"), V("ni"), AF.Relu, bias=V("sm", 10, 11), scale=float(2 ** 20))
        scan(V("th"), V("nf"), V("np2"), 0.0, OP.max, OP.min)
        ts(V("thB"), V("th"), float(ALL), 2.0 ** -10, OP.max, OP.mult)
        climb("NP", "ng", 16, 200.0, "tNP")
        for p in range(2):
            tt(V("K", p, 256, 2), P, V("th", p, 256, 2), OP.is_ge)
        scan(pc, V("K"), V("K"), BASE, OP.add, OP.max)
        for m in range(4):
            w, o = V("pcw", 16 + 16 * m, 16 + 16 * m + SPAN), SPAN * (m % 2)
            if m < 2:
                ts(V("ec", o, o + SPAN), w, V("sm", m, m + 1), None, OP.is_le)
                scan(V("cn", o, o + SPAN), V("ec", o, o + SPAN), V("ec", o, o + SPAN), 16.0 * m, OP.add, OP.max)
            else:
                act(V("ed", o, o + SPAN), w, AF.Sign, bias=V("sm", m, m + 1), scale=-1.0, acc=V("sm", 16 + m, 17 + m))
                ts(V("su", 8 + m, 9 + m), V("sm", 16 + m, 17 + m), 0.5, SPAN / 2.0 + 16.0 * m, OP.mult, OP.add)
        copy(V("su", 8, 10), V("cn", SPAN - 1, 2 * SPAN, SPAN))
        for b in range(2):
            act(V("Tf", 256 * b, 256 * b + 256), V("pst", 512 * b, 512 * b + 256), AF.Copy)
        for b in range(4):
            act(V("TE", 64 * b, 64 * b + 64), V("Th", 512 * b, 512 * b + 256), AF.Copy, l=EL)
        for p in range(2):
            less(V("CT", p, 256, 2), V("np2", p, 256, 2), V("Gp"))
        ts(V("g128", 31, 128, 32), EL, -1.0, None, OP.mult)
        tt(V("g128", 0, 128, 2), V("CT"), V("mkS"), OP.add, l=EL)
        scan(V("s128"), V("sgb"), V("g128"), 0.0, OP.mult, OP.min)
        ts(QL, V("s128", 31, 128, 32), -1.0, None, OP.mult)
        for b in range(4):
            tt(V("F", b, 256, 4), V("Th", 512 * b, 512 * b + 512), V("TE", 64 * b, 64 * b + 64), OP.add, l=QL)
        quant(V("Fq%d" % t), V("Fs%d" % t), V("F"))
        send(t)
        ts(NL, V("tNP", 15, 128, 16), -2.0, V("sm", 8, 9), OP.mult, OP.add)
        act(V("vL"), V("pcw"), AF.Copy, bias=-65.0, l=NL)
        less(V("WD", 0, 384, 3), V("pcw", 17, 272, 2), V("vL"))
        for p in range(2):
            less(V("r", 16 + p, 272, 2), V("WD", 0, 384, 3), V("thB", p, 256, 2))
        act(V("BB2"), V("r", 16, 272), AF.Copy, bias=-1e27, scale=2e27)
        act(V("Sg"), V("r", 16, 272), AF.Sign, bias=0.5, scale=-1.0)
        act(V("pen"), V("Sg"), AF.Copy, bias=192.0, scale=64.0)
        ts(V("WM", 2, 384, 3), P, V("sm", 12, 13), None, OP.is_lt)
        scan(V("WO"), V("WM"), V("WD"), 0.0, OP.mult, OP.add)
        for p in range(2):
            less(V("uu", p, 256, 2), V("pcw", 16 + p, 272, 2), V("WO", 2, 384, 3))
        less(V("bv"), V("uu"), V("pen"))
        scan(V("lm", 255, -1, -1), V("Sw", 263, 7, -1), V("BB2", 255, -1, -1), -1e25, OP.min, OP.max)
        for h in range(2):
            o, e = 128 * h + 1, 128 - h
            tt(V("nE", o, o + e), V("ps%d" % h, 0, e), V("lm", o, o + e), OP.is_ge)
        scan(V("D"), V("nE"), V("r", 15, 271), 0.0, OP.min, OP.max)
        scan(V("D2", 255, -1, -1), V("nW", 255, -1, -1), V("D", 255, -1, -1), 1.0, OP.max, OP.min)
        scan(V("vl"), V("D2"), V("bv"), 0.0, OP.mult, OP.max)
        ts(V("u2"), V("vl"), 0.0, None, OP.is_equal)
        scan(V("hv", 255, -1, -1), V("u2", 255, -1, -1), V("vl", 255, -1, -1), 0.0, OP.mult, OP.add)
        dscan(V("tsb"), V("hv"), V("dL2"))
        ts(HL, V("tsb", 15, 256, 16), V("sm", 9, 10), None, OP.add)
        if t == R - 1:
            act(V("s64"), V("col"), AF.Copy, l=EL)
            act(V("out"), V("s64"), AF.Copy, l=HL)
            dma("s", T.ol[:, :], T.out[0:128:16, :], [V("out")], [])
        X = "X%d" % ((t + 1) % 2)
        for b in (0, 3, 1, 2):
            o = ("pst", "ps1", "ps0", "psr")[b]
            mm(V(o, 0, 128), V("wq", 128 * b, 128 * b + 128), V("wp", 128 * b, 128 * b + 128), V("lc%d" % t), V("ls%d" % t))
            if b == 0:
                ts(V("H", 0, 64), V(o, 0, 64), 0.0, 0.03125, OP.max, OP.mult)
            else:
                act(V("H", 64 * b, 64 * b + 64), V(o, 0, 64), AF.Relu, scale=0.03125)
        for h in range(2):
            hl = V("su", 24 + 8 * h, 32 + 8 * h)
            for b in (0, 1, 3, 2) if h == 0 else (0, 3, 2, 1):
                o = 256 * b + 128 * h
                x = V(X, 512 * h + b, 512 * h + 512, 4)
                if b < 2 - h:
                    tt(x, V("H", 64 * b, 64 * b + 64), V("Tf", o, o + 128), OP.add, l=hl)
                else:
                    k = 512 if b == 1 else o - 512
                    act(V("G3", k, k + 128), V("H", 64 * b, 64 * b + 64), AF.Copy, l=hl)
                    tt(x, V("pst", 512 * b + 128 * h, 512 * b + 128 * h + 128), V("G3", k, k + 128), OP.add)
    product("vq", "vs", "X%d" % (R % 2), ("ps",))
    dma("a", T.oc[:, :], T.XQ[:, :].bitcast(dt.uint8), [XQ], [])
    for k in range(4):
        dma("a" if k % 2 else "s", T.osc[4 * k:4 * k + 4, :], T.XS[32 * k:32 * k + 4, :], [XS], [])
    copy(V("yb", 0, 128), V("ps0", 0, 128))
    copy(V("yb", 128, 256), V("ps1", 0, 128))
    dma("s", T.y[:, :], T.yb[:, :], [V("yb")], [])
    issue()
